import numpy as np
import ml_dtypes


def mxq(x, axis, fmt="e4m3"):
    dtype, down = {"e4m3": (ml_dtypes.float8_e4m3fn, 7), "e5m2": (ml_dtypes.float8_e5m2, 14)}[fmt]
    v = np.moveaxis(np.asarray(x, np.float32).astype(ml_dtypes.bfloat16).astype(np.float64), axis, -1)
    blocks = v.reshape(v.shape[:-1] + (-1, 32))
    amax = np.abs(blocks).max(-1, keepdims=True)
    byte = np.maximum(np.where(amax > 0, np.frexp(amax)[1] - 1 + 127, 0) - down, 1)
    scale = np.exp2(byte - 127.0)
    codes = (blocks / scale).astype(np.float32).astype(dtype).astype(np.float64)
    return np.moveaxis((codes * scale).reshape(v.shape), -1, axis)


WIDE = False


def mx_kscale(k):
    if not WIDE:
        return np.ones(k)
    levels = np.array([10, -10, 5, -5, 0])
    if k % 512:
        return np.exp2(np.random.permutation(np.resize(levels, k // 32))).repeat(32)
    a = np.empty((k // 512, 16))
    for p in range(k // 512):
        a[p, :8] = np.random.permutation(np.resize(levels, 8))
        for g in range(8):
            far = levels[np.abs(levels - a[p, g]) >= 10]
            a[p, g + 8] = far[np.random.randint(len(far))]
    return np.exp2(a.ravel()).repeat(32)


BF16 = ml_dtypes.bfloat16


def bf(x):
    return np.asarray(x, np.float32).astype(BF16)


def f64(x):
    return np.asarray(x).astype(np.float64)


E2M1 = np.array([0.0, 0.5, 1.0, 1.5, 2.0, 3.0, 4.0, 6.0, -0.0, -0.5, -1.0, -1.5, -2.0, -3.0, -4.0, -6.0])


def pack_weight(w, fmt):
    k, n = w.shape
    w = f64(bf(w)).reshape(k // 32, 32, n)
    amax = np.abs(w).max(1)
    if fmt == "e4m3":
        byte = np.frexp(amax)[1] - 1 + 127 - 7
    else:
        mant, ex = np.frexp(amax / 6.0)
        byte = np.where(mant > 0.5, ex, ex - 1) + 127
    byte = np.clip(np.where(amax > 0, byte, 1), 1, 254)
    scaled = (w * np.exp2(127.0 - byte)[:, None, :]).reshape(k, n).astype(np.float32)
    by_word = np.ascontiguousarray(scaled.reshape(k // 512, 128, 4, n).transpose(0, 1, 3, 2))
    if fmt == "e4m3":
        words = by_word.astype(ml_dtypes.float8_e4m3fn).view(np.uint8)
    else:
        c = by_word.astype(ml_dtypes.float4_e2m1fn).view(np.uint8) & 0xF
        words = c[..., 0::2] | (c[..., 1::2] << 4)
    return np.ascontiguousarray(words), np.ascontiguousarray(byte.astype(np.uint8).reshape(k // 512, 16, n))


def unpack_weight(words, scales, fmt):
    g, p, n, _ = words.shape
    if fmt == "e4m3":
        vals = np.ascontiguousarray(words).view(ml_dtypes.float8_e4m3fn).astype(np.float64)
    else:
        nib = np.empty((g, p, n, 4), np.uint8)
        nib[..., 0::2] = words & 0xF
        nib[..., 1::2] = words >> 4
        vals = E2M1[nib]
    vals = vals * np.repeat(np.exp2(scales.astype(np.float64) - 127.0), 8, axis=1)[..., None]
    return vals.transpose(0, 1, 3, 2).reshape(g * 512, n)
def pack4(w):
    words, scales = pack_weight(w, "e2m1")
    return words.reshape(words.shape[0], 128, -1), scales


def unpack4(words, scales):
    return unpack_weight(words.reshape(words.shape[0], 128, -1, 2), scales, "e2m1")


def planes(Y):
    n, m = Y.shape
    b = f64(bf(Y)).reshape(n // 32, 32, m)
    amax = np.abs(b).max(1)
    byte = np.clip(np.where(amax > 0, np.frexp(amax)[1] - 1 + 127 - 7, 1), 1, 254)
    codes = (b * np.exp2(127.0 - byte)[:, None, :]).reshape(n, m).astype(np.float32).astype(ml_dtypes.float8_e4m3fn).view(np.uint8)
    words = codes.reshape(n // 512, 128, 4, m).transpose(0, 1, 3, 2)
    return np.ascontiguousarray(words), np.ascontiguousarray(byte.astype(np.uint8).reshape(n // 512, 16, m))


U, I, B = 2048, 1024, 1536
BETA = 0.4

def setup_inputs():
    s, t = mx_kscale(U), mx_kscale(I)
    activity = np.exp(0.5 * np.random.randn(U, 1))
    appeal = np.exp(1.2 * np.random.randn(1, I))
    angle_u = 2 * np.pi * np.random.rand(U, 1)
    angle_i = 2 * np.pi * np.random.rand(1, I)
    r = activity * appeal * np.exp(2 * np.cos(angle_u - angle_i) + 0.5 * np.random.randn(U, I))
    L = r / r.sum(axis=0, keepdims=True)
    R = I * r / r.sum(axis=1, keepdims=True)
    lw, ls = pack4(L * s[:, None] * t[None, :])
    rw, rs = pack4(R / s[:, None])
    pop = r.sum(axis=0)
    return {
        "item_user_words": lw, "item_user_scales": ls,
        "user_item_words": rw, "user_item_scales": rs,
        "popularity": bf(pop / pop.mean()),
        "prefs": bf(np.random.randn(B, I) / np.sqrt(I) / t[None, :]),
        "user_gain": bf(np.exp(0.3 * np.random.randn(B))),
        "item_bias": bf(0.2 * np.random.randn(I)),
    }

def reference(item_user_words, item_user_scales, user_item_words, user_item_scales,
              popularity, prefs, user_gain, item_bias):
    L = unpack4(item_user_words, item_user_scales)
    R = unpack4(user_item_words, user_item_scales)
    walk = L.T @ R
    sim = walk / f64(popularity)[None, :] ** BETA
    scores = mxq(f64(prefs), 1) @ mxq(sim, 0)
    y = scores * f64(user_gain)[:, None] + f64(item_bias)[None, :]
    words, scales = planes(y.T)
    return y, words, scales

@@ -1,0 +1,381 @@
+from contextlib import ExitStack
+
+import concourse.mybir as mybir
+from concourse.masks import make_identity
+
+U, I, B = 2048, 1024, 1536
+BETA = 0.4
+FLOPS = 2 * U * I * I + 2 * B * I * I
+
+F32 = mybir.dt.float32
+BF16 = mybir.dt.bfloat16
+I32 = mybir.dt.int32
+U32 = mybir.dt.uint32
+U8 = mybir.dt.uint8
+FP8X4 = mybir.dt.float8_e4m3fn_x4
+FP4X4 = mybir.dt.float4_e2m1fn_x4
+ALU = mybir.AluOpType
+ACT = mybir.ActivationFunctionType
+ENG = mybir.EngineType
+
+P = 128
+HALF = 512
+U_PASSES = U // HALF
+BANKS = 8
+
+
+def tile_rp3beta_item_scores_k5_kernel(
+    tc, item_user_words, item_user_scales, user_item_words, user_item_scales,
+    popularity, prefs, user_gain, item_bias, out_0, out_1, out_2,
+):
+    nc = tc.nc
+    with ExitStack() as ctx:
+        keep = ctx.enter_context(tc.tile_pool(name="keep", bufs=1))
+        work = ctx.enter_context(tc.tile_pool(name="work", bufs=3))
+        psum = ctx.enter_context(tc.psum_pool(name="psum", bufs=1))
+        ctx.enter_context(tc.manual_schedule(engines={ENG.PE, ENG.SP, ENG.Pool}))
+
+        bank_count = [0]
+
+        def next_bank():
+            k = bank_count[0] % BANKS
+            bank_count[0] += 1
+            return psum.tile([P, HALF], F32, name="bank%d" % k, tag="bank%d" % k)
+
+        def kept(name, shape, dtype):
+            return keep.tile(shape, dtype, name=name, tag=name, align_bytes=64)
+
+        l_words = [kept("l_words%d" % h, [P, U_PASSES, 2 * HALF], U8) for h in range(2)]
+        r_words = [kept("r_words%d" % h, [P, U_PASSES, 2 * HALF], U8) for h in range(2)]
+        l_scales = [kept("l_scales%d" % h, [P, U_PASSES, HALF], U8) for h in range(2)]
+        r_scales = [kept("r_scales%d" % h, [P, U_PASSES, HALF], U8) for h in range(2)]
+        prefs_raw = [kept("prefs_raw%d" % k, [P, 2, I], BF16) for k in range(6)]
+        prefs_split = [kept("prefs_split%d" % k, [P, 2, I], BF16) for k in range(6)]
+        prefs_grouped = [kept("prefs_grouped%d" % k, [P, 2, 2, P, 4], BF16) for k in range(6)]
+        prefs_codes = [kept("prefs_codes%d" % k, [P, 2, 2, P], U32) for k in range(6)]
+        prefs_scales = [kept("prefs_scales%d" % k, [P, 2, 2, P], U8) for k in range(6)]
+        sim_t = [kept("sim_t%d" % jt, [P, I], BF16) for jt in range(8)]
+        sim_grouped = [kept("sim_grouped%d" % h, [P, 2, HALF, 4], BF16) for h in range(2)]
+        sim_codes = [kept("sim_codes%d" % h, [P, 2, HALF], U32) for h in range(2)]
+        sim_scales = [kept("sim_scales%d" % h, [P, 2, HALF], U8) for h in range(2)]
+        y_grouped = [kept("y_grouped%d" % h, [P, B, 4], BF16) for h in range(2)]
+        y_codes = [kept("y_codes%d" % h, [P, B], U32) for h in range(2)]
+        y_scales = [kept("y_scales%d" % h, [P, B], U8) for h in range(2)]
+        rows_bf = kept("rows_bf", [P, P], BF16)
+        warm_bf = kept("warm_bf", [P, HALF], BF16)
+        warm_codes = kept("warm_codes", [P, P], U32)
+        warm_scales = kept("warm_scales", [P, P], U8)
+        rows_f32 = kept("rows_f32", [P, P], F32)
+        columns = kept("columns", [P, 32], F32)
+        exponent = kept("exponent", [P, 8], F32)
+        damping = kept("damping", [P, 8], F32)
+        identity = kept("identity", [P, P], F32)
+        bias_rows = kept("bias_rows", [P, 32], BF16)
+        bias_cols = kept("bias_cols", [P, 32], BF16)
+        bias_spread = kept("bias_spread", [P, 32, 32], BF16)
+        bias_all = kept("bias_all", [P, I], BF16)
+
+        def load_words(queue, dst, src, h, g0, g1):
+            queue.dma_start(
+                out=dst[h][:, g0:g1, :].bitcast(I32),
+                in_=src[g0:g1, :, 2 * HALF * h : 2 * HALF * (h + 1)].rearrange("g p n -> p g n").bitcast(I32),
+            )
+
+        def load_scales(queue, dst, src, h):
+            for r in range(4):
+                queue.dma_start(
+                    out=dst[h][r:P:32, :, :].bitcast(I32),
+                    in_=src[:, r:16:4, HALF * h : HALF * (h + 1)].rearrange("g q n -> q g n").bitcast(I32),
+                )
+
+        def load_prefs(k):
+            nc.sync.dma_start(
+                out=prefs_raw[k][:], in_=prefs[256 * k : 256 * (k + 1), :].rearrange("(c p) i -> p c i", p=P)
+            )
+
+        nc.vector.memset(rows_bf[:], 0.0)
+        for plane in (l_scales[0], r_scales[0]):
+            nc.vector.memset(plane[:].rearrange("p g n -> p (g n)").bitcast(I32), 0)
+        nc.vector.memset(warm_bf[:], 0.0)
+        nc.vector.quantize_mx(out=warm_codes[:].bitcast(FP8X4), scales=warm_scales[:], in_=warm_bf[:])
+        for plane in (l_scales[1], r_scales[1]):
+            nc.vector.memset(plane[:].rearrange("p g n -> p (g n)").bitcast(I32), 0)
+
+        nc.gpsimd.dma_start(out=rows_bf[0:8, :], in_=popularity.rearrange("(c n) -> c n", n=P))
+        nc.gpsimd.dma_start(out=rows_bf[8:20, :], in_=user_gain.rearrange("(c n) -> c n", n=P))
+        make_identity(nc, identity[:])
+        nc.gpsimd.memset(exponent[:], 1.0)
+        nc.gpsimd.tensor_scalar(out=exponent[:], in0=exponent[:], scalar1=-BETA, scalar2=0.0, op0=ALU.mult, op1=ALU.add)
+        nc.gpsimd.dma_start(out=bias_rows[:], in_=item_bias.rearrange("(c x) -> c x", x=32).unsqueeze(0).to_broadcast([4, 32, 32]))
+
+        load_words(nc.sync, l_words, item_user_words, 0, 0, 1)
+        load_words(nc.scalar, r_words, user_item_words, 0, 0, 1)
+        load_scales(nc.sync, l_scales, item_user_scales, 0)
+        load_scales(nc.scalar, r_scales, user_item_scales, 0)
+        for g0, g1 in ((1, 2), (2, 4)):
+            load_words(nc.sync, l_words, item_user_words, 0, g0, g1)
+            load_words(nc.sync, r_words, user_item_words, 0, g0, g1)
+        load_scales(nc.sync, l_scales, item_user_scales, 1)
+        load_prefs(0)
+        load_prefs(1)
+        load_words(nc.sync, l_words, item_user_words, 1, 0, U_PASSES)
+        load_prefs(2)
+        load_prefs(3)
+        load_scales(nc.sync, r_scales, user_item_scales, 1)
+        load_prefs(4)
+        load_prefs(5)
+        load_words(nc.sync, r_words, user_item_words, 1, 0, U_PASSES)
+
+        nc.vector.tensor_copy(out=rows_f32[:], in_=rows_bf[:])
+
+        def small():
+            small_bank = next_bank()
+            nc.tensor.transpose(small_bank[:, 0:P], rows_f32[:], identity[:])
+            nc.scalar.activation(out=columns[:], in_=small_bank[:, 0:32], func=ACT.Copy)
+            nc.gpsimd.tensor_tensor(out=damping[:], in0=columns[:, 0:8], in1=exponent[:], op=ALU.pow)
+
+        def bias_spreading():
+            nc.vector.transpose(out=bias_cols[:], in_=bias_rows[:])
+            nc.vector.tensor_copy(out=bias_spread[:], in_=bias_cols[:].unsqueeze(2).to_broadcast([P, 32, 32]))
+            nc.vector.transpose(out=bias_all[:], in_=bias_spread[:].rearrange("p c y -> p (c y)"))
+
+        def warm(n):
+            bank = next_bank()
+            for w in range(n):
+                nc.tensor.matmul_mx(
+                    out=bank[:, 0:P], lhsT=warm_codes[:].bitcast(FP8X4), lhsT_scale=warm_scales[:],
+                    rhs=warm_codes[:].bitcast(FP8X4), rhs_scale=warm_scales[:], start=True, stop=True,
+                )
+
+        def copy_words(engine, out, in_):
+            if engine == "v":
+                nc.vector.tensor_copy(out=out, in_=in_)
+            elif engine == "g":
+                nc.gpsimd.tensor_scalar(out=out, in0=in_, scalar1=1.0, scalar2=0.0, op0=ALU.mult, op1=ALU.add)
+            else:
+                nc.scalar.copy(out=out, in_=in_)
+
+        def walk_pass(bank, jt, ih, g):
+            jh, c = divmod(jt, 4)
+            nc.tensor.matmul_mx(
+                out=bank[:],
+                lhsT=r_words[jh][:, g, 2 * P * c : 2 * P * (c + 1)].bitcast(FP4X4),
+                lhsT_scale=r_scales[jh][:, g, P * c : P * (c + 1)],
+                rhs=l_words[ih][:, g, :].bitcast(FP4X4),
+                rhs_scale=l_scales[ih][:, g, :],
+                start=(g == 0),
+                stop=(g == U_PASSES - 1),
+            )
+
+        def walk_out(bank, jt, ih):
+            nc.scalar.activation(
+                out=sim_t[jt][:, HALF * ih : HALF * (ih + 1)].rearrange("q (u m e) -> q u m e", u=2, e=2),
+                in_=bank[:].rearrange("q (m u e) -> q u m e", u=2, e=2),
+                func=ACT.Copy,
+                scale=damping[:, jt : jt + 1],
+            )
+
+        def walk(jt, ih):
+            bank = next_bank()
+            for g in range(U_PASSES):
+                walk_pass(bank, jt, ih, g)
+            walk_out(bank, jt, ih)
+
+        def turn(sources):
+            bank = next_bank()
+            for s, source in enumerate(sources):
+                nc.tensor.transpose(bank[:, P * s : P * (s + 1)], source, identity[:])
+            return bank
+
+        def turn_sim(jt, engine):
+            jh, c = divmod(jt, 4)
+            words = sim_t[jt][:].bitcast(F32)
+            bank = turn([words[:, P * s : P * (s + 1)] for s in range(4)])
+            target = sim_grouped[jh][:].rearrange("q h j t -> q h (j t)").bitcast(F32)
+            copy_words(
+                engine,
+                target[:, :, 2 * P * c : 2 * P * (c + 1)].rearrange("q h (j u) -> q h j u", u=2),
+                bank[:].rearrange("q (h u j) -> q h j u", h=2, u=2),
+            )
+            if c == 3:
+                for ih in range(2):
+                    nc.vector.quantize_mx(
+                        out=sim_codes[jh][:, ih, :].bitcast(FP8X4),
+                        scales=sim_scales[jh][:, ih, :],
+                        in_=sim_grouped[jh][:, ih, :, :].rearrange("q j t -> q (j t)"),
+                    )
+
+        def split_prefs(k):
+            nc.vector.tensor_copy(
+                out=prefs_split[k][:].rearrange("q c i -> q (c i)").bitcast(F32).rearrange("q (s u m) -> q s u m", u=2, m=P),
+                in_=prefs_raw[k][:].rearrange("q c i -> q (c i)").bitcast(F32).rearrange("q (s m u) -> q s u m", u=2, m=P),
+            )
+
+        def turn_prefs(bt, engine):
+            k, c = divmod(bt, 2)
+            words = prefs_split[k][:, c, :].bitcast(F32)
+            bank = turn([words[:, P * s : P * (s + 1)] for s in range(4)])
+            target = prefs_grouped[k][:, c, :, :, :].rearrange("q g b t -> q g (b t)").bitcast(F32)
+            copy_words(
+                engine,
+                target.rearrange("q g (b u) -> q g b u", u=2),
+                bank[:].rearrange("q (g u b) -> q g b u", g=2, u=2),
+            )
+            if c == 1:
+                nc.vector.quantize_mx(
+                    out=prefs_codes[k][:].rearrange("q c g b -> q (c g b)").bitcast(FP8X4),
+                    scales=prefs_scales[k][:].rearrange("q c g b -> q (c g b)"),
+                    in_=prefs_grouped[k][:].rearrange("q c g b t -> q (c g b t)"),
+                )
+
+        y_split = {}
+
+        def score(bt, jh, cast_engine):
+            k, c = divmod(bt, 2)
+            bank = next_bank()
+            for g in range(2):
+                nc.tensor.matmul_mx(
+                    out=bank[:],
+                    lhsT=prefs_codes[k][:, c, g, :].bitcast(FP8X4),
+                    lhsT_scale=prefs_scales[k][:, c, g, :],
+                    rhs=sim_codes[jh][:, g, :].bitcast(FP8X4),
+                    rhs_scale=sim_scales[jh][:, g, :],
+                    start=(g == 0),
+                    stop=(g == 1),
+                )
+            y = work.tile([P, HALF], F32, name="y", tag="y", bufs=6)
+            nc.vector.scalar_tensor_tensor(
+                out=y[:], in0=bank[:], scalar=columns[:, 8 + bt : 9 + bt],
+                in1=bias_all[:, HALF * jh : HALF * (jh + 1)], op0=ALU.mult, op1=ALU.add,
+            )
+            nc.sync.dma_start(out=out_0[P * bt : P * (bt + 1), HALF * jh : HALF * (jh + 1)], in_=y[:])
+            y_bf = work.tile([P, HALF], BF16, name="y_bf", tag="y_bf", bufs=10)
+            copy_words(
+                cast_engine,
+                y_bf[:].rearrange("q (u m e) -> q u m e", u=2, e=2),
+                y[:].rearrange("q (m u e) -> q u m e", u=2, e=2),
+            )
+            y_split[(bt, jh)] = y_bf
+
+        def turn_y(k, jh, engine):
+            sources = []
+            for c in range(2):
+                words = y_split[(2 * k + c, jh)][:].bitcast(F32)
+                sources += [words[:, 0:P], words[:, P : 2 * P]]
+            bank = turn(sources)
+            target = y_grouped[jh][:, 256 * k : 256 * (k + 1), :].rearrange("q b t -> q (b t)").bitcast(F32)
+            copy_words(
+                engine,
+                target.rearrange("q (c b u) -> q c b u", c=2, u=2),
+                bank[:].rearrange("q (c u b) -> q c b u", c=2, u=2),
+            )
+
+        def planes_out(jh, b0, b1):
+            nc.vector.quantize_mx(
+                out=y_codes[jh][:, b0:b1].bitcast(FP8X4),
+                scales=y_scales[jh][:, b0:b1],
+                in_=y_grouped[jh][:, b0:b1, :].rearrange("q b t -> q (b t)"),
+            )
+            nc.sync.dma_start(
+                out=out_1[jh].rearrange("p m t -> p (m t)").bitcast(I32)[:, b0:b1],
+                in_=y_codes[jh][:, b0:b1].bitcast(I32),
+            )
+
+        def scales_out(jh, b0, b1):
+            for r in range(4):
+                nc.sync.dma_start(
+                    out=out_2[jh, r:16:4, b0:b1].bitcast(I32), in_=y_scales[jh][r:P:32, b0:b1].bitcast(I32)
+                )
+
+        warm(16)
+        small()
+        bias_spreading()
+        split_prefs(0)
+        split_prefs(1)
+        split_prefs(2)
+        split_prefs(3)
+        split_prefs(4)
+        split_prefs(5)
+        first = [next_bank() for jt in range(4)]
+        for g in range(U_PASSES):
+            for jt in range(4):
+                walk_pass(first[jt], jt, 0, g)
+        for jt in range(4):
+            walk_out(first[jt], jt, 0)
+        turn_prefs(0, "v")
+        turn_prefs(1, "v")
+        turn_prefs(2, "v")
+        turn_prefs(3, "v")
+        walk(0, 1)
+        walk(1, 1)
+        walk(2, 1)
+        walk(3, 1)
+        turn_prefs(4, "v")
+        turn_prefs(5, "s")
+        turn_sim(0, "v")
+        turn_sim(1, "v")
+        turn_prefs(6, "s")
+        turn_prefs(7, "s")
+        turn_sim(2, "v")
+        turn_sim(3, "v")
+        walk(4, 0)
+        walk(4, 1)
+        walk(5, 0)
+        walk(5, 1)
+        score(0, 0, "s")
+        score(1, 0, "s")
+        score(2, 0, "s")
+        score(3, 0, "s")
+        turn_sim(4, "v")
+        turn_sim(5, "v")
+        turn_prefs(8, "s")
+        turn_prefs(9, "s")
+        turn_prefs(10, "v")
+        turn_prefs(11, "s")
+        turn_y(0, 0, "s")
+        turn_y(1, 0, "s")
+        planes_out(0, 0, 512)
+        walk(6, 0)
+        walk(6, 1)
+        walk(7, 0)
+        walk(7, 1)
+        score(4, 0, "s")
+        score(5, 0, "s")
+        turn_sim(6, "v")
+        turn_sim(7, "v")
+        turn_y(2, 0, "s")
+        score(6, 0, "s")
+        score(7, 0, "s")
+        score(8, 0, "s")
+        score(9, 0, "s")
+        score(10, 0, "s")
+        score(11, 0, "s")
+        score(0, 1, "s")
+        score(1, 1, "v")
+        turn_y(3, 0, "s")
+        planes_out(0, 512, 1024)
+        turn_y(4, 0, "s")
+        turn_y(5, 0, "s")
+        planes_out(0, 1024, 1536)
+        turn_y(0, 1, "s")
+        scales_out(0, 0, 1536)
+        score(2, 1, "v")
+        score(3, 1, "s")
+        score(4, 1, "s")
+        score(5, 1, "v")
+        score(6, 1, "s")
+        score(7, 1, "s")
+        turn_y(1, 1, "s")
+        planes_out(1, 0, 512)
+        turn_y(2, 1, "s")
+        score(8, 1, "v")
+        score(9, 1, "s")
+        score(10, 1, "v")
+        score(11, 1, "v")
+        turn_y(3, 1, "s")
+        planes_out(1, 512, 1024)
+        turn_y(4, 1, "s")
+        planes_out(1, 1024, 1280)
+        turn_y(5, 1, "s")
+        planes_out(1, 1280, 1536)
+        scales_out(1, 0, 1536)

@@ -33,7 +33,6 @@ def tile_rp3beta_item_scores_k5_kernel(
         keep = ctx.enter_context(tc.tile_pool(name="keep", bufs=1))
         work = ctx.enter_context(tc.tile_pool(name="work", bufs=3))
         psum = ctx.enter_context(tc.psum_pool(name="psum", bufs=1))
-        ctx.enter_context(tc.manual_schedule(engines={ENG.PE, ENG.SP, ENG.Pool}))
 
         bank_count = [0]
 
@@ -50,12 +49,12 @@ def tile_rp3beta_item_scores_k5_kernel(
         l_scales = [kept("l_scales%d" % h, [P, U_PASSES, HALF], U8) for h in range(2)]
         r_scales = [kept("r_scales%d" % h, [P, U_PASSES, HALF], U8) for h in range(2)]
         prefs_raw = [kept("prefs_raw%d" % k, [P, 2, I], BF16) for k in range(6)]
-        prefs_split = [kept("prefs_split%d" % k, [P, 2, I], BF16) for k in range(6)]
-        prefs_grouped = [kept("prefs_grouped%d" % k, [P, 2, 2, P, 4], BF16) for k in range(6)]
+        prefs_split = {}
+        prefs_grouped = {}
         prefs_codes = [kept("prefs_codes%d" % k, [P, 2, 2, P], U32) for k in range(6)]
         prefs_scales = [kept("prefs_scales%d" % k, [P, 2, 2, P], U8) for k in range(6)]
         sim_t = [kept("sim_t%d" % jt, [P, I], BF16) for jt in range(8)]
-        sim_grouped = [kept("sim_grouped%d" % h, [P, 2, HALF, 4], BF16) for h in range(2)]
+        sim_grouped = [kept("sim_grouped%d" % jt, [P, 2, P, 4], BF16) for jt in range(8)]
         sim_codes = [kept("sim_codes%d" % h, [P, 2, HALF], U32) for h in range(2)]
         sim_scales = [kept("sim_scales%d" % h, [P, 2, HALF], U8) for h in range(2)]
         y_grouped = [kept("y_grouped%d" % h, [P, B, 4], BF16) for h in range(2)]
@@ -93,39 +92,42 @@ def tile_rp3beta_item_scores_k5_kernel(
                 out=prefs_raw[k][:], in_=prefs[256 * k : 256 * (k + 1), :].rearrange("(c p) i -> p c i", p=P)
             )
 
-        nc.vector.memset(rows_bf[:], 0.0)
-        for plane in (l_scales[0], r_scales[0]):
-            nc.vector.memset(plane[:].rearrange("p g n -> p (g n)").bitcast(I32), 0)
-        nc.vector.memset(warm_bf[:], 0.0)
-        nc.vector.quantize_mx(out=warm_codes[:].bitcast(FP8X4), scales=warm_scales[:], in_=warm_bf[:])
-        for plane in (l_scales[1], r_scales[1]):
-            nc.vector.memset(plane[:].rearrange("p g n -> p (g n)").bitcast(I32), 0)
+        def clear(tile_ap):
+            nc.vector.memset(tile_ap.bitcast(I32), 0)
 
-        nc.gpsimd.dma_start(out=rows_bf[0:8, :], in_=popularity.rearrange("(c n) -> c n", n=P))
-        nc.gpsimd.dma_start(out=rows_bf[8:20, :], in_=user_gain.rearrange("(c n) -> c n", n=P))
-        make_identity(nc, identity[:])
-        nc.gpsimd.memset(exponent[:], 1.0)
-        nc.gpsimd.tensor_scalar(out=exponent[:], in0=exponent[:], scalar1=-BETA, scalar2=0.0, op0=ALU.mult, op1=ALU.add)
-        nc.gpsimd.dma_start(out=bias_rows[:], in_=item_bias.rearrange("(c x) -> c x", x=32).unsqueeze(0).to_broadcast([4, 32, 32]))
+        with tc.manual_schedule():
+            clear(rows_bf[:])
+            clear(l_scales[0][:].rearrange("p g n -> p (g n)"))
+            clear(warm_bf[:])
+            clear(r_scales[0][:].rearrange("p g n -> p (g n)"))
+            nc.vector.quantize_mx(out=warm_codes[:].bitcast(FP8X4), scales=warm_scales[:], in_=warm_bf[:])
+            clear(l_scales[1][:].rearrange("p g n -> p (g n)"))
+            clear(r_scales[1][:].rearrange("p g n -> p (g n)"))
+            nc.gpsimd.dma_start(out=rows_bf[0:8, :], in_=popularity.rearrange("(c n) -> c n", n=P))
+            nc.gpsimd.dma_start(out=rows_bf[8:20, :], in_=user_gain.rearrange("(c n) -> c n", n=P))
+            make_identity(nc, identity[:])
+            nc.gpsimd.memset(exponent[:], 1.0)
+            nc.gpsimd.tensor_scalar(out=exponent[:], in0=exponent[:], scalar1=-BETA, scalar2=0.0, op0=ALU.mult, op1=ALU.add)
+            nc.gpsimd.dma_start(out=bias_rows[:], in_=item_bias.rearrange("(c x) -> c x", x=32).unsqueeze(0).to_broadcast([4, 32, 32]))
 
-        load_words(nc.sync, l_words, item_user_words, 0, 0, 1)
-        load_words(nc.scalar, r_words, user_item_words, 0, 0, 1)
-        load_scales(nc.sync, l_scales, item_user_scales, 0)
-        load_scales(nc.scalar, r_scales, user_item_scales, 0)
-        for g0, g1 in ((1, 2), (2, 4)):
-            load_words(nc.sync, l_words, item_user_words, 0, g0, g1)
-            load_words(nc.sync, r_words, user_item_words, 0, g0, g1)
-        load_scales(nc.sync, l_scales, item_user_scales, 1)
-        load_prefs(0)
-        load_prefs(1)
-        load_words(nc.sync, l_words, item_user_words, 1, 0, U_PASSES)
-        load_prefs(2)
-        load_prefs(3)
-        load_scales(nc.sync, r_scales, user_item_scales, 1)
-        load_prefs(4)
-        load_prefs(5)
-        load_words(nc.sync, r_words, user_item_words, 1, 0, U_PASSES)
+            load_words(nc.sync, l_words, item_user_words, 0, 0, 1)
+            load_words(nc.scalar, r_words, user_item_words, 0, 0, 1)
+            load_scales(nc.sync, l_scales, item_user_scales, 0)
+            load_scales(nc.scalar, r_scales, user_item_scales, 0)
+            for g0, g1 in ((1, 2), (2, 4)):
+                load_words(nc.sync, l_words, item_user_words, 0, g0, g1)
+                load_words(nc.sync, r_words, user_item_words, 0, g0, g1)
+            load_scales(nc.sync, l_scales, item_user_scales, 1)
+            load_words(nc.sync, l_words, item_user_words, 1, 0, U_PASSES)
+            load_prefs(0)
+            load_prefs(1)
+            load_scales(nc.sync, r_scales, user_item_scales, 1)
+            load_words(nc.sync, r_words, user_item_words, 1, 0, U_PASSES)
+            for k in range(2, 6):
+                load_prefs(k)
 
+
+        ctx.enter_context(tc.manual_schedule())
         nc.vector.tensor_copy(out=rows_f32[:], in_=rows_bf[:])
 
         def small():
@@ -155,6 +157,10 @@ def tile_rp3beta_item_scores_k5_kernel(
             else:
                 nc.scalar.copy(out=out, in_=in_)
 
+        banks = {}
+        y_f32 = {}
+        y_split = {}
+
         def walk_pass(bank, jt, ih, g):
             jh, c = divmod(jt, 4)
             nc.tensor.matmul_mx(
@@ -167,19 +173,25 @@ def tile_rp3beta_item_scores_k5_kernel(
                 stop=(g == U_PASSES - 1),
             )
 
-        def walk_out(bank, jt, ih):
+        def sweep():
+            for jt in range(4):
+                banks[("walk", jt, 0)] = next_bank()
+            for g in range(U_PASSES):
+                for jt in range(4):
+                    walk_pass(banks[("walk", jt, 0)], jt, 0, g)
+
+        def walk(jt, ih):
+            banks[("walk", jt, ih)] = next_bank()
+            for g in range(U_PASSES):
+                walk_pass(banks[("walk", jt, ih)], jt, ih, g)
+
+        def walk_out(jt, ih):
             nc.scalar.activation(
-                out=sim_t[jt][:, HALF * ih : HALF * (ih + 1)].rearrange("q (u m e) -> q u m e", u=2, e=2),
-                in_=bank[:].rearrange("q (m u e) -> q u m e", u=2, e=2),
+                out=sim_t[jt][:].rearrange("q (s n z) -> q s n z", s=4, z=16)[:, :, 8 * ih : 8 * (ih + 1), :],
+                in_=banks[("walk", jt, ih)][:].rearrange("q (n s z) -> q s n z", s=4, z=16),
                 func=ACT.Copy,
                 scale=damping[:, jt : jt + 1],
             )
-
-        def walk(jt, ih):
-            bank = next_bank()
-            for g in range(U_PASSES):
-                walk_pass(bank, jt, ih, g)
-            walk_out(bank, jt, ih)
 
         def turn(sources):
             bank = next_bank()
@@ -187,55 +199,61 @@ def tile_rp3beta_item_scores_k5_kernel(
                 nc.tensor.transpose(bank[:, P * s : P * (s + 1)], source, identity[:])
             return bank
 
-        def turn_sim(jt, engine):
-            jh, c = divmod(jt, 4)
+        def turn_sim(jt):
             words = sim_t[jt][:].bitcast(F32)
-            bank = turn([words[:, P * s : P * (s + 1)] for s in range(4)])
-            target = sim_grouped[jh][:].rearrange("q h j t -> q h (j t)").bitcast(F32)
+            banks[("sim", jt)] = turn([words[:, P * s : P * (s + 1)] for s in range(4)])
+
+        def sim_out(jt, engine):
+            target = sim_grouped[jt][:].rearrange("q g j t -> q (g j t)").bitcast(F32)
             copy_words(
                 engine,
-                target[:, :, 2 * P * c : 2 * P * (c + 1)].rearrange("q h (j u) -> q h j u", u=2),
-                bank[:].rearrange("q (h u j) -> q h j u", h=2, u=2),
+                target.rearrange("q (g j u) -> q g j u", g=2, u=2),
+                banks[("sim", jt)][:].rearrange("q (g u j) -> q g j u", g=2, u=2),
             )
-            if c == 3:
-                for ih in range(2):
-                    nc.vector.quantize_mx(
-                        out=sim_codes[jh][:, ih, :].bitcast(FP8X4),
-                        scales=sim_scales[jh][:, ih, :],
-                        in_=sim_grouped[jh][:, ih, :, :].rearrange("q j t -> q (j t)"),
-                    )
+
+        def quantize_sim(jt, g):
+            jh, c = divmod(jt, 4)
+            nc.vector.quantize_mx(
+                out=sim_codes[jh][:, g, P * c : P * (c + 1)].bitcast(FP8X4),
+                scales=sim_scales[jh][:, g, P * c : P * (c + 1)],
+                in_=sim_grouped[jt][:, g, :, :].rearrange("q j t -> q (j t)"),
+            )
 
         def split_prefs(k):
+            prefs_split[k] = work.tile([P, 2, I], BF16, name="prefs_split", tag="prefs_split", bufs=6, align_bytes=64)
             nc.vector.tensor_copy(
-                out=prefs_split[k][:].rearrange("q c i -> q (c i)").bitcast(F32).rearrange("q (s u m) -> q s u m", u=2, m=P),
-                in_=prefs_raw[k][:].rearrange("q c i -> q (c i)").bitcast(F32).rearrange("q (s m u) -> q s u m", u=2, m=P),
+                out=prefs_split[k][:].rearrange("q c i -> q (c i)").bitcast(F32).rearrange("q (s n r) -> q s n r", s=4, r=8),
+                in_=prefs_raw[k][:].rearrange("q c i -> q (c i)").bitcast(F32).rearrange("q (n s r) -> q s n r", s=4, r=8),
             )
 
-        def turn_prefs(bt, engine):
+        def turn_prefs(bt):
             k, c = divmod(bt, 2)
-            words = prefs_split[k][:, c, :].bitcast(F32)
-            bank = turn([words[:, P * s : P * (s + 1)] for s in range(4)])
-            target = prefs_grouped[k][:, c, :, :, :].rearrange("q g b t -> q g (b t)").bitcast(F32)
+            words = prefs_split[k][:].rearrange("q c i -> q (c i)").bitcast(F32)
+            banks[("prefs", bt)] = turn([words[:, P * (2 * s + c) : P * (2 * s + c + 1)] for s in range(4)])
+
+        def prefs_out(bt, engine):
+            prefs_grouped[bt] = work.tile([P, 2, P, 4], BF16, name="prefs_grouped", tag="prefs_grouped", bufs=6, align_bytes=64)
+            target = prefs_grouped[bt][:].rearrange("q g b t -> q (g b t)").bitcast(F32)
             copy_words(
                 engine,
-                target.rearrange("q g (b u) -> q g b u", u=2),
-                bank[:].rearrange("q (g u b) -> q g b u", g=2, u=2),
+                target.rearrange("q (g b u) -> q g b u", g=2, u=2),
+                banks[("prefs", bt)][:].rearrange("q (g u b) -> q g b u", g=2, u=2),
             )
-            if c == 1:
-                nc.vector.quantize_mx(
-                    out=prefs_codes[k][:].rearrange("q c g b -> q (c g b)").bitcast(FP8X4),
-                    scales=prefs_scales[k][:].rearrange("q c g b -> q (c g b)"),
-                    in_=prefs_grouped[k][:].rearrange("q c g b t -> q (c g b t)"),
-                )
 
-        y_split = {}
-
-        def score(bt, jh, cast_engine):
+        def quantize_prefs(bt):
             k, c = divmod(bt, 2)
-            bank = next_bank()
+            nc.vector.quantize_mx(
+                out=prefs_codes[k][:, c, :, :].rearrange("q g b -> q (g b)").bitcast(FP8X4),
+                scales=prefs_scales[k][:, c, :, :].rearrange("q g b -> q (g b)"),
+                in_=prefs_grouped[bt][:].rearrange("q g b t -> q (g b t)"),
+            )
+
+        def score(bt, jh):
+            k, c = divmod(bt, 2)
+            banks[("score", bt, jh)] = next_bank()
             for g in range(2):
                 nc.tensor.matmul_mx(
-                    out=bank[:],
+                    out=banks[("score", bt, jh)][:],
                     lhsT=prefs_codes[k][:, c, g, :].bitcast(FP8X4),
                     lhsT_scale=prefs_scales[k][:, c, g, :],
                     rhs=sim_codes[jh][:, g, :].bitcast(FP8X4),
@@ -243,34 +261,42 @@ def tile_rp3beta_item_scores_k5_kernel(
                     start=(g == 0),
                     stop=(g == 1),
                 )
-            y = work.tile([P, HALF], F32, name="y", tag="y", bufs=6)
+
+        def score_out(bt, jh):
+            y = work.tile([P, HALF], F32, name="y", tag="y", bufs=10)
             nc.vector.scalar_tensor_tensor(
-                out=y[:], in0=bank[:], scalar=columns[:, 8 + bt : 9 + bt],
+                out=y[:], in0=banks[("score", bt, jh)][:], scalar=columns[:, 8 + bt : 9 + bt],
                 in1=bias_all[:, HALF * jh : HALF * (jh + 1)], op0=ALU.mult, op1=ALU.add,
             )
             nc.sync.dma_start(out=out_0[P * bt : P * (bt + 1), HALF * jh : HALF * (jh + 1)], in_=y[:])
-            y_bf = work.tile([P, HALF], BF16, name="y_bf", tag="y_bf", bufs=10)
+            y_f32[(bt, jh)] = y
+
+        def round_y(bt, jh, engine):
+            y_bf = work.tile([P, HALF], BF16, name="y_bf", tag="y_bf", bufs=16)
             copy_words(
-                cast_engine,
+                engine,
                 y_bf[:].rearrange("q (u m e) -> q u m e", u=2, e=2),
-                y[:].rearrange("q (m u e) -> q u m e", u=2, e=2),
+                y_f32[(bt, jh)][:].rearrange("q (m u e) -> q u m e", u=2, e=2),
             )
             y_split[(bt, jh)] = y_bf
 
-        def turn_y(k, jh, engine):
+        def turn_y(bt, count, jh):
             sources = []
-            for c in range(2):
-                words = y_split[(2 * k + c, jh)][:].bitcast(F32)
+            for c in range(count):
+                words = y_split[(bt + c, jh)][:].bitcast(F32)
                 sources += [words[:, 0:P], words[:, P : 2 * P]]
-            bank = turn(sources)
-            target = y_grouped[jh][:, 256 * k : 256 * (k + 1), :].rearrange("q b t -> q (b t)").bitcast(F32)
+            banks[("y", bt, jh)] = turn(sources)
+
+        def y_out(bt, count, jh, engine):
+            target = y_grouped[jh][:, P * bt : P * (bt + count), :].rearrange("q b t -> q (b t)").bitcast(F32)
             copy_words(
                 engine,
-                target.rearrange("q (c b u) -> q c b u", c=2, u=2),
-                bank[:].rearrange("q (c u b) -> q c b u", c=2, u=2),
+                target.rearrange("q (c b u) -> q c b u", c=count, u=2),
+                banks[("y", bt, jh)][:, 0 : 2 * P * count].rearrange("q (c u b) -> q c b u", c=count, u=2),
             )
 
-        def planes_out(jh, b0, b1):
+        def planes_out(jh, bt0, bt1):
+            b0, b1 = P * bt0, P * bt1
             nc.vector.quantize_mx(
                 out=y_codes[jh][:, b0:b1].bitcast(FP8X4),
                 scales=y_scales[jh][:, b0:b1],
@@ -281,101 +307,236 @@ def tile_rp3beta_item_scores_k5_kernel(
                 in_=y_codes[jh][:, b0:b1].bitcast(I32),
             )
 
-        def scales_out(jh, b0, b1):
+        def scales_out(jh, bt0, bt1, last):
+            b0, b1 = P * bt0, P * bt1
             for r in range(4):
-                nc.sync.dma_start(
+                queue = nc.scalar if last and r % 2 == 0 else nc.sync
+                queue.dma_start(
                     out=out_2[jh, r:16:4, b0:b1].bitcast(I32), in_=y_scales[jh][r:P:32, b0:b1].bitcast(I32)
                 )
 
-        warm(16)
+        def bias_step(n):
+            if n == 0:
+                nc.vector.transpose(out=bias_cols[:], in_=bias_rows[:])
+            elif n == 1:
+                nc.vector.tensor_copy(out=bias_spread[:], in_=bias_cols[:].unsqueeze(2).to_broadcast([P, 32, 32]))
+            else:
+                nc.vector.transpose(out=bias_all[:], in_=bias_spread[:].rearrange("p c y -> p (c y)"))
+
+        warm(14)
         small()
-        bias_spreading()
-        split_prefs(0)
-        split_prefs(1)
-        split_prefs(2)
-        split_prefs(3)
-        split_prefs(4)
-        split_prefs(5)
-        first = [next_bank() for jt in range(4)]
-        for g in range(U_PASSES):
-            for jt in range(4):
-                walk_pass(first[jt], jt, 0, g)
-        for jt in range(4):
-            walk_out(first[jt], jt, 0)
-        turn_prefs(0, "v")
-        turn_prefs(1, "v")
-        turn_prefs(2, "v")
-        turn_prefs(3, "v")
-        walk(0, 1)
+        sweep()
         walk(1, 1)
+        bias_step(0)
+        walk_out(1, 0)
+        walk_out(3, 0)
+        walk_out(0, 0)
+        split_prefs(1)
+        walk(0, 1)
         walk(2, 1)
-        walk(3, 1)
-        turn_prefs(4, "v")
-        turn_prefs(5, "s")
-        turn_sim(0, "v")
-        turn_sim(1, "v")
-        turn_prefs(6, "s")
-        turn_prefs(7, "s")
-        turn_sim(2, "v")
-        turn_sim(3, "v")
-        walk(4, 0)
-        walk(4, 1)
-        walk(5, 0)
-        walk(5, 1)
-        score(0, 0, "s")
-        score(1, 0, "s")
-        score(2, 0, "s")
-        score(3, 0, "s")
-        turn_sim(4, "v")
-        turn_sim(5, "v")
-        turn_prefs(8, "s")
-        turn_prefs(9, "s")
-        turn_prefs(10, "v")
-        turn_prefs(11, "s")
-        turn_y(0, 0, "s")
-        turn_y(1, 0, "s")
-        planes_out(0, 0, 512)
+        walk_out(2, 0)
+        walk_out(0, 1)
+        split_prefs(0)
+        turn_sim(0)
+        turn_prefs(0)
+        walk_out(1, 1)
+        turn_sim(1)
+        turn_prefs(2)
+        sim_out(0, "s")
+        walk_out(2, 1)
+        bias_step(1)
+        sim_out(1, "s")
+        prefs_out(0, "s")
+        quantize_sim(0, 0)
         walk(6, 0)
+        turn_prefs(1)
+        turn_sim(2)
+        walk(3, 1)
+        walk(4, 0)
+        split_prefs(2)
+        bias_step(2)
+        walk_out(6, 0)
+        prefs_out(2, "s")
+        sim_out(2, "v")
+        turn_prefs(4)
+        walk_out(3, 1)
+        turn_sim(3)
+        turn_prefs(3)
+        quantize_sim(1, 1)
+        prefs_out(1, "v")
+        quantize_sim(0, 1)
+        split_prefs(4)
+        quantize_prefs(0)
+        walk(4, 1)
+        sim_out(3, "s")
+        walk_out(4, 0)
+        quantize_sim(1, 0)
+        quantize_prefs(1)
+        quantize_sim(2, 0)
+        quantize_sim(2, 1)
+        prefs_out(3, "s")
+        walk(5, 0)
+        quantize_sim(3, 0)
+        quantize_sim(3, 1)
+        score(0, 0)
+        walk_out(4, 1)
+        split_prefs(3)
+        quantize_prefs(3)
+        quantize_prefs(2)
+        score_out(0, 0)
+        round_y(0, 0, "g")
+        score(1, 0)
+        prefs_out(4, "s")
+        score_out(1, 0)
+        score(3, 0)
+        walk_out(5, 0)
+        quantize_prefs(4)
+        score(2, 0)
+        turn_prefs(5)
+        round_y(1, 0, "s")
+        turn_prefs(6)
+        turn_y(0, 2, 0)
+        turn_sim(4)
+        score_out(3, 0)
+        prefs_out(6, "s")
+        split_prefs(5)
+        prefs_out(5, "s")
+        sim_out(4, "s")
+        score_out(2, 0)
+        y_out(0, 2, 0, "v")
+        walk(5, 1)
+        score(4, 0)
+        turn_prefs(7)
+        turn_prefs(8)
+        walk_out(5, 1)
+        score_out(4, 0)
+        prefs_out(7, "v")
+        round_y(3, 0, "g")
+        turn_prefs(9)
+        turn_sim(5)
+        prefs_out(8, "s")
+        quantize_prefs(5)
+        quantize_prefs(6)
         walk(6, 1)
+        prefs_out(9, "s")
+        quantize_prefs(9)
+        score(5, 0)
+        score(6, 0)
+        quantize_prefs(8)
+        score(8, 0)
+        round_y(2, 0, "g")
+        walk_out(6, 1)
+        quantize_prefs(7)
+        score_out(5, 0)
+        score(7, 0)
+        score_out(6, 0)
+        sim_out(5, "s")
+        score_out(7, 0)
+        turn_y(2, 2, 0)
+        round_y(5, 0, "s")
+        score_out(8, 0)
+        turn_sim(6)
+        round_y(4, 0, "g")
+        round_y(6, 0, "g")
+        turn_y(4, 2, 0)
+        quantize_sim(5, 1)
+        sim_out(6, "v")
+        quantize_sim(4, 0)
+        y_out(2, 2, 0, "s")
+        y_out(4, 2, 0, "s")
+        quantize_sim(6, 1)
         walk(7, 0)
+        planes_out(0, 0, 4)
+        quantize_sim(4, 1)
+        quantize_sim(5, 0)
         walk(7, 1)
-        score(4, 0, "s")
-        score(5, 0, "s")
-        turn_sim(6, "v")
-        turn_sim(7, "v")
-        turn_y(2, 0, "s")
-        score(6, 0, "s")
-        score(7, 0, "s")
-        score(8, 0, "s")
-        score(9, 0, "s")
-        score(10, 0, "s")
-        score(11, 0, "s")
-        score(0, 1, "s")
-        score(1, 1, "v")
-        turn_y(3, 0, "s")
-        planes_out(0, 512, 1024)
-        turn_y(4, 0, "s")
-        turn_y(5, 0, "s")
-        planes_out(0, 1024, 1536)
-        turn_y(0, 1, "s")
-        scales_out(0, 0, 1536)
-        score(2, 1, "v")
-        score(3, 1, "s")
-        score(4, 1, "s")
-        score(5, 1, "v")
-        score(6, 1, "s")
-        score(7, 1, "s")
-        turn_y(1, 1, "s")
-        planes_out(1, 0, 512)
-        turn_y(2, 1, "s")
-        score(8, 1, "v")
-        score(9, 1, "s")
-        score(10, 1, "v")
-        score(11, 1, "v")
-        turn_y(3, 1, "s")
-        planes_out(1, 512, 1024)
-        turn_y(4, 1, "s")
-        planes_out(1, 1024, 1280)
-        turn_y(5, 1, "s")
-        planes_out(1, 1280, 1536)
-        scales_out(1, 0, 1536)
+        turn_prefs(11)
+        quantize_sim(6, 0)
+        turn_prefs(10)
+        round_y(8, 0, "g")
+        prefs_out(10, "v")
+        walk_out(7, 0)
+        walk_out(7, 1)
+        prefs_out(11, "s")
+        score(9, 0)
+        round_y(7, 0, "s")
+        quantize_prefs(11)
+        turn_sim(7)
+        turn_y(6, 2, 0)
+        sim_out(7, "s")
+        score(11, 0)
+        quantize_prefs(10)
+        score(10, 0)
+        score_out(9, 0)
+        quantize_sim(7, 0)
+        quantize_sim(7, 1)
+        score(1, 1)
+        y_out(6, 2, 0, "s")
+        score(3, 1)
+        score(2, 1)
+        score_out(11, 0)
+        round_y(11, 0, "s")
+        score(0, 1)
+        score_out(10, 0)
+        planes_out(0, 4, 8)
+        score_out(3, 1)
+        score_out(0, 1)
+        score(5, 1)
+        score_out(1, 1)
+        round_y(10, 0, "s")
+        score(4, 1)
+        round_y(0, 1, "g")
+        score_out(4, 1)
+        round_y(9, 0, "g")
+        score(6, 1)
+        score_out(2, 1)
+        round_y(4, 1, "g")
+        score(7, 1)
+        round_y(2, 1, "g")
+        score_out(5, 1)
+        round_y(1, 1, "s")
+        score_out(6, 1)
+        round_y(3, 1, "s")
+        turn_y(10, 2, 0)
+        turn_y(0, 2, 1)
+        turn_y(8, 2, 0)
+        score(9, 1)
+        score(8, 1)
+        score_out(7, 1)
+        y_out(0, 2, 1, "s")
+        y_out(8, 2, 0, "s")
+        round_y(5, 1, "s")
+        score_out(9, 1)
+        y_out(10, 2, 0, "s")
+        score_out(8, 1)
+        planes_out(0, 8, 12)
+        score(10, 1)
+        turn_y(4, 2, 1)
+        round_y(6, 1, "g")
+        scales_out(0, 0, 12, False)
+        turn_y(2, 2, 1)
+        y_out(2, 2, 1, "s")
+        score_out(10, 1)
+        y_out(4, 2, 1, "s")
+        round_y(7, 1, "g")
+        turn_y(6, 2, 1)
+        planes_out(1, 0, 4)
+        score(11, 1)
+        y_out(6, 2, 1, "s")
+        round_y(10, 1, "v")
+        planes_out(1, 4, 8)
+        turn_y(10, 1, 1)
+        round_y(8, 1, "s")
+        scales_out(1, 0, 8, False)
+        round_y(9, 1, "s")
+        score_out(11, 1)
+        y_out(10, 1, 1, "s")
+        turn_y(8, 2, 1)
+        y_out(8, 2, 1, "s")
+        round_y(11, 1, "v")
+        turn_y(11, 1, 1)
+        planes_out(1, 8, 10)
+        y_out(11, 1, 1, "s")
+        planes_out(1, 10, 11)
+        planes_out(1, 11, 12)
+        scales_out(1, 8, 12, True)

@@ -65,7 +65,10 @@ def tile_rp3beta_item_scores_k5_kernel(
         warm_codes = kept("warm_codes", [P, P], U32)
         warm_scales = kept("warm_scales", [P, P], U8)
         rows_f32 = kept("rows_f32", [P, P], F32)
-        columns = kept("columns", [P, 32], F32)
+        columns = kept("columns", [P, 16], F32)
+        pop_rows = kept("pop_rows", [P, 32], BF16)
+        pop_cols = kept("pop_cols", [P, 32], BF16)
+        pop_own = kept("pop_own", [P, 8], F32)
         exponent = kept("exponent", [P, 8], F32)
         damping = kept("damping", [P, 8], F32)
         identity = kept("identity", [P, P], F32)
@@ -95,25 +98,27 @@ def tile_rp3beta_item_scores_k5_kernel(
         def clear(tile_ap):
             nc.vector.memset(tile_ap.bitcast(I32), 0)
 
+        def spread_rows(vector):
+            return vector.rearrange("(c x) -> c x", x=32).unsqueeze(0).to_broadcast([4, 32, 32])
+
         with tc.manual_schedule():
-            clear(rows_bf[:])
             clear(l_scales[0][:].rearrange("p g n -> p (g n)"))
             clear(warm_bf[:])
             clear(r_scales[0][:].rearrange("p g n -> p (g n)"))
             nc.vector.quantize_mx(out=warm_codes[:].bitcast(FP8X4), scales=warm_scales[:], in_=warm_bf[:])
             clear(l_scales[1][:].rearrange("p g n -> p (g n)"))
             clear(r_scales[1][:].rearrange("p g n -> p (g n)"))
-            nc.gpsimd.dma_start(out=rows_bf[0:8, :], in_=popularity.rearrange("(c n) -> c n", n=P))
-            nc.gpsimd.dma_start(out=rows_bf[8:20, :], in_=user_gain.rearrange("(c n) -> c n", n=P))
-            make_identity(nc, identity[:])
+            clear(rows_bf[:])
+            nc.gpsimd.dma_start(out=pop_rows[:], in_=spread_rows(popularity))
             nc.gpsimd.memset(exponent[:], 1.0)
             nc.gpsimd.tensor_scalar(out=exponent[:], in0=exponent[:], scalar1=-BETA, scalar2=0.0, op0=ALU.mult, op1=ALU.add)
-            nc.gpsimd.dma_start(out=bias_rows[:], in_=item_bias.rearrange("(c x) -> c x", x=32).unsqueeze(0).to_broadcast([4, 32, 32]))
-
-            load_words(nc.sync, l_words, item_user_words, 0, 0, 1)
+            nc.gpsimd.dma_start(out=bias_rows[:], in_=spread_rows(item_bias))
+            nc.gpsimd.dma_start(out=rows_bf[0:12, :], in_=user_gain.rearrange("(c n) -> c n", n=P))
+            make_identity(nc, identity[:])
+            load_words(nc.scalar, l_words, item_user_words, 0, 0, 1)
             load_words(nc.scalar, r_words, user_item_words, 0, 0, 1)
             load_scales(nc.sync, l_scales, item_user_scales, 0)
-            load_scales(nc.scalar, r_scales, user_item_scales, 0)
+            load_scales(nc.sync, r_scales, user_item_scales, 0)
             for g0, g1 in ((1, 2), (2, 4)):
                 load_words(nc.sync, l_words, item_user_words, 0, g0, g1)
                 load_words(nc.sync, r_words, user_item_words, 0, g0, g1)
@@ -126,20 +131,19 @@ def tile_rp3beta_item_scores_k5_kernel(
             for k in range(2, 6):
                 load_prefs(k)
 
-
         ctx.enter_context(tc.manual_schedule())
+        nc.vector.transpose(out=pop_cols[:], in_=pop_rows[:])
+        for a in range(4):
+            nc.scalar.activation(out=pop_own[32 * a : 32 * (a + 1), :], in_=pop_cols[32 * a : 32 * (a + 1), a:32:4], func=ACT.Copy)
+        nc.gpsimd.tensor_tensor(out=damping[:], in0=pop_own[:], in1=exponent[:], op=ALU.pow)
         nc.vector.tensor_copy(out=rows_f32[:], in_=rows_bf[:])
 
-        def small():
-            small_bank = next_bank()
-            nc.tensor.transpose(small_bank[:, 0:P], rows_f32[:], identity[:])
-            nc.scalar.activation(out=columns[:], in_=small_bank[:, 0:32], func=ACT.Copy)
-            nc.gpsimd.tensor_tensor(out=damping[:], in0=columns[:, 0:8], in1=exponent[:], op=ALU.pow)
+        def turn_gain():
+            banks["gain"] = next_bank()
+            nc.tensor.transpose(banks["gain"][:, 0:P], rows_f32[:], identity[:])
 
-        def bias_spreading():
-            nc.vector.transpose(out=bias_cols[:], in_=bias_rows[:])
-            nc.vector.tensor_copy(out=bias_spread[:], in_=bias_cols[:].unsqueeze(2).to_broadcast([P, 32, 32]))
-            nc.vector.transpose(out=bias_all[:], in_=bias_spread[:].rearrange("p c y -> p (c y)"))
+        def gain_out():
+            nc.scalar.copy(out=columns[:], in_=banks["gain"][:, 0:16])
 
         def warm(n):
             bank = next_bank()
@@ -265,7 +269,7 @@ def tile_rp3beta_item_scores_k5_kernel(
         def score_out(bt, jh):
             y = work.tile([P, HALF], F32, name="y", tag="y", bufs=10)
             nc.vector.scalar_tensor_tensor(
-                out=y[:], in0=banks[("score", bt, jh)][:], scalar=columns[:, 8 + bt : 9 + bt],
+                out=y[:], in0=banks[("score", bt, jh)][:], scalar=columns[:, bt : bt + 1],
                 in1=bias_all[:, HALF * jh : HALF * (jh + 1)], op0=ALU.mult, op1=ALU.add,
             )
             nc.sync.dma_start(out=out_0[P * bt : P * (bt + 1), HALF * jh : HALF * (jh + 1)], in_=y[:])
@@ -295,17 +299,18 @@ def tile_rp3beta_item_scores_k5_kernel(
                 banks[("y", bt, jh)][:, 0 : 2 * P * count].rearrange("q (c u b) -> q c b u", c=count, u=2),
             )
 
-        def planes_out(jh, bt0, bt1):
+        def planes_out(jh, bt0, bt1, store_from):
             b0, b1 = P * bt0, P * bt1
             nc.vector.quantize_mx(
                 out=y_codes[jh][:, b0:b1].bitcast(FP8X4),
                 scales=y_scales[jh][:, b0:b1],
                 in_=y_grouped[jh][:, b0:b1, :].rearrange("q b t -> q (b t)"),
             )
-            nc.sync.dma_start(
-                out=out_1[jh].rearrange("p m t -> p (m t)").bitcast(I32)[:, b0:b1],
-                in_=y_codes[jh][:, b0:b1].bitcast(I32),
-            )
+            if store_from is not None:
+                nc.sync.dma_start(
+                    out=out_1[jh].rearrange("p m t -> p (m t)").bitcast(I32)[:, P * store_from : b1],
+                    in_=y_codes[jh][:, P * store_from : b1].bitcast(I32),
+                )
 
         def scales_out(jh, bt0, bt1, last):
             b0, b1 = P * bt0, P * bt1
@@ -323,220 +328,220 @@ def tile_rp3beta_item_scores_k5_kernel(
             else:
                 nc.vector.transpose(out=bias_all[:], in_=bias_spread[:].rearrange("p c y -> p (c y)"))
 
-        warm(14)
-        small()
+        warm(13)
         sweep()
-        walk(1, 1)
         bias_step(0)
-        walk_out(1, 0)
-        walk_out(3, 0)
         walk_out(0, 0)
-        split_prefs(1)
-        walk(0, 1)
-        walk(2, 1)
+        walk_out(1, 0)
         walk_out(2, 0)
-        walk_out(0, 1)
-        split_prefs(0)
-        turn_sim(0)
-        turn_prefs(0)
-        walk_out(1, 1)
-        turn_sim(1)
-        turn_prefs(2)
-        sim_out(0, "s")
-        walk_out(2, 1)
+        walk_out(3, 0)
         bias_step(1)
-        sim_out(1, "s")
-        prefs_out(0, "s")
-        quantize_sim(0, 0)
-        walk(6, 0)
-        turn_prefs(1)
-        turn_sim(2)
-        walk(3, 1)
-        walk(4, 0)
-        split_prefs(2)
+        split_prefs(0)
         bias_step(2)
-        walk_out(6, 0)
-        prefs_out(2, "s")
-        sim_out(2, "v")
-        turn_prefs(4)
-        walk_out(3, 1)
-        turn_sim(3)
-        turn_prefs(3)
-        quantize_sim(1, 1)
+        walk(0, 1)
+        walk_out(0, 1)
+        walk(1, 1)
+        walk_out(1, 1)
+        split_prefs(1)
+        walk(2, 1)
+        walk_out(2, 1)
+        turn_gain()
+        gain_out()
+        turn_sim(0)
+        sim_out(0, "s")
+        turn_prefs(0)
+        prefs_out(0, "s")
+        turn_prefs(1)
         prefs_out(1, "v")
+        turn_sim(1)
+        quantize_sim(0, 0)
         quantize_sim(0, 1)
-        split_prefs(4)
+        sim_out(1, "v")
+        split_prefs(2)
+        walk(3, 1)
         quantize_prefs(0)
-        walk(4, 1)
-        sim_out(3, "s")
-        walk_out(4, 0)
-        quantize_sim(1, 0)
+        walk_out(3, 1)
+        walk(4, 0)
         quantize_prefs(1)
+        walk_out(4, 0)
+        walk(6, 0)
+        quantize_sim(1, 0)
+        quantize_sim(1, 1)
+        walk_out(6, 0)
+        split_prefs(3)
+        turn_sim(2)
+        sim_out(2, "s")
+        turn_sim(3)
+        sim_out(3, "v")
+        turn_prefs(2)
+        prefs_out(2, "s")
+        turn_prefs(3)
         quantize_sim(2, 0)
         quantize_sim(2, 1)
-        prefs_out(3, "s")
-        walk(5, 0)
+        prefs_out(3, "v")
+        split_prefs(4)
+        walk(6, 1)
         quantize_sim(3, 0)
         quantize_sim(3, 1)
-        score(0, 0)
-        walk_out(4, 1)
-        split_prefs(3)
-        quantize_prefs(3)
-        quantize_prefs(2)
-        score_out(0, 0)
-        round_y(0, 0, "g")
-        score(1, 0)
-        prefs_out(4, "s")
-        score_out(1, 0)
-        score(3, 0)
-        walk_out(5, 0)
-        quantize_prefs(4)
-        score(2, 0)
-        turn_prefs(5)
-        round_y(1, 0, "s")
-        turn_prefs(6)
-        turn_y(0, 2, 0)
-        turn_sim(4)
-        score_out(3, 0)
-        prefs_out(6, "s")
-        split_prefs(5)
-        prefs_out(5, "s")
-        sim_out(4, "s")
-        score_out(2, 0)
-        y_out(0, 2, 0, "v")
-        walk(5, 1)
-        score(4, 0)
-        turn_prefs(7)
-        turn_prefs(8)
-        walk_out(5, 1)
-        score_out(4, 0)
-        prefs_out(7, "v")
-        round_y(3, 0, "g")
-        turn_prefs(9)
-        turn_sim(5)
-        prefs_out(8, "s")
-        quantize_prefs(5)
-        quantize_prefs(6)
-        walk(6, 1)
-        prefs_out(9, "s")
-        quantize_prefs(9)
-        score(5, 0)
-        score(6, 0)
-        quantize_prefs(8)
-        score(8, 0)
-        round_y(2, 0, "g")
         walk_out(6, 1)
-        quantize_prefs(7)
-        score_out(5, 0)
-        score(7, 0)
-        score_out(6, 0)
-        sim_out(5, "s")
-        score_out(7, 0)
-        turn_y(2, 2, 0)
-        round_y(5, 0, "s")
-        score_out(8, 0)
-        turn_sim(6)
-        round_y(4, 0, "g")
-        round_y(6, 0, "g")
-        turn_y(4, 2, 0)
-        quantize_sim(5, 1)
-        sim_out(6, "v")
-        quantize_sim(4, 0)
-        y_out(2, 2, 0, "s")
-        y_out(4, 2, 0, "s")
-        quantize_sim(6, 1)
+        walk(5, 0)
+        quantize_prefs(2)
+        walk_out(5, 0)
         walk(7, 0)
-        planes_out(0, 0, 4)
-        quantize_sim(4, 1)
-        quantize_sim(5, 0)
-        walk(7, 1)
-        turn_prefs(11)
-        quantize_sim(6, 0)
-        turn_prefs(10)
-        round_y(8, 0, "g")
-        prefs_out(10, "v")
+        quantize_prefs(3)
         walk_out(7, 0)
+        turn_prefs(4)
+        prefs_out(4, "v")
+        turn_prefs(5)
+        prefs_out(5, "s")
+        split_prefs(5)
+        turn_prefs(6)
+        prefs_out(6, "s")
+        turn_prefs(7)
+        quantize_prefs(4)
+        prefs_out(7, "v")
+        score(0, 0)
+        quantize_prefs(5)
+        score_out(0, 0)
+        score(1, 0)
+        quantize_prefs(6)
+        score_out(1, 0)
+        walk(4, 1)
+        quantize_prefs(7)
+        walk_out(4, 1)
+        score(2, 0)
+        round_y(0, 0, "g")
+        score_out(2, 0)
+        walk(5, 1)
+        round_y(1, 0, "g")
+        walk_out(5, 1)
+        score(3, 0)
+        score_out(3, 0)
+        score(4, 0)
+        round_y(2, 0, "g")
+        score_out(4, 0)
+        score(5, 0)
+        score_out(5, 0)
+        turn_sim(4)
+        round_y(3, 0, "g")
+        sim_out(4, "v")
+        turn_sim(5)
+        round_y(4, 0, "g")
+        sim_out(5, "s")
+        turn_sim(6)
+        round_y(5, 0, "g")
+        sim_out(6, "s")
+        turn_prefs(8)
+        quantize_sim(4, 0)
+        quantize_sim(4, 1)
+        prefs_out(8, "s")
+        walk(7, 1)
+        quantize_sim(5, 0)
+        quantize_sim(5, 1)
         walk_out(7, 1)
+        turn_prefs(9)
+        quantize_sim(6, 0)
+        quantize_sim(6, 1)
+        prefs_out(9, "s")
+        turn_y(0, 2, 0)
+        quantize_prefs(8)
+        y_out(0, 2, 0, "s")
+        turn_y(2, 2, 0)
+        y_out(2, 2, 0, "s")
+        score(6, 0)
+        quantize_prefs(9)
+        score_out(6, 0)
+        score(7, 0)
+        score_out(7, 0)
+        score(8, 0)
+        planes_out(0, 0, 4, 0)
+        score_out(8, 0)
+        turn_sim(7)
+        round_y(6, 0, "s")
+        sim_out(7, "s")
+        turn_prefs(10)
+        round_y(7, 0, "g")
+        prefs_out(10, "s")
+        turn_prefs(11)
+        round_y(8, 0, "s")
         prefs_out(11, "s")
         score(9, 0)
-        round_y(7, 0, "s")
-        quantize_prefs(11)
-        turn_sim(7)
-        turn_y(6, 2, 0)
-        sim_out(7, "s")
-        score(11, 0)
-        quantize_prefs(10)
-        score(10, 0)
-        score_out(9, 0)
         quantize_sim(7, 0)
         quantize_sim(7, 1)
-        score(1, 1)
-        y_out(6, 2, 0, "s")
-        score(3, 1)
-        score(2, 1)
-        score_out(11, 0)
-        round_y(11, 0, "s")
+        score_out(9, 0)
         score(0, 1)
-        score_out(10, 0)
-        planes_out(0, 4, 8)
-        score_out(3, 1)
+        quantize_prefs(10)
         score_out(0, 1)
-        score(5, 1)
+        score(1, 1)
+        quantize_prefs(11)
         score_out(1, 1)
-        round_y(10, 0, "s")
-        score(4, 1)
-        round_y(0, 1, "g")
-        score_out(4, 1)
-        round_y(9, 0, "g")
-        score(6, 1)
+        score(2, 1)
+        round_y(9, 0, "s")
         score_out(2, 1)
-        round_y(4, 1, "g")
-        score(7, 1)
-        round_y(2, 1, "g")
-        score_out(5, 1)
+        score(10, 0)
+        round_y(0, 1, "g")
+        score_out(10, 0)
+        score(3, 1)
         round_y(1, 1, "s")
-        score_out(6, 1)
-        round_y(3, 1, "s")
-        turn_y(10, 2, 0)
+        score_out(3, 1)
+        score(11, 0)
+        round_y(2, 1, "s")
+        score_out(11, 0)
+        score(4, 1)
+        round_y(10, 0, "g")
+        score_out(4, 1)
+        score(5, 1)
+        round_y(3, 1, "g")
+        score_out(5, 1)
+        turn_y(4, 2, 0)
+        round_y(11, 0, "g")
+        y_out(4, 2, 0, "s")
         turn_y(0, 2, 1)
-        turn_y(8, 2, 0)
-        score(9, 1)
-        score(8, 1)
-        score_out(7, 1)
+        round_y(4, 1, "g")
         y_out(0, 2, 1, "s")
+        turn_y(6, 2, 0)
+        round_y(5, 1, "g")
+        y_out(6, 2, 0, "s")
+        score(6, 1)
+        score_out(6, 1)
+        score(7, 1)
+        score_out(7, 1)
+        turn_y(8, 2, 0)
+        planes_out(0, 4, 8, 4)
         y_out(8, 2, 0, "s")
-        round_y(5, 1, "s")
-        score_out(9, 1)
+        turn_y(10, 2, 0)
+        round_y(6, 1, "s")
         y_out(10, 2, 0, "s")
-        score_out(8, 1)
-        planes_out(0, 8, 12)
-        score(10, 1)
-        turn_y(4, 2, 1)
-        round_y(6, 1, "g")
-        scales_out(0, 0, 12, False)
-        turn_y(2, 2, 1)
-        y_out(2, 2, 1, "s")
-        score_out(10, 1)
-        y_out(4, 2, 1, "s")
+        score(8, 1)
         round_y(7, 1, "g")
-        turn_y(6, 2, 1)
-        planes_out(1, 0, 4)
-        score(11, 1)
-        y_out(6, 2, 1, "s")
-        round_y(10, 1, "v")
-        planes_out(1, 4, 8)
-        turn_y(10, 1, 1)
+        score_out(8, 1)
+        score(9, 1)
+        score_out(9, 1)
+        turn_y(2, 2, 1)
+        planes_out(0, 8, 12, 8)
+        scales_out(0, 0, 12, False)
+        y_out(2, 2, 1, "s")
+        turn_y(4, 2, 1)
         round_y(8, 1, "s")
-        scales_out(1, 0, 8, False)
+        y_out(4, 2, 1, "s")
+        score(10, 1)
         round_y(9, 1, "s")
+        score_out(10, 1)
+        score(11, 1)
+        planes_out(1, 0, 4, 0)
         score_out(11, 1)
-        y_out(10, 1, 1, "s")
+        turn_y(6, 2, 1)
+        y_out(6, 2, 1, "s")
         turn_y(8, 2, 1)
+        round_y(10, 1, "g")
         y_out(8, 2, 1, "s")
+        turn_y(10, 1, 1)
         round_y(11, 1, "v")
+        y_out(10, 1, 1, "s")
         turn_y(11, 1, 1)
-        planes_out(1, 8, 10)
+        planes_out(1, 4, 8, 4)
         y_out(11, 1, 1, "s")
-        planes_out(1, 10, 11)
-        planes_out(1, 11, 12)
-        scales_out(1, 8, 12, True)
+        planes_out(1, 8, 10, 8)
+        planes_out(1, 10, 11, None)
+        planes_out(1, 11, 12, 10)
+        scales_out(1, 0, 12, True)

@@ -16,12 +16,22 @@ FP8X4 = mybir.dt.float8_e4m3fn_x4
 FP4X4 = mybir.dt.float4_e2m1fn_x4
 ALU = mybir.AluOpType
 ACT = mybir.ActivationFunctionType
-ENG = mybir.EngineType
 
 P = 128
+QUAD = 32
 HALF = 512
-U_PASSES = U // HALF
+U_PASSES = U // 512
+I_PASSES = I // 512
+ITEM_TILES = I // P
+USER_TILES = B // P
 BANKS = 8
+WARM_PASSES = 13
+
+ROUND_LAG = 4
+PREFS_LAG = 3
+REGROUP_LAG = 1
+SIM_LAG = 2
+PLANES_LAG = 2
 
 
 def tile_rp3beta_item_scores_k5_kernel(
@@ -29,16 +39,17 @@ def tile_rp3beta_item_scores_k5_kernel(
     popularity, prefs, user_gain, item_bias, out_0, out_1, out_2,
 ):
     nc = tc.nc
+    on_vector, on_scalar = nc.vector.tensor_copy, nc.scalar.copy
     with ExitStack() as ctx:
         keep = ctx.enter_context(tc.tile_pool(name="keep", bufs=1))
         work = ctx.enter_context(tc.tile_pool(name="work", bufs=3))
         psum = ctx.enter_context(tc.psum_pool(name="psum", bufs=1))
 
-        bank_count = [0]
+        banks_taken = [0]
 
         def next_bank():
-            k = bank_count[0] % BANKS
-            bank_count[0] += 1
+            k = banks_taken[0] % BANKS
+            banks_taken[0] += 1
             return psum.tile([P, HALF], F32, name="bank%d" % k, tag="bank%d" % k)
 
         def kept(name, shape, dtype):
@@ -48,34 +59,36 @@ def tile_rp3beta_item_scores_k5_kernel(
         r_words = [kept("r_words%d" % h, [P, U_PASSES, 2 * HALF], U8) for h in range(2)]
         l_scales = [kept("l_scales%d" % h, [P, U_PASSES, HALF], U8) for h in range(2)]
         r_scales = [kept("r_scales%d" % h, [P, U_PASSES, HALF], U8) for h in range(2)]
-        prefs_raw = [kept("prefs_raw%d" % k, [P, 2, I], BF16) for k in range(6)]
+        prefs_raw = [kept("prefs_raw%d" % k, [P, 2, I], BF16) for k in range(USER_TILES // 2)]
         prefs_split = {}
         prefs_grouped = {}
-        prefs_codes = [kept("prefs_codes%d" % k, [P, 2, 2, P], U32) for k in range(6)]
-        prefs_scales = [kept("prefs_scales%d" % k, [P, 2, 2, P], U8) for k in range(6)]
-        sim_t = [kept("sim_t%d" % jt, [P, I], BF16) for jt in range(8)]
-        sim_grouped = [kept("sim_grouped%d" % jt, [P, 2, P, 4], BF16) for jt in range(8)]
-        sim_codes = [kept("sim_codes%d" % h, [P, 2, HALF], U32) for h in range(2)]
-        sim_scales = [kept("sim_scales%d" % h, [P, 2, HALF], U8) for h in range(2)]
+        prefs_turned = {}
+        prefs_codes = [kept("prefs_codes%d" % k, [P, 2, I_PASSES, P], U32) for k in range(USER_TILES // 2)]
+        prefs_scales = [kept("prefs_scales%d" % k, [P, 2, I_PASSES, P], U8) for k in range(USER_TILES // 2)]
+        sim_t = [kept("sim_t%d" % jt, [P, I], BF16) for jt in range(ITEM_TILES)]
+        sim_grouped = [kept("sim_grouped%d" % jt, [P, I_PASSES, P, 4], BF16) for jt in range(ITEM_TILES)]
+        sim_codes = [kept("sim_codes%d" % h, [P, I_PASSES, HALF], U32) for h in range(2)]
+        sim_scales = [kept("sim_scales%d" % h, [P, I_PASSES, HALF], U8) for h in range(2)]
         y_grouped = [kept("y_grouped%d" % h, [P, B, 4], BF16) for h in range(2)]
         y_codes = [kept("y_codes%d" % h, [P, B], U32) for h in range(2)]
         y_scales = [kept("y_scales%d" % h, [P, B], U8) for h in range(2)]
-        rows_bf = kept("rows_bf", [P, P], BF16)
+        gain_rows = kept("gain_rows", [P, P], BF16)
         warm_bf = kept("warm_bf", [P, HALF], BF16)
         warm_codes = kept("warm_codes", [P, P], U32)
         warm_scales = kept("warm_scales", [P, P], U8)
-        rows_f32 = kept("rows_f32", [P, P], F32)
-        columns = kept("columns", [P, 16], F32)
-        pop_rows = kept("pop_rows", [P, 32], BF16)
-        pop_cols = kept("pop_cols", [P, 32], BF16)
-        pop_own = kept("pop_own", [P, 8], F32)
-        exponent = kept("exponent", [P, 8], F32)
-        damping = kept("damping", [P, 8], F32)
+        gain_rows_f32 = kept("gain_rows_f32", [P, P], F32)
+        gain_cols = kept("gain_cols", [P, 16], F32)
+        pop_rows = kept("pop_rows", [P, QUAD], BF16)
+        pop_cols = kept("pop_cols", [P, QUAD], BF16)
+        pop_own = kept("pop_own", [P, ITEM_TILES], F32)
+        exponent = kept("exponent", [P, ITEM_TILES], F32)
+        damping = kept("damping", [P, ITEM_TILES], F32)
         identity = kept("identity", [P, P], F32)
-        bias_rows = kept("bias_rows", [P, 32], BF16)
-        bias_cols = kept("bias_cols", [P, 32], BF16)
-        bias_spread = kept("bias_spread", [P, 32, 32], BF16)
+        bias_rows = kept("bias_rows", [P, QUAD], BF16)
+        bias_cols = kept("bias_cols", [P, QUAD], BF16)
+        bias_spread = kept("bias_spread", [P, QUAD, QUAD], BF16)
         bias_all = kept("bias_all", [P, I], BF16)
+
 
         def load_words(queue, dst, src, h, g0, g1):
             queue.dma_start(
@@ -83,23 +96,31 @@ def tile_rp3beta_item_scores_k5_kernel(
                 in_=src[g0:g1, :, 2 * HALF * h : 2 * HALF * (h + 1)].rearrange("g p n -> p g n").bitcast(I32),
             )
 
-        def load_scales(queue, dst, src, h):
+        def load_scales(dst, src, h):
             for r in range(4):
-                queue.dma_start(
-                    out=dst[h][r:P:32, :, :].bitcast(I32),
+                nc.sync.dma_start(
+                    out=dst[h][r:P:QUAD, :, :].bitcast(I32),
                     in_=src[:, r:16:4, HALF * h : HALF * (h + 1)].rearrange("g q n -> q g n").bitcast(I32),
+                )
+
+        def load_prefs_blocks(k):
+            for beta in range(2 * P // QUAD):
+                first = 2 * P * k + QUAD * beta
+                nc.sync.dma_start(
+                    out=prefs_raw[k][:].rearrange("q c i -> q (c i)")[:, 256 * beta : 256 * (beta + 1)],
+                    in_=prefs[first : first + QUAD, :].rearrange("y (a i) -> a y i", a=4),
                 )
 
         def load_prefs(k):
             nc.sync.dma_start(
-                out=prefs_raw[k][:], in_=prefs[256 * k : 256 * (k + 1), :].rearrange("(c p) i -> p c i", p=P)
+                out=prefs_raw[k][:], in_=prefs[2 * P * k : 2 * P * (k + 1), :].rearrange("(c p) i -> p c i", p=P)
             )
 
         def clear(tile_ap):
             nc.vector.memset(tile_ap.bitcast(I32), 0)
 
-        def spread_rows(vector):
-            return vector.rearrange("(c x) -> c x", x=32).unsqueeze(0).to_broadcast([4, 32, 32])
+        def rows_in_every_quadrant(vector):
+            return vector.rearrange("(c x) -> c x", x=QUAD).unsqueeze(0).to_broadcast([4, QUAD, QUAD])
 
         with tc.manual_schedule():
             clear(l_scales[0][:].rearrange("p g n -> p (g n)"))
@@ -108,62 +129,67 @@ def tile_rp3beta_item_scores_k5_kernel(
             nc.vector.quantize_mx(out=warm_codes[:].bitcast(FP8X4), scales=warm_scales[:], in_=warm_bf[:])
             clear(l_scales[1][:].rearrange("p g n -> p (g n)"))
             clear(r_scales[1][:].rearrange("p g n -> p (g n)"))
-            clear(rows_bf[:])
-            nc.gpsimd.dma_start(out=pop_rows[:], in_=spread_rows(popularity))
+            clear(gain_rows[:])
+            nc.gpsimd.dma_start(out=pop_rows[:], in_=rows_in_every_quadrant(popularity))
             nc.gpsimd.memset(exponent[:], 1.0)
-            nc.gpsimd.tensor_scalar(out=exponent[:], in0=exponent[:], scalar1=-BETA, scalar2=0.0, op0=ALU.mult, op1=ALU.add)
-            nc.gpsimd.dma_start(out=bias_rows[:], in_=spread_rows(item_bias))
-            nc.gpsimd.dma_start(out=rows_bf[0:12, :], in_=user_gain.rearrange("(c n) -> c n", n=P))
+            nc.gpsimd.tensor_scalar(
+                out=exponent[:], in0=exponent[:], scalar1=-BETA, scalar2=0.0, op0=ALU.mult, op1=ALU.add
+            )
+            nc.gpsimd.dma_start(out=bias_rows[:], in_=rows_in_every_quadrant(item_bias))
+            nc.gpsimd.dma_start(out=gain_rows[0:USER_TILES, :], in_=user_gain.rearrange("(c n) -> c n", n=P))
             make_identity(nc, identity[:])
             load_words(nc.scalar, l_words, item_user_words, 0, 0, 1)
             load_words(nc.scalar, r_words, user_item_words, 0, 0, 1)
-            load_scales(nc.sync, l_scales, item_user_scales, 0)
-            load_scales(nc.sync, r_scales, user_item_scales, 0)
-            for g0, g1 in ((1, 2), (2, 4)):
+            load_scales(l_scales, item_user_scales, 0)
+            load_scales(r_scales, user_item_scales, 0)
+            for g0, g1 in ((1, 2), (2, U_PASSES)):
                 load_words(nc.sync, l_words, item_user_words, 0, g0, g1)
                 load_words(nc.sync, r_words, user_item_words, 0, g0, g1)
-            load_scales(nc.sync, l_scales, item_user_scales, 1)
+            load_scales(l_scales, item_user_scales, 1)
             load_words(nc.sync, l_words, item_user_words, 1, 0, U_PASSES)
-            load_prefs(0)
-            load_prefs(1)
-            load_scales(nc.sync, r_scales, user_item_scales, 1)
+            load_prefs_blocks(0)
+            load_prefs_blocks(1)
+            load_scales(r_scales, user_item_scales, 1)
             load_words(nc.sync, r_words, user_item_words, 1, 0, U_PASSES)
-            for k in range(2, 6):
+            for k in range(2, USER_TILES // 2):
                 load_prefs(k)
 
         ctx.enter_context(tc.manual_schedule())
+
         nc.vector.transpose(out=pop_cols[:], in_=pop_rows[:])
         for a in range(4):
-            nc.scalar.activation(out=pop_own[32 * a : 32 * (a + 1), :], in_=pop_cols[32 * a : 32 * (a + 1), a:32:4], func=ACT.Copy)
+            quadrant = slice(QUAD * a, QUAD * (a + 1))
+            nc.scalar.activation(out=pop_own[quadrant, :], in_=pop_cols[quadrant, a:QUAD:4], func=ACT.Copy)
         nc.gpsimd.tensor_tensor(out=damping[:], in0=pop_own[:], in1=exponent[:], op=ALU.pow)
-        nc.vector.tensor_copy(out=rows_f32[:], in_=rows_bf[:])
+        nc.vector.tensor_copy(out=gain_rows_f32[:], in_=gain_rows[:])
 
-        def turn_gain():
-            banks["gain"] = next_bank()
-            nc.tensor.transpose(banks["gain"][:, 0:P], rows_f32[:], identity[:])
 
-        def gain_out():
-            nc.scalar.copy(out=columns[:], in_=banks["gain"][:, 0:16])
+        steps_done = [0]
+        waiting = []
 
-        def warm(n):
+        def later(lag, product, call):
+            waiting.append((steps_done[0] + lag, product, call))
+
+        def release(needed=(), everything=False):
+            for entry in list(waiting):
+                due, product, call = entry
+                if everything or (product in needed if needed else due <= steps_done[0]):
+                    waiting.remove(entry)
+                    call()
+
+        def tensor_step(needed, tensor_work, empty_bank):
+            steps_done[0] += 1
+            if needed:
+                release(needed)
             bank = next_bank()
-            for w in range(n):
-                nc.tensor.matmul_mx(
-                    out=bank[:, 0:P], lhsT=warm_codes[:].bitcast(FP8X4), lhsT_scale=warm_scales[:],
-                    rhs=warm_codes[:].bitcast(FP8X4), rhs_scale=warm_scales[:], start=True, stop=True,
-                )
+            tensor_work(bank)
+            release()
+            empty_bank(bank)
 
-        def copy_words(engine, out, in_):
-            if engine == "v":
-                nc.vector.tensor_copy(out=out, in_=in_)
-            elif engine == "g":
-                nc.gpsimd.tensor_scalar(out=out, in0=in_, scalar1=1.0, scalar2=0.0, op0=ALU.mult, op1=ALU.add)
-            else:
-                nc.scalar.copy(out=out, in_=in_)
+        def transposes(bank, sources):
+            for s, source in enumerate(sources):
+                nc.tensor.transpose(bank[:, P * s : P * (s + 1)], source, identity[:])
 
-        banks = {}
-        y_f32 = {}
-        y_split = {}
 
         def walk_pass(bank, jt, ih, g):
             jh, c = divmod(jt, 4)
@@ -177,72 +203,60 @@ def tile_rp3beta_item_scores_k5_kernel(
                 stop=(g == U_PASSES - 1),
             )
 
-        def sweep():
-            for jt in range(4):
-                banks[("walk", jt, 0)] = next_bank()
-            for g in range(U_PASSES):
-                for jt in range(4):
-                    walk_pass(banks[("walk", jt, 0)], jt, 0, g)
-
-        def walk(jt, ih):
-            banks[("walk", jt, ih)] = next_bank()
-            for g in range(U_PASSES):
-                walk_pass(banks[("walk", jt, ih)], jt, ih, g)
-
-        def walk_out(jt, ih):
+        def walk_out(bank, jt, ih):
             nc.scalar.activation(
                 out=sim_t[jt][:].rearrange("q (s n z) -> q s n z", s=4, z=16)[:, :, 8 * ih : 8 * (ih + 1), :],
-                in_=banks[("walk", jt, ih)][:].rearrange("q (n s z) -> q s n z", s=4, z=16),
+                in_=bank[:].rearrange("q (n s z) -> q s n z", s=4, z=16),
                 func=ACT.Copy,
                 scale=damping[:, jt : jt + 1],
             )
 
-        def turn(sources):
-            bank = next_bank()
-            for s, source in enumerate(sources):
-                nc.tensor.transpose(bank[:, P * s : P * (s + 1)], source, identity[:])
-            return bank
+        def walk(jt, ih):
+            def passes(bank):
+                for g in range(U_PASSES):
+                    walk_pass(bank, jt, ih, g)
 
-        def turn_sim(jt):
-            words = sim_t[jt][:].bitcast(F32)
-            banks[("sim", jt)] = turn([words[:, P * s : P * (s + 1)] for s in range(4)])
+            tensor_step((), passes, lambda bank: walk_out(bank, jt, ih))
 
-        def sim_out(jt, engine):
-            target = sim_grouped[jt][:].rearrange("q g j t -> q (g j t)").bitcast(F32)
-            copy_words(
-                engine,
-                target.rearrange("q (g j u) -> q g j u", g=2, u=2),
-                banks[("sim", jt)][:].rearrange("q (g u j) -> q g j u", g=2, u=2),
-            )
-
-        def quantize_sim(jt, g):
+        def turn_sim(jt, copy):
             jh, c = divmod(jt, 4)
-            nc.vector.quantize_mx(
-                out=sim_codes[jh][:, g, P * c : P * (c + 1)].bitcast(FP8X4),
-                scales=sim_scales[jh][:, g, P * c : P * (c + 1)],
-                in_=sim_grouped[jt][:, g, :, :].rearrange("q j t -> q (j t)"),
-            )
+            columns = slice(P * c, P * (c + 1))
+            pairs = sim_t[jt][:].bitcast(F32)
+
+            def group(bank):
+                target = sim_grouped[jt][:].rearrange("q g j t -> q (g j t)").bitcast(F32)
+                copy(
+                    out=target.rearrange("q (g j u) -> q g j u", g=I_PASSES, u=2),
+                    in_=bank[:].rearrange("q (g u j) -> q g j u", g=I_PASSES, u=2),
+                )
+
+            def quantize():
+                for g in range(I_PASSES):
+                    nc.vector.quantize_mx(
+                        out=sim_codes[jh][:, g, columns].bitcast(FP8X4),
+                        scales=sim_scales[jh][:, g, columns],
+                        in_=sim_grouped[jt][:, g, :, :].rearrange("q j t -> q (j t)"),
+                    )
+
+            tensor_step((), lambda bank: transposes(bank, [pairs[:, P * s : P * (s + 1)] for s in range(4)]), group)
+            later(SIM_LAG, ("sim", jh), quantize)
+
 
         def split_prefs(k):
             prefs_split[k] = work.tile([P, 2, I], BF16, name="prefs_split", tag="prefs_split", bufs=6, align_bytes=64)
+            target = prefs_split[k][:].rearrange("q c i -> q (c i)").bitcast(F32)
+            source = prefs_raw[k][:].rearrange("q c i -> q (c i)").bitcast(F32)
             nc.vector.tensor_copy(
-                out=prefs_split[k][:].rearrange("q c i -> q (c i)").bitcast(F32).rearrange("q (s n r) -> q s n r", s=4, r=8),
-                in_=prefs_raw[k][:].rearrange("q c i -> q (c i)").bitcast(F32).rearrange("q (n s r) -> q s n r", s=4, r=8),
+                out=target.rearrange("q (s n r) -> q s n r", s=4, r=8),
+                in_=source.rearrange("q (n s r) -> q s n r", s=4, r=8),
             )
 
-        def turn_prefs(bt):
-            k, c = divmod(bt, 2)
-            words = prefs_split[k][:].rearrange("q c i -> q (c i)").bitcast(F32)
-            banks[("prefs", bt)] = turn([words[:, P * (2 * s + c) : P * (2 * s + c + 1)] for s in range(4)])
-
-        def prefs_out(bt, engine):
-            prefs_grouped[bt] = work.tile([P, 2, P, 4], BF16, name="prefs_grouped", tag="prefs_grouped", bufs=6, align_bytes=64)
+        def group_prefs(bt, copy, source):
+            prefs_grouped[bt] = work.tile(
+                [P, I_PASSES, P, 4], BF16, name="prefs_grouped", tag="prefs_grouped", bufs=6, align_bytes=64
+            )
             target = prefs_grouped[bt][:].rearrange("q g b t -> q (g b t)").bitcast(F32)
-            copy_words(
-                engine,
-                target.rearrange("q (g b u) -> q g b u", g=2, u=2),
-                banks[("prefs", bt)][:].rearrange("q (g u b) -> q g b u", g=2, u=2),
-            )
+            copy(out=target.rearrange("q (g b u) -> q g b u", g=I_PASSES, u=2), in_=source)
 
         def quantize_prefs(bt):
             k, c = divmod(bt, 2)
@@ -252,296 +266,216 @@ def tile_rp3beta_item_scores_k5_kernel(
                 in_=prefs_grouped[bt][:].rearrange("q g b t -> q (g b t)"),
             )
 
-        def score(bt, jh):
+        def block_turn(k):
+            prefs_turned[k] = work.tile([P, I], F32, name="prefs_turned", tag="prefs_turned", bufs=2, align_bytes=64)
+            nc.vector.transpose(
+                out=prefs_turned[k][:], in_=prefs_split[k][:].rearrange("q c i -> q (c i)").bitcast(F32)
+            )
+
+        def regroup(bt, copy):
             k, c = divmod(bt, 2)
-            banks[("score", bt, jh)] = next_bank()
-            for g in range(2):
-                nc.tensor.matmul_mx(
-                    out=banks[("score", bt, jh)][:],
-                    lhsT=prefs_codes[k][:, c, g, :].bitcast(FP8X4),
-                    lhsT_scale=prefs_scales[k][:, c, g, :],
-                    rhs=sim_codes[jh][:, g, :].bitcast(FP8X4),
-                    rhs_scale=sim_scales[jh][:, g, :],
-                    start=(g == 0),
-                    stop=(g == 1),
+            turned = prefs_turned[k][:].rearrange("q (g u c b) -> q c g b u", g=I_PASSES, u=2, c=2)
+            group_prefs(bt, copy, turned[:, c, :, :, :])
+            later(REGROUP_LAG, ("prefs", bt), lambda: quantize_prefs(bt))
+
+        def turn_prefs(bt, copy):
+            k, c = divmod(bt, 2)
+            pairs = prefs_split[k][:].rearrange("q c i -> q (c i)").bitcast(F32)
+            tensor_step(
+                (),
+                lambda bank: transposes(bank, [pairs[:, P * (2 * s + c) : P * (2 * s + c + 1)] for s in range(4)]),
+                lambda bank: group_prefs(bt, copy, bank[:].rearrange("q (g u b) -> q g b u", g=I_PASSES, u=2)),
+            )
+            later(PREFS_LAG, ("prefs", bt), lambda: quantize_prefs(bt))
+
+
+        y_f32 = {}
+        y_split = {}
+
+        def score(bt, jh, copy):
+            k, c = divmod(bt, 2)
+            columns = slice(HALF * jh, HALF * (jh + 1))
+
+            def passes(bank):
+                for g in range(I_PASSES):
+                    nc.tensor.matmul_mx(
+                        out=bank[:],
+                        lhsT=prefs_codes[k][:, c, g, :].bitcast(FP8X4),
+                        lhsT_scale=prefs_scales[k][:, c, g, :],
+                        rhs=sim_codes[jh][:, g, :].bitcast(FP8X4),
+                        rhs_scale=sim_scales[jh][:, g, :],
+                        start=(g == 0),
+                        stop=(g == I_PASSES - 1),
+                    )
+
+            def finish(bank):
+                y_f32[(bt, jh)] = work.tile([P, HALF], F32, name="y", tag="y", bufs=10)
+                nc.vector.scalar_tensor_tensor(
+                    out=y_f32[(bt, jh)][:], in0=bank[:], scalar=gain_cols[:, bt : bt + 1],
+                    in1=bias_all[:, columns], op0=ALU.mult, op1=ALU.add,
+                )
+                nc.sync.dma_start(out=out_0[P * bt : P * (bt + 1), columns], in_=y_f32[(bt, jh)][:])
+
+            def round_y():
+                y_split[(bt, jh)] = work.tile([P, HALF], BF16, name="y_bf", tag="y_bf", bufs=16)
+                copy(
+                    out=y_split[(bt, jh)][:].rearrange("q (u m e) -> q u m e", u=2, e=2),
+                    in_=y_f32[(bt, jh)][:].rearrange("q (m u e) -> q u m e", u=2, e=2),
                 )
 
-        def score_out(bt, jh):
-            y = work.tile([P, HALF], F32, name="y", tag="y", bufs=10)
-            nc.vector.scalar_tensor_tensor(
-                out=y[:], in0=banks[("score", bt, jh)][:], scalar=columns[:, bt : bt + 1],
-                in1=bias_all[:, HALF * jh : HALF * (jh + 1)], op0=ALU.mult, op1=ALU.add,
-            )
-            nc.sync.dma_start(out=out_0[P * bt : P * (bt + 1), HALF * jh : HALF * (jh + 1)], in_=y[:])
-            y_f32[(bt, jh)] = y
+            tensor_step((("prefs", bt), ("sim", jh)), passes, finish)
+            later(ROUND_LAG, ("y", bt, jh), round_y)
 
-        def round_y(bt, jh, engine):
-            y_bf = work.tile([P, HALF], BF16, name="y_bf", tag="y_bf", bufs=16)
-            copy_words(
-                engine,
-                y_bf[:].rearrange("q (u m e) -> q u m e", u=2, e=2),
-                y_f32[(bt, jh)][:].rearrange("q (m u e) -> q u m e", u=2, e=2),
-            )
-            y_split[(bt, jh)] = y_bf
 
-        def turn_y(bt, count, jh):
-            sources = []
-            for c in range(count):
-                words = y_split[(bt + c, jh)][:].bitcast(F32)
-                sources += [words[:, 0:P], words[:, P : 2 * P]]
-            banks[("y", bt, jh)] = turn(sources)
+        def turn_y(bt, count, jh, copy):
+            def turn(bank):
+                pairs = [y_split[(bt + c, jh)][:].bitcast(F32) for c in range(count)]
+                transposes(bank, [tile_pairs[:, P * u : P * (u + 1)] for tile_pairs in pairs for u in range(2)])
 
-        def y_out(bt, count, jh, engine):
-            target = y_grouped[jh][:, P * bt : P * (bt + count), :].rearrange("q b t -> q (b t)").bitcast(F32)
-            copy_words(
-                engine,
-                target.rearrange("q (c b u) -> q c b u", c=count, u=2),
-                banks[("y", bt, jh)][:, 0 : 2 * P * count].rearrange("q (c u b) -> q c b u", c=count, u=2),
-            )
+            def group(bank):
+                target = y_grouped[jh][:, P * bt : P * (bt + count), :].rearrange("q b t -> q (b t)").bitcast(F32)
+                copy(
+                    out=target.rearrange("q (c b u) -> q c b u", c=count, u=2),
+                    in_=bank[:, 0 : 2 * P * count].rearrange("q (c u b) -> q c b u", c=count, u=2),
+                )
 
-        def planes_out(jh, bt0, bt1, store_from):
-            b0, b1 = P * bt0, P * bt1
+            tensor_step([("y", bt + c, jh) for c in range(count)], turn, group)
+
+        def quantize_y(jh, bt0, bt1):
+            users = slice(P * bt0, P * bt1)
             nc.vector.quantize_mx(
-                out=y_codes[jh][:, b0:b1].bitcast(FP8X4),
-                scales=y_scales[jh][:, b0:b1],
-                in_=y_grouped[jh][:, b0:b1, :].rearrange("q b t -> q (b t)"),
+                out=y_codes[jh][:, users].bitcast(FP8X4),
+                scales=y_scales[jh][:, users],
+                in_=y_grouped[jh][:, users, :].rearrange("q b t -> q (b t)"),
             )
-            if store_from is not None:
-                nc.sync.dma_start(
-                    out=out_1[jh].rearrange("p m t -> p (m t)").bitcast(I32)[:, P * store_from : b1],
-                    in_=y_codes[jh][:, P * store_from : b1].bitcast(I32),
-                )
 
-        def scales_out(jh, bt0, bt1, last):
-            b0, b1 = P * bt0, P * bt1
+        def store_codes(jh, bt0, bt1):
+            users = slice(P * bt0, P * bt1)
+            nc.sync.dma_start(
+                out=out_1[jh].rearrange("p m t -> p (m t)").bitcast(I32)[:, users],
+                in_=y_codes[jh][:, users].bitcast(I32),
+            )
+
+        def store_scales(jh, queues):
             for r in range(4):
-                queue = nc.scalar if last and r % 2 == 0 else nc.sync
-                queue.dma_start(
-                    out=out_2[jh, r:16:4, b0:b1].bitcast(I32), in_=y_scales[jh][r:P:32, b0:b1].bitcast(I32)
+                queues[r % len(queues)].dma_start(
+                    out=out_2[jh, r:16:4, :].bitcast(I32), in_=y_scales[jh][r:P:QUAD, :].bitcast(I32)
                 )
 
-        def bias_step(n):
-            if n == 0:
-                nc.vector.transpose(out=bias_cols[:], in_=bias_rows[:])
-            elif n == 1:
-                nc.vector.tensor_copy(out=bias_spread[:], in_=bias_cols[:].unsqueeze(2).to_broadcast([P, 32, 32]))
-            else:
-                nc.vector.transpose(out=bias_all[:], in_=bias_spread[:].rearrange("p c y -> p (c y)"))
+        def planes(jh, bt0, bt1, store_from):
+            def call():
+                quantize_y(jh, bt0, bt1)
+                if store_from is not None:
+                    store_codes(jh, store_from, bt1)
+                if bt1 == USER_TILES:
+                    store_scales(jh, [nc.scalar, nc.sync] if jh == 1 else [nc.sync])
 
-        warm(13)
-        sweep()
-        bias_step(0)
-        walk_out(0, 0)
-        walk_out(1, 0)
-        walk_out(2, 0)
-        walk_out(3, 0)
-        bias_step(1)
+            later(PLANES_LAG, ("planes", jh, bt0), call)
+
+
+        warm_bank = next_bank()
+        for w in range(WARM_PASSES):
+            nc.tensor.matmul_mx(
+                out=warm_bank[:, 0:P], lhsT=warm_codes[:].bitcast(FP8X4), lhsT_scale=warm_scales[:],
+                rhs=warm_codes[:].bitcast(FP8X4), rhs_scale=warm_scales[:], start=True, stop=True,
+            )
+
+        first_banks = [next_bank() for jt in range(4)]
+        for g in range(U_PASSES):
+            for jt in range(4):
+                walk_pass(first_banks[jt], jt, 0, g)
+        nc.vector.transpose(out=bias_cols[:], in_=bias_rows[:])
+        for jt in range(4):
+            walk_out(first_banks[jt], jt, 0)
+        nc.vector.tensor_copy(out=bias_spread[:], in_=bias_cols[:].unsqueeze(2).to_broadcast([P, QUAD, QUAD]))
+        nc.vector.transpose(out=bias_all[:], in_=bias_spread[:].rearrange("p c y -> p (c y)"))
+
         split_prefs(0)
-        bias_step(2)
-        walk(0, 1)
-        walk_out(0, 1)
-        walk(1, 1)
-        walk_out(1, 1)
         split_prefs(1)
+        walk(0, 1)
+        walk(1, 1)
+        block_turn(0)
         walk(2, 1)
-        walk_out(2, 1)
-        turn_gain()
-        gain_out()
-        turn_sim(0)
-        sim_out(0, "s")
-        turn_prefs(0)
-        prefs_out(0, "s")
-        turn_prefs(1)
-        prefs_out(1, "v")
-        turn_sim(1)
-        quantize_sim(0, 0)
-        quantize_sim(0, 1)
-        sim_out(1, "v")
-        split_prefs(2)
         walk(3, 1)
-        quantize_prefs(0)
-        walk_out(3, 1)
-        walk(4, 0)
-        quantize_prefs(1)
-        walk_out(4, 0)
-        walk(6, 0)
-        quantize_sim(1, 0)
-        quantize_sim(1, 1)
-        walk_out(6, 0)
+        gain_bank = next_bank()
+        transposes(gain_bank, [gain_rows_f32[:]])
+        nc.scalar.copy(out=gain_cols[:], in_=gain_bank[:, 0:16])
+        turn_sim(0, on_scalar)
+        block_turn(1)
+        turn_sim(1, on_scalar)
+        regroup(0, on_vector)
+        turn_sim(2, on_scalar)
+        split_prefs(2)
         split_prefs(3)
-        turn_sim(2)
-        sim_out(2, "s")
-        turn_sim(3)
-        sim_out(3, "v")
-        turn_prefs(2)
-        prefs_out(2, "s")
-        turn_prefs(3)
-        quantize_sim(2, 0)
-        quantize_sim(2, 1)
-        prefs_out(3, "v")
-        split_prefs(4)
-        walk(6, 1)
-        quantize_sim(3, 0)
-        quantize_sim(3, 1)
-        walk_out(6, 1)
-        walk(5, 0)
-        quantize_prefs(2)
-        walk_out(5, 0)
-        walk(7, 0)
-        quantize_prefs(3)
-        walk_out(7, 0)
-        turn_prefs(4)
-        prefs_out(4, "v")
-        turn_prefs(5)
-        prefs_out(5, "s")
-        split_prefs(5)
-        turn_prefs(6)
-        prefs_out(6, "s")
-        turn_prefs(7)
-        quantize_prefs(4)
-        prefs_out(7, "v")
-        score(0, 0)
-        quantize_prefs(5)
-        score_out(0, 0)
-        score(1, 0)
-        quantize_prefs(6)
-        score_out(1, 0)
+        turn_sim(3, on_scalar)
+        regroup(1, on_vector)
+        walk(4, 0)
+        regroup(2, on_scalar)
+        regroup(3, on_scalar)
         walk(4, 1)
-        quantize_prefs(7)
-        walk_out(4, 1)
-        score(2, 0)
-        round_y(0, 0, "g")
-        score_out(2, 0)
+        walk(5, 0)
         walk(5, 1)
-        round_y(1, 0, "g")
-        walk_out(5, 1)
-        score(3, 0)
-        score_out(3, 0)
-        score(4, 0)
-        round_y(2, 0, "g")
-        score_out(4, 0)
-        score(5, 0)
-        score_out(5, 0)
-        turn_sim(4)
-        round_y(3, 0, "g")
-        sim_out(4, "v")
-        turn_sim(5)
-        round_y(4, 0, "g")
-        sim_out(5, "s")
-        turn_sim(6)
-        round_y(5, 0, "g")
-        sim_out(6, "s")
-        turn_prefs(8)
-        quantize_sim(4, 0)
-        quantize_sim(4, 1)
-        prefs_out(8, "s")
+        split_prefs(4)
+        walk(6, 0)
+        score(0, 0, on_vector)
+        score(1, 0, on_scalar)
+        score(2, 0, on_vector)
+        split_prefs(5)
+        turn_prefs(4, on_scalar)
+        turn_prefs(5, on_scalar)
+        turn_prefs(6, on_scalar)
+        walk(6, 1)
+        score(3, 0, on_vector)
+        turn_prefs(7, on_scalar)
+        turn_prefs(8, on_vector)
+        turn_sim(4, on_scalar)
+        turn_y(0, 2, 0, on_scalar)
+        turn_sim(5, on_scalar)
+        turn_prefs(9, on_scalar)
+        turn_prefs(10, on_scalar)
+        turn_y(2, 2, 0, on_scalar)
+        planes(0, 0, 4, 0)
+        score(4, 0, on_scalar)
+        walk(7, 0)
+        score(5, 0, on_vector)
         walk(7, 1)
-        quantize_sim(5, 0)
-        quantize_sim(5, 1)
-        walk_out(7, 1)
-        turn_prefs(9)
-        quantize_sim(6, 0)
-        quantize_sim(6, 1)
-        prefs_out(9, "s")
-        turn_y(0, 2, 0)
-        quantize_prefs(8)
-        y_out(0, 2, 0, "s")
-        turn_y(2, 2, 0)
-        y_out(2, 2, 0, "s")
-        score(6, 0)
-        quantize_prefs(9)
-        score_out(6, 0)
-        score(7, 0)
-        score_out(7, 0)
-        score(8, 0)
-        planes_out(0, 0, 4, 0)
-        score_out(8, 0)
-        turn_sim(7)
-        round_y(6, 0, "s")
-        sim_out(7, "s")
-        turn_prefs(10)
-        round_y(7, 0, "g")
-        prefs_out(10, "s")
-        turn_prefs(11)
-        round_y(8, 0, "s")
-        prefs_out(11, "s")
-        score(9, 0)
-        quantize_sim(7, 0)
-        quantize_sim(7, 1)
-        score_out(9, 0)
-        score(0, 1)
-        quantize_prefs(10)
-        score_out(0, 1)
-        score(1, 1)
-        quantize_prefs(11)
-        score_out(1, 1)
-        score(2, 1)
-        round_y(9, 0, "s")
-        score_out(2, 1)
-        score(10, 0)
-        round_y(0, 1, "g")
-        score_out(10, 0)
-        score(3, 1)
-        round_y(1, 1, "s")
-        score_out(3, 1)
-        score(11, 0)
-        round_y(2, 1, "s")
-        score_out(11, 0)
-        score(4, 1)
-        round_y(10, 0, "g")
-        score_out(4, 1)
-        score(5, 1)
-        round_y(3, 1, "g")
-        score_out(5, 1)
-        turn_y(4, 2, 0)
-        round_y(11, 0, "g")
-        y_out(4, 2, 0, "s")
-        turn_y(0, 2, 1)
-        round_y(4, 1, "g")
-        y_out(0, 2, 1, "s")
-        turn_y(6, 2, 0)
-        round_y(5, 1, "g")
-        y_out(6, 2, 0, "s")
-        score(6, 1)
-        score_out(6, 1)
-        score(7, 1)
-        score_out(7, 1)
-        turn_y(8, 2, 0)
-        planes_out(0, 4, 8, 4)
-        y_out(8, 2, 0, "s")
-        turn_y(10, 2, 0)
-        round_y(6, 1, "s")
-        y_out(10, 2, 0, "s")
-        score(8, 1)
-        round_y(7, 1, "g")
-        score_out(8, 1)
-        score(9, 1)
-        score_out(9, 1)
-        turn_y(2, 2, 1)
-        planes_out(0, 8, 12, 8)
-        scales_out(0, 0, 12, False)
-        y_out(2, 2, 1, "s")
-        turn_y(4, 2, 1)
-        round_y(8, 1, "s")
-        y_out(4, 2, 1, "s")
-        score(10, 1)
-        round_y(9, 1, "s")
-        score_out(10, 1)
-        score(11, 1)
-        planes_out(1, 0, 4, 0)
-        score_out(11, 1)
-        turn_y(6, 2, 1)
-        y_out(6, 2, 1, "s")
-        turn_y(8, 2, 1)
-        round_y(10, 1, "g")
-        y_out(8, 2, 1, "s")
-        turn_y(10, 1, 1)
-        round_y(11, 1, "v")
-        y_out(10, 1, 1, "s")
-        turn_y(11, 1, 1)
-        planes_out(1, 4, 8, 4)
-        y_out(11, 1, 1, "s")
-        planes_out(1, 8, 10, 8)
-        planes_out(1, 10, 11, None)
-        planes_out(1, 11, 12, 10)
-        scales_out(1, 0, 12, True)
+        score(6, 0, on_scalar)
+        turn_sim(6, on_scalar)
+        score(7, 0, on_scalar)
+        score(8, 0, on_scalar)
+        turn_sim(7, on_scalar)
+        turn_prefs(11, on_scalar)
+        score(9, 0, on_scalar)
+        score(10, 0, on_scalar)
+        score(0, 1, on_scalar)
+        score(1, 1, on_vector)
+        score(2, 1, on_scalar)
+        score(3, 1, on_scalar)
+        turn_y(4, 2, 0, on_scalar)
+        turn_y(6, 2, 0, on_scalar)
+        planes(0, 4, 8, 4)
+        score(4, 1, on_scalar)
+        score(5, 1, on_scalar)
+        turn_y(0, 2, 1, on_scalar)
+        turn_y(8, 2, 0, on_scalar)
+        score(11, 0, on_scalar)
+        score(6, 1, on_scalar)
+        score(7, 1, on_scalar)
+        score(8, 1, on_scalar)
+        score(9, 1, on_scalar)
+        score(10, 1, on_vector)
+        turn_y(10, 2, 0, on_vector)
+        planes(0, 8, 12, 8)
+        score(11, 1, on_vector)
+        turn_y(2, 2, 1, on_scalar)
+        planes(1, 0, 4, 0)
+        turn_y(4, 2, 1, on_scalar)
+        turn_y(6, 2, 1, on_scalar)
+        planes(1, 4, 8, 4)
+        turn_y(8, 2, 1, on_scalar)
+        planes(1, 8, 10, 8)
+        turn_y(10, 1, 1, on_scalar)
+        planes(1, 10, 11, None)
+        turn_y(11, 1, 1, on_scalar)
+        planes(1, 11, 12, 10)
+        release(everything=True)

@@ -25,13 +25,12 @@ I_PASSES = I // 512
 ITEM_TILES = I // P
 USER_TILES = B // P
 BANKS = 8
-WARM_PASSES = 13
+WARM_PASSES = 20
 
-ROUND_LAG = 4
-PREFS_LAG = 3
-REGROUP_LAG = 1
-SIM_LAG = 2
-PLANES_LAG = 2
+ROUND_LAG = 3
+PREFS_LAG = 2
+SIM_LAG = 3
+PLANES_LAG = 3
 
 
 def tile_rp3beta_item_scores_k5_kernel(
@@ -40,6 +39,10 @@ def tile_rp3beta_item_scores_k5_kernel(
 ):
     nc = tc.nc
     on_vector, on_scalar = nc.vector.tensor_copy, nc.scalar.copy
+
+    def on_gpsimd(out, in_):
+        nc.gpsimd.tensor_scalar(out=out, in0=in_, scalar1=1.0, scalar2=0.0, op0=ALU.mult, op1=ALU.add)
+
     with ExitStack() as ctx:
         keep = ctx.enter_context(tc.tile_pool(name="keep", bufs=1))
         work = ctx.enter_context(tc.tile_pool(name="work", bufs=3))
@@ -62,7 +65,6 @@ def tile_rp3beta_item_scores_k5_kernel(
         prefs_raw = [kept("prefs_raw%d" % k, [P, 2, I], BF16) for k in range(USER_TILES // 2)]
         prefs_split = {}
         prefs_grouped = {}
-        prefs_turned = {}
         prefs_codes = [kept("prefs_codes%d" % k, [P, 2, I_PASSES, P], U32) for k in range(USER_TILES // 2)]
         prefs_scales = [kept("prefs_scales%d" % k, [P, 2, I_PASSES, P], U8) for k in range(USER_TILES // 2)]
         sim_t = [kept("sim_t%d" % jt, [P, I], BF16) for jt in range(ITEM_TILES)]
@@ -71,7 +73,7 @@ def tile_rp3beta_item_scores_k5_kernel(
         sim_scales = [kept("sim_scales%d" % h, [P, I_PASSES, HALF], U8) for h in range(2)]
         y_grouped = [kept("y_grouped%d" % h, [P, B, 4], BF16) for h in range(2)]
         y_codes = [kept("y_codes%d" % h, [P, B], U32) for h in range(2)]
-        y_scales = [kept("y_scales%d" % h, [P, B], U8) for h in range(2)]
+        y_scales = kept("y_scales", [P, 2, B], U8)
         gain_rows = kept("gain_rows", [P, P], BF16)
         warm_bf = kept("warm_bf", [P, HALF], BF16)
         warm_codes = kept("warm_codes", [P, P], U32)
@@ -101,14 +103,6 @@ def tile_rp3beta_item_scores_k5_kernel(
                 nc.sync.dma_start(
                     out=dst[h][r:P:QUAD, :, :].bitcast(I32),
                     in_=src[:, r:16:4, HALF * h : HALF * (h + 1)].rearrange("g q n -> q g n").bitcast(I32),
-                )
-
-        def load_prefs_blocks(k):
-            for beta in range(2 * P // QUAD):
-                first = 2 * P * k + QUAD * beta
-                nc.sync.dma_start(
-                    out=prefs_raw[k][:].rearrange("q c i -> q (c i)")[:, 256 * beta : 256 * (beta + 1)],
-                    in_=prefs[first : first + QUAD, :].rearrange("y (a i) -> a y i", a=4),
                 )
 
         def load_prefs(k):
@@ -147,8 +141,8 @@ def tile_rp3beta_item_scores_k5_kernel(
                 load_words(nc.sync, r_words, user_item_words, 0, g0, g1)
             load_scales(l_scales, item_user_scales, 1)
             load_words(nc.sync, l_words, item_user_words, 1, 0, U_PASSES)
-            load_prefs_blocks(0)
-            load_prefs_blocks(1)
+            load_prefs(0)
+            load_prefs(1)
             load_scales(r_scales, user_item_scales, 1)
             load_words(nc.sync, r_words, user_item_words, 1, 0, U_PASSES)
             for k in range(2, USER_TILES // 2):
@@ -266,18 +260,6 @@ def tile_rp3beta_item_scores_k5_kernel(
                 in_=prefs_grouped[bt][:].rearrange("q g b t -> q (g b t)"),
             )
 
-        def block_turn(k):
-            prefs_turned[k] = work.tile([P, I], F32, name="prefs_turned", tag="prefs_turned", bufs=2, align_bytes=64)
-            nc.vector.transpose(
-                out=prefs_turned[k][:], in_=prefs_split[k][:].rearrange("q c i -> q (c i)").bitcast(F32)
-            )
-
-        def regroup(bt, copy):
-            k, c = divmod(bt, 2)
-            turned = prefs_turned[k][:].rearrange("q (g u c b) -> q c g b u", g=I_PASSES, u=2, c=2)
-            group_prefs(bt, copy, turned[:, c, :, :, :])
-            later(REGROUP_LAG, ("prefs", bt), lambda: quantize_prefs(bt))
-
         def turn_prefs(bt, copy):
             k, c = divmod(bt, 2)
             pairs = prefs_split[k][:].rearrange("q c i -> q (c i)").bitcast(F32)
@@ -345,7 +327,7 @@ def tile_rp3beta_item_scores_k5_kernel(
             users = slice(P * bt0, P * bt1)
             nc.vector.quantize_mx(
                 out=y_codes[jh][:, users].bitcast(FP8X4),
-                scales=y_scales[jh][:, users],
+                scales=y_scales[:, jh, users],
                 in_=y_grouped[jh][:, users, :].rearrange("q b t -> q (b t)"),
             )
 
@@ -356,10 +338,12 @@ def tile_rp3beta_item_scores_k5_kernel(
                 in_=y_codes[jh][:, users].bitcast(I32),
             )
 
-        def store_scales(jh, queues):
+        def store_scales():
             for r in range(4):
-                queues[r % len(queues)].dma_start(
-                    out=out_2[jh, r:16:4, :].bitcast(I32), in_=y_scales[jh][r:P:QUAD, :].bitcast(I32)
+                queue = nc.scalar if r % 2 == 0 else nc.sync
+                queue.dma_start(
+                    out=out_2[:, r:16:4, :].rearrange("g q m -> q g m").bitcast(I32),
+                    in_=y_scales[r:P:QUAD, :, :].bitcast(I32),
                 )
 
         def planes(jh, bt0, bt1, store_from):
@@ -367,8 +351,6 @@ def tile_rp3beta_item_scores_k5_kernel(
                 quantize_y(jh, bt0, bt1)
                 if store_from is not None:
                     store_codes(jh, store_from, bt1)
-                if bt1 == USER_TILES:
-                    store_scales(jh, [nc.scalar, nc.sync] if jh == 1 else [nc.sync])
 
             later(PLANES_LAG, ("planes", jh, bt0), call)
 
@@ -388,88 +370,86 @@ def tile_rp3beta_item_scores_k5_kernel(
         for jt in range(4):
             walk_out(first_banks[jt], jt, 0)
         nc.vector.tensor_copy(out=bias_spread[:], in_=bias_cols[:].unsqueeze(2).to_broadcast([P, QUAD, QUAD]))
+        split_prefs(0)
         nc.vector.transpose(out=bias_all[:], in_=bias_spread[:].rearrange("p c y -> p (c y)"))
 
-        split_prefs(0)
-        split_prefs(1)
         walk(0, 1)
         walk(1, 1)
-        block_turn(0)
         walk(2, 1)
-        walk(3, 1)
         gain_bank = next_bank()
         transposes(gain_bank, [gain_rows_f32[:]])
         nc.scalar.copy(out=gain_cols[:], in_=gain_bank[:, 0:16])
-        turn_sim(0, on_scalar)
-        block_turn(1)
-        turn_sim(1, on_scalar)
-        regroup(0, on_vector)
-        turn_sim(2, on_scalar)
+        turn_prefs(0, on_scalar)
+        turn_prefs(1, on_scalar)
+        split_prefs(1)
+        walk(3, 1)
         split_prefs(2)
-        split_prefs(3)
-        turn_sim(3, on_scalar)
-        regroup(1, on_vector)
         walk(4, 0)
-        regroup(2, on_scalar)
-        regroup(3, on_scalar)
+        turn_prefs(2, on_vector)
+        turn_prefs(3, on_scalar)
+        split_prefs(3)
+        turn_sim(0, on_vector)
+        turn_sim(1, on_scalar)
+        turn_sim(2, on_scalar)
+        turn_sim(3, on_scalar)
         walk(4, 1)
-        walk(5, 0)
-        walk(5, 1)
-        split_prefs(4)
-        walk(6, 0)
-        score(0, 0, on_vector)
-        score(1, 0, on_scalar)
-        score(2, 0, on_vector)
-        split_prefs(5)
         turn_prefs(4, on_scalar)
-        turn_prefs(5, on_scalar)
-        turn_prefs(6, on_scalar)
-        walk(6, 1)
-        score(3, 0, on_vector)
+        turn_prefs(5, on_vector)
+        turn_prefs(6, on_vector)
         turn_prefs(7, on_scalar)
-        turn_prefs(8, on_vector)
-        turn_sim(4, on_scalar)
-        turn_y(0, 2, 0, on_scalar)
-        turn_sim(5, on_scalar)
-        turn_prefs(9, on_scalar)
-        turn_prefs(10, on_scalar)
-        turn_y(2, 2, 0, on_scalar)
-        planes(0, 0, 4, 0)
+        split_prefs(4)
+        walk(5, 0)
+        score(0, 0, on_vector)
+        split_prefs(5)
+        walk(5, 1)
+        score(1, 0, on_gpsimd)
+        walk(6, 0)
+        score(2, 0, on_scalar)
+        score(3, 0, on_vector)
         score(4, 0, on_scalar)
+        score(5, 0, on_scalar)
+        walk(6, 1)
+        score(6, 0, on_gpsimd)
         walk(7, 0)
-        score(5, 0, on_vector)
+        turn_y(0, 2, 0, on_scalar)
+        turn_y(2, 2, 0, on_vector)
+        planes(0, 0, 4, 0)
+        turn_prefs(8, on_scalar)
+        turn_prefs(9, on_vector)
+        turn_sim(4, on_scalar)
         walk(7, 1)
-        score(6, 0, on_scalar)
+        score(7, 0, on_vector)
+        turn_sim(5, on_scalar)
         turn_sim(6, on_scalar)
-        score(7, 0, on_scalar)
-        score(8, 0, on_scalar)
         turn_sim(7, on_scalar)
-        turn_prefs(11, on_scalar)
-        score(9, 0, on_scalar)
-        score(10, 0, on_scalar)
-        score(0, 1, on_scalar)
-        score(1, 1, on_vector)
-        score(2, 1, on_scalar)
-        score(3, 1, on_scalar)
+        score(8, 0, on_scalar)
+        turn_prefs(10, on_scalar)
         turn_y(4, 2, 0, on_scalar)
         turn_y(6, 2, 0, on_scalar)
         planes(0, 4, 8, 4)
+        score(9, 0, on_scalar)
+        score(0, 1, on_gpsimd)
+        score(1, 1, on_gpsimd)
+        score(2, 1, on_scalar)
+        score(10, 0, on_gpsimd)
+        score(3, 1, on_scalar)
+        turn_prefs(11, on_scalar)
         score(4, 1, on_scalar)
-        score(5, 1, on_scalar)
+        score(5, 1, on_gpsimd)
+        score(6, 1, on_gpsimd)
         turn_y(0, 2, 1, on_scalar)
-        turn_y(8, 2, 0, on_scalar)
-        score(11, 0, on_scalar)
-        score(6, 1, on_scalar)
-        score(7, 1, on_scalar)
-        score(8, 1, on_scalar)
-        score(9, 1, on_scalar)
-        score(10, 1, on_vector)
-        turn_y(10, 2, 0, on_vector)
-        planes(0, 8, 12, 8)
-        score(11, 1, on_vector)
         turn_y(2, 2, 1, on_scalar)
         planes(1, 0, 4, 0)
+        score(11, 0, on_scalar)
+        score(7, 1, on_gpsimd)
+        score(8, 1, on_scalar)
+        turn_y(8, 2, 0, on_scalar)
+        turn_y(10, 2, 0, on_scalar)
+        planes(0, 8, 12, 8)
+        score(9, 1, on_scalar)
+        score(10, 1, on_gpsimd)
         turn_y(4, 2, 1, on_scalar)
+        score(11, 1, on_vector)
         turn_y(6, 2, 1, on_scalar)
         planes(1, 4, 8, 4)
         turn_y(8, 2, 1, on_scalar)
@@ -479,3 +459,4 @@ def tile_rp3beta_item_scores_k5_kernel(
         turn_y(11, 1, 1, on_scalar)
         planes(1, 11, 12, 10)
         release(everything=True)
+        store_scales()

@@ -25,12 +25,14 @@ I_PASSES = I // 512
 ITEM_TILES = I // P
 USER_TILES = B // P
 BANKS = 8
-WARM_PASSES = 20
+WARM_N = 256
+WARM_PASSES = 7
 
 ROUND_LAG = 3
-PREFS_LAG = 2
+PREFS_LAG = 3
 SIM_LAG = 3
-PLANES_LAG = 3
+PLANES_LAG = 4
+LAST_LAG = 4
 
 
 def tile_rp3beta_item_scores_k5_kernel(
@@ -75,9 +77,9 @@ def tile_rp3beta_item_scores_k5_kernel(
         y_codes = [kept("y_codes%d" % h, [P, B], U32) for h in range(2)]
         y_scales = kept("y_scales", [P, 2, B], U8)
         gain_rows = kept("gain_rows", [P, P], BF16)
-        warm_bf = kept("warm_bf", [P, HALF], BF16)
-        warm_codes = kept("warm_codes", [P, P], U32)
-        warm_scales = kept("warm_scales", [P, P], U8)
+        warm_bf = kept("warm_bf", [P, 4 * WARM_N], BF16)
+        warm_codes = kept("warm_codes", [P, WARM_N], U32)
+        warm_scales = kept("warm_scales", [P, WARM_N], U8)
         gain_rows_f32 = kept("gain_rows_f32", [P, P], F32)
         gain_cols = kept("gain_cols", [P, 16], F32)
         pop_rows = kept("pop_rows", [P, QUAD], BF16)
@@ -116,46 +118,48 @@ def tile_rp3beta_item_scores_k5_kernel(
         def rows_in_every_quadrant(vector):
             return vector.rearrange("(c x) -> c x", x=QUAD).unsqueeze(0).to_broadcast([4, QUAD, QUAD])
 
-        with tc.manual_schedule():
-            clear(l_scales[0][:].rearrange("p g n -> p (g n)"))
-            clear(warm_bf[:])
-            clear(r_scales[0][:].rearrange("p g n -> p (g n)"))
-            nc.vector.quantize_mx(out=warm_codes[:].bitcast(FP8X4), scales=warm_scales[:], in_=warm_bf[:])
-            clear(l_scales[1][:].rearrange("p g n -> p (g n)"))
-            clear(r_scales[1][:].rearrange("p g n -> p (g n)"))
-            clear(gain_rows[:])
-            nc.gpsimd.dma_start(out=pop_rows[:], in_=rows_in_every_quadrant(popularity))
-            nc.gpsimd.memset(exponent[:], 1.0)
-            nc.gpsimd.tensor_scalar(
-                out=exponent[:], in0=exponent[:], scalar1=-BETA, scalar2=0.0, op0=ALU.mult, op1=ALU.add
-            )
-            nc.gpsimd.dma_start(out=bias_rows[:], in_=rows_in_every_quadrant(item_bias))
-            nc.gpsimd.dma_start(out=gain_rows[0:USER_TILES, :], in_=user_gain.rearrange("(c n) -> c n", n=P))
-            make_identity(nc, identity[:])
-            load_words(nc.scalar, l_words, item_user_words, 0, 0, 1)
-            load_words(nc.scalar, r_words, user_item_words, 0, 0, 1)
-            load_scales(l_scales, item_user_scales, 0)
-            load_scales(r_scales, user_item_scales, 0)
-            for g0, g1 in ((1, 2), (2, U_PASSES)):
-                load_words(nc.sync, l_words, item_user_words, 0, g0, g1)
-                load_words(nc.sync, r_words, user_item_words, 0, g0, g1)
-            load_scales(l_scales, item_user_scales, 1)
-            load_words(nc.sync, l_words, item_user_words, 1, 0, U_PASSES)
-            load_prefs(0)
-            load_prefs(1)
-            load_scales(r_scales, user_item_scales, 1)
-            load_words(nc.sync, r_words, user_item_words, 1, 0, U_PASSES)
-            for k in range(2, USER_TILES // 2):
-                load_prefs(k)
-
         ctx.enter_context(tc.manual_schedule())
+
+        nc.gpsimd.memset(warm_bf[:].bitcast(I32), 0)
+        clear(l_scales[0][:].rearrange("p g n -> p (g n)"))
+        clear(r_scales[0][:].rearrange("p g n -> p (g n)"))
+        nc.vector.quantize_mx(out=warm_codes[:].bitcast(FP8X4), scales=warm_scales[:], in_=warm_bf[:])
+        clear(l_scales[1][:].rearrange("p g n -> p (g n)"))
+        clear(identity[:])
+        make_identity(nc, identity[:], nomemset=True)
+        clear(r_scales[1][:].rearrange("p g n -> p (g n)"))
+        clear(gain_rows[:])
+        nc.vector.memset(exponent[:], 1.0)
+        nc.gpsimd.tensor_scalar(
+            out=exponent[:], in0=exponent[:], scalar1=-BETA, scalar2=0.0, op0=ALU.mult, op1=ALU.add
+        )
+        load_words(nc.scalar, l_words, item_user_words, 0, 0, 1)
+        load_words(nc.scalar, r_words, user_item_words, 0, 0, 1)
+        load_scales(l_scales, item_user_scales, 0)
+        load_scales(r_scales, user_item_scales, 0)
+        nc.sync.dma_start(out=pop_rows[:], in_=rows_in_every_quadrant(popularity))
+        for g0, g1 in ((1, 2), (2, U_PASSES)):
+            load_words(nc.sync, l_words, item_user_words, 0, g0, g1)
+            load_words(nc.sync, r_words, user_item_words, 0, g0, g1)
+        nc.sync.dma_start(out=bias_rows[:], in_=rows_in_every_quadrant(item_bias))
+        load_scales(l_scales, item_user_scales, 1)
+        load_words(nc.sync, l_words, item_user_words, 1, 0, U_PASSES)
+        load_prefs(0)
+        nc.sync.dma_start(out=gain_rows[0:USER_TILES, :], in_=user_gain.rearrange("(c n) -> c n", n=P))
+        load_prefs(1)
+        load_scales(r_scales, user_item_scales, 1)
+        load_words(nc.sync, r_words, user_item_words, 1, 0, U_PASSES)
+        for k in range(2, USER_TILES // 2):
+            load_prefs(k)
 
         nc.vector.transpose(out=pop_cols[:], in_=pop_rows[:])
         for a in range(4):
             quadrant = slice(QUAD * a, QUAD * (a + 1))
             nc.scalar.activation(out=pop_own[quadrant, :], in_=pop_cols[quadrant, a:QUAD:4], func=ACT.Copy)
         nc.gpsimd.tensor_tensor(out=damping[:], in0=pop_own[:], in1=exponent[:], op=ALU.pow)
-        nc.vector.tensor_copy(out=gain_rows_f32[:], in_=gain_rows[:])
+        nc.vector.transpose(out=bias_cols[:], in_=bias_rows[:])
+        nc.vector.tensor_copy(out=bias_spread[:], in_=bias_cols[:].unsqueeze(2).to_broadcast([P, QUAD, QUAD]))
+        nc.vector.transpose(out=bias_all[:], in_=bias_spread[:].rearrange("p c y -> p (c y)"))
 
 
         steps_done = [0]
@@ -198,12 +202,9 @@ def tile_rp3beta_item_scores_k5_kernel(
             )
 
         def walk_out(bank, jt, ih):
-            nc.scalar.activation(
-                out=sim_t[jt][:].rearrange("q (s n z) -> q s n z", s=4, z=16)[:, :, 8 * ih : 8 * (ih + 1), :],
-                in_=bank[:].rearrange("q (n s z) -> q s n z", s=4, z=16),
-                func=ACT.Copy,
-                scale=damping[:, jt : jt + 1],
-            )
+            target = sim_t[jt][:].rearrange("q (s n z) -> q s n z", s=4, z=16)[:, :, 8 * ih : 8 * (ih + 1), :]
+            source = bank[:].rearrange("q (n s z) -> q s n z", s=4, z=16)
+            nc.scalar.activation(out=target, in_=source, func=ACT.Copy, scale=damping[:, jt : jt + 1])
 
         def walk(jt, ih):
             def passes(bank):
@@ -213,8 +214,6 @@ def tile_rp3beta_item_scores_k5_kernel(
             tensor_step((), passes, lambda bank: walk_out(bank, jt, ih))
 
         def turn_sim(jt, copy):
-            jh, c = divmod(jt, 4)
-            columns = slice(P * c, P * (c + 1))
             pairs = sim_t[jt][:].bitcast(F32)
 
             def group(bank):
@@ -224,16 +223,18 @@ def tile_rp3beta_item_scores_k5_kernel(
                     in_=bank[:].rearrange("q (g u j) -> q g j u", g=I_PASSES, u=2),
                 )
 
-            def quantize():
-                for g in range(I_PASSES):
-                    nc.vector.quantize_mx(
-                        out=sim_codes[jh][:, g, columns].bitcast(FP8X4),
-                        scales=sim_scales[jh][:, g, columns],
-                        in_=sim_grouped[jt][:, g, :, :].rearrange("q j t -> q (j t)"),
-                    )
-
             tensor_step((), lambda bank: transposes(bank, [pairs[:, P * s : P * (s + 1)] for s in range(4)]), group)
-            later(SIM_LAG, ("sim", jh), quantize)
+            later(SIM_LAG, ("sim", jt // 4), lambda: quantize_sim(jt))
+
+        def quantize_sim(jt):
+            jh, c = divmod(jt, 4)
+            columns = slice(P * c, P * (c + 1))
+            for g in range(I_PASSES):
+                nc.vector.quantize_mx(
+                    out=sim_codes[jh][:, g, columns].bitcast(FP8X4),
+                    scales=sim_scales[jh][:, g, columns],
+                    in_=sim_grouped[jt][:, g, :, :].rearrange("q j t -> q (j t)"),
+                )
 
 
         def split_prefs(k):
@@ -246,18 +247,19 @@ def tile_rp3beta_item_scores_k5_kernel(
             )
 
         def group_prefs(bt, copy, source):
-            prefs_grouped[bt] = work.tile(
-                [P, I_PASSES, P, 4], BF16, name="prefs_grouped", tag="prefs_grouped", bufs=6, align_bytes=64
-            )
-            target = prefs_grouped[bt][:].rearrange("q g b t -> q (g b t)").bitcast(F32)
+            k, c = divmod(bt, 2)
+            if c == 0:
+                prefs_grouped[k] = work.tile(
+                    [P, 2 * I_PASSES * P * 4], BF16, name="prefs_grouped", tag="prefs_grouped", bufs=3, align_bytes=64
+                )
+            target = prefs_grouped[k][:, I * c : I * (c + 1)].bitcast(F32)
             copy(out=target.rearrange("q (g b u) -> q g b u", g=I_PASSES, u=2), in_=source)
 
-        def quantize_prefs(bt):
-            k, c = divmod(bt, 2)
+        def quantize_prefs(k):
             nc.vector.quantize_mx(
-                out=prefs_codes[k][:, c, :, :].rearrange("q g b -> q (g b)").bitcast(FP8X4),
-                scales=prefs_scales[k][:, c, :, :].rearrange("q g b -> q (g b)"),
-                in_=prefs_grouped[bt][:].rearrange("q g b t -> q (g b t)"),
+                out=prefs_codes[k][:].rearrange("q c g b -> q (c g b)").bitcast(FP8X4),
+                scales=prefs_scales[k][:].rearrange("q c g b -> q (c g b)"),
+                in_=prefs_grouped[k][:],
             )
 
         def turn_prefs(bt, copy):
@@ -268,45 +270,62 @@ def tile_rp3beta_item_scores_k5_kernel(
                 lambda bank: transposes(bank, [pairs[:, P * (2 * s + c) : P * (2 * s + c + 1)] for s in range(4)]),
                 lambda bank: group_prefs(bt, copy, bank[:].rearrange("q (g u b) -> q g b u", g=I_PASSES, u=2)),
             )
-            later(PREFS_LAG, ("prefs", bt), lambda: quantize_prefs(bt))
+            if c == 1:
+                later(PREFS_LAG, ("prefs", k), lambda: quantize_prefs(k))
 
 
         y_f32 = {}
         y_split = {}
 
-        def score(bt, jh, copy):
+        def score_passes(bank, bt, jh):
             k, c = divmod(bt, 2)
+            for g in range(I_PASSES):
+                nc.tensor.matmul_mx(
+                    out=bank[:],
+                    lhsT=prefs_codes[k][:, c, g, :].bitcast(FP8X4),
+                    lhsT_scale=prefs_scales[k][:, c, g, :],
+                    rhs=sim_codes[jh][:, g, :].bitcast(FP8X4),
+                    rhs_scale=sim_scales[jh][:, g, :],
+                    start=(g == 0),
+                    stop=(g == I_PASSES - 1),
+                )
+
+        def gain_and_bias(out, scores, bias, bt):
+            nc.vector.scalar_tensor_tensor(
+                out=out, in0=scores, scalar=gain_cols[:, bt : bt + 1], in1=bias, op0=ALU.mult, op1=ALU.add
+            )
+
+        def finish_y(bank, bt, jh):
             columns = slice(HALF * jh, HALF * (jh + 1))
+            y_f32[(bt, jh)] = work.tile([P, HALF], F32, name="y", tag="y", bufs=12)
+            gain_and_bias(y_f32[(bt, jh)][:], bank[:], bias_all[:, columns], bt)
+            nc.sync.dma_start(out=out_0[P * bt : P * (bt + 1), columns], in_=y_f32[(bt, jh)][:])
 
-            def passes(bank):
-                for g in range(I_PASSES):
-                    nc.tensor.matmul_mx(
-                        out=bank[:],
-                        lhsT=prefs_codes[k][:, c, g, :].bitcast(FP8X4),
-                        lhsT_scale=prefs_scales[k][:, c, g, :],
-                        rhs=sim_codes[jh][:, g, :].bitcast(FP8X4),
-                        rhs_scale=sim_scales[jh][:, g, :],
-                        start=(g == 0),
-                        stop=(g == I_PASSES - 1),
-                    )
+        def by_pairs(columns):
+            return columns.rearrange("q (m u e) -> q u m e", u=2, e=2)
 
-            def finish(bank):
-                y_f32[(bt, jh)] = work.tile([P, HALF], F32, name="y", tag="y", bufs=10)
-                nc.vector.scalar_tensor_tensor(
-                    out=y_f32[(bt, jh)][:], in0=bank[:], scalar=gain_cols[:, bt : bt + 1],
-                    in1=bias_all[:, columns], op0=ALU.mult, op1=ALU.add,
-                )
-                nc.sync.dma_start(out=out_0[P * bt : P * (bt + 1), columns], in_=y_f32[(bt, jh)][:])
+        def new_y_split(bt, jh):
+            y_split[(bt, jh)] = work.tile([P, HALF], BF16, name="y_bf", tag="y_bf", bufs=16)
+            return y_split[(bt, jh)][:].rearrange("q (u m e) -> q u m e", u=2, e=2)
 
-            def round_y():
-                y_split[(bt, jh)] = work.tile([P, HALF], BF16, name="y_bf", tag="y_bf", bufs=16)
-                copy(
-                    out=y_split[(bt, jh)][:].rearrange("q (u m e) -> q u m e", u=2, e=2),
-                    in_=y_f32[(bt, jh)][:].rearrange("q (m u e) -> q u m e", u=2, e=2),
-                )
+        def score(bt, jh):
+            copy = on_scalar if bt % 2 else on_gpsimd
+            tensor_step(
+                (("prefs", bt // 2), ("sim", jh)),
+                lambda bank: score_passes(bank, bt, jh),
+                lambda bank: finish_y(bank, bt, jh),
+            )
+            later(ROUND_LAG, ("y", bt, jh), lambda: copy(out=new_y_split(bt, jh), in_=by_pairs(y_f32[(bt, jh)][:])))
 
-            tensor_step((("prefs", bt), ("sim", jh)), passes, finish)
-            later(ROUND_LAG, ("y", bt, jh), round_y)
+        def last_score(bt, jh):
+            def rounded(bank):
+                target = new_y_split(bt, jh)
+                for u in range(2):
+                    bias = by_pairs(bias_all[:, HALF * jh : HALF * (jh + 1)])
+                    gain_and_bias(target[:, u], by_pairs(bank[:])[:, u], bias[:, u], bt)
+                later(LAST_LAG, ("y32", bt, jh), lambda: finish_y(bank, bt, jh))
+
+            tensor_step((), lambda bank: score_passes(bank, bt, jh), rounded)
 
 
         def turn_y(bt, count, jh, copy):
@@ -338,27 +357,38 @@ def tile_rp3beta_item_scores_k5_kernel(
                 in_=y_codes[jh][:, users].bitcast(I32),
             )
 
-        def store_scales():
+        def store_scales(jh, bt0, bt1, queues):
+            users = slice(P * bt0, P * bt1)
             for r in range(4):
-                queue = nc.scalar if r % 2 == 0 else nc.sync
-                queue.dma_start(
-                    out=out_2[:, r:16:4, :].rearrange("g q m -> q g m").bitcast(I32),
-                    in_=y_scales[r:P:QUAD, :, :].bitcast(I32),
+                queues[r % len(queues)].dma_start(
+                    out=out_2[jh, r:16:4, users].bitcast(I32), in_=y_scales[r:P:QUAD, jh, users].bitcast(I32)
                 )
 
-        def planes(jh, bt0, bt1, store_from):
-            def call():
-                quantize_y(jh, bt0, bt1)
-                if store_from is not None:
-                    store_codes(jh, store_from, bt1)
+        def planes(jh, bt0, bt1):
+            quantize_y(jh, bt0, bt1)
+            store_codes(jh, bt0, bt1)
 
-            later(PLANES_LAG, ("planes", jh, bt0), call)
+        def planes_later(jh, bt0, bt1):
+            later(PLANES_LAG, ("planes", jh, bt0), lambda: planes(jh, bt0, bt1))
+
+        def in_turn(steps, first, second):
+            for n, step in enumerate(steps):
+                step(second if n % 2 else first)
+
+        def prefs_steps(tiles):
+            return [lambda copy, bt=bt: turn_prefs(bt, copy) for bt in tiles]
+
+        def sim_steps(tiles):
+            return [lambda copy, jt=jt: turn_sim(jt, copy) for jt in tiles]
+
+        def y_steps(tiles, jh):
+            return [lambda copy, bt=bt: turn_y(bt, 2, jh, copy) for bt in tiles]
 
 
         warm_bank = next_bank()
         for w in range(WARM_PASSES):
             nc.tensor.matmul_mx(
-                out=warm_bank[:, 0:P], lhsT=warm_codes[:].bitcast(FP8X4), lhsT_scale=warm_scales[:],
+                out=warm_bank[:, 0:WARM_N], lhsT=warm_codes[:, 0:P].bitcast(FP8X4), lhsT_scale=warm_scales[:, 0:P],
                 rhs=warm_codes[:].bitcast(FP8X4), rhs_scale=warm_scales[:], start=True, stop=True,
             )
 
@@ -366,97 +396,77 @@ def tile_rp3beta_item_scores_k5_kernel(
         for g in range(U_PASSES):
             for jt in range(4):
                 walk_pass(first_banks[jt], jt, 0, g)
-        nc.vector.transpose(out=bias_cols[:], in_=bias_rows[:])
         for jt in range(4):
             walk_out(first_banks[jt], jt, 0)
-        nc.vector.tensor_copy(out=bias_spread[:], in_=bias_cols[:].unsqueeze(2).to_broadcast([P, QUAD, QUAD]))
-        split_prefs(0)
-        nc.vector.transpose(out=bias_all[:], in_=bias_spread[:].rearrange("p c y -> p (c y)"))
 
+        split_prefs(0)
         walk(0, 1)
+        split_prefs(1)
         walk(1, 1)
         walk(2, 1)
-        gain_bank = next_bank()
-        transposes(gain_bank, [gain_rows_f32[:]])
-        nc.scalar.copy(out=gain_cols[:], in_=gain_bank[:, 0:16])
-        turn_prefs(0, on_scalar)
-        turn_prefs(1, on_scalar)
-        split_prefs(1)
-        walk(3, 1)
+        nc.vector.tensor_copy(out=gain_rows_f32[:], in_=gain_rows[:])
+        tensor_step(
+            (),
+            lambda bank: transposes(bank, [gain_rows_f32[:]]),
+            lambda bank: nc.vector.tensor_copy(out=gain_cols[:], in_=bank[:, 0:16]),
+        )
+        in_turn(prefs_steps((0, 1)) + sim_steps((0, 1)), on_vector, on_scalar)
         split_prefs(2)
+        walk(3, 1)
         walk(4, 0)
-        turn_prefs(2, on_vector)
-        turn_prefs(3, on_scalar)
+        in_turn(sim_steps((2, 3)) + prefs_steps(range(2, 6)), on_vector, on_scalar)
+
         split_prefs(3)
-        turn_sim(0, on_vector)
-        turn_sim(1, on_scalar)
-        turn_sim(2, on_scalar)
-        turn_sim(3, on_scalar)
         walk(4, 1)
-        turn_prefs(4, on_scalar)
-        turn_prefs(5, on_vector)
-        turn_prefs(6, on_vector)
-        turn_prefs(7, on_scalar)
         split_prefs(4)
-        walk(5, 0)
-        score(0, 0, on_vector)
+        score(0, 0)
+        score(1, 0)
         split_prefs(5)
+        walk(5, 0)
+        score(2, 0)
+        score(3, 0)
+        in_turn(prefs_steps(range(6, USER_TILES)), on_scalar, on_vector)
         walk(5, 1)
-        score(1, 0, on_gpsimd)
+        score(4, 0)
+        score(5, 0)
         walk(6, 0)
-        score(2, 0, on_scalar)
-        score(3, 0, on_vector)
-        score(4, 0, on_scalar)
-        score(5, 0, on_scalar)
+        score(6, 0)
+        score(7, 0)
+        in_turn(y_steps((0, 2), 0), on_scalar, on_vector)
+        planes_later(0, 0, 4)
+        in_turn(sim_steps((4, 5)), on_scalar, on_vector)
+
         walk(6, 1)
-        score(6, 0, on_gpsimd)
         walk(7, 0)
-        turn_y(0, 2, 0, on_scalar)
-        turn_y(2, 2, 0, on_vector)
-        planes(0, 0, 4, 0)
-        turn_prefs(8, on_scalar)
-        turn_prefs(9, on_vector)
-        turn_sim(4, on_scalar)
         walk(7, 1)
-        score(7, 0, on_vector)
-        turn_sim(5, on_scalar)
-        turn_sim(6, on_scalar)
-        turn_sim(7, on_scalar)
-        score(8, 0, on_scalar)
-        turn_prefs(10, on_scalar)
-        turn_y(4, 2, 0, on_scalar)
-        turn_y(6, 2, 0, on_scalar)
-        planes(0, 4, 8, 4)
-        score(9, 0, on_scalar)
-        score(0, 1, on_gpsimd)
-        score(1, 1, on_gpsimd)
-        score(2, 1, on_scalar)
-        score(10, 0, on_gpsimd)
-        score(3, 1, on_scalar)
-        turn_prefs(11, on_scalar)
-        score(4, 1, on_scalar)
-        score(5, 1, on_gpsimd)
-        score(6, 1, on_gpsimd)
-        turn_y(0, 2, 1, on_scalar)
-        turn_y(2, 2, 1, on_scalar)
-        planes(1, 0, 4, 0)
-        score(11, 0, on_scalar)
-        score(7, 1, on_gpsimd)
-        score(8, 1, on_scalar)
-        turn_y(8, 2, 0, on_scalar)
-        turn_y(10, 2, 0, on_scalar)
-        planes(0, 8, 12, 8)
-        score(9, 1, on_scalar)
-        score(10, 1, on_gpsimd)
-        turn_y(4, 2, 1, on_scalar)
-        score(11, 1, on_vector)
-        turn_y(6, 2, 1, on_scalar)
-        planes(1, 4, 8, 4)
+        score(8, 0)
+        score(9, 0)
+        in_turn(sim_steps((6, 7)), on_scalar, on_vector)
+        in_turn(y_steps((4, 6), 0), on_scalar, on_scalar)
+        planes_later(0, 4, 8)
+        score(10, 0)
+        score(11, 0)
+
+        for bt in range(0, 4):
+            score(bt, 1)
+        in_turn(y_steps((8, 10), 0), on_scalar, on_scalar)
+        planes_later(0, 8, 12)
+        later(PLANES_LAG, ("scales", 0), lambda: store_scales(0, 0, USER_TILES, [nc.sync]))
+        for bt in range(4, 8):
+            score(bt, 1)
+        in_turn(y_steps((0, 2), 1), on_scalar, on_scalar)
+        planes_later(1, 0, 4)
+        for bt in range(8, 11):
+            score(bt, 1)
+        last_score(11, 1)
+        in_turn(y_steps((4, 6), 1), on_scalar, on_scalar)
+        planes_later(1, 4, 8)
         turn_y(8, 2, 1, on_scalar)
-        planes(1, 8, 10, 8)
-        turn_y(10, 1, 1, on_scalar)
-        planes(1, 10, 11, None)
-        turn_y(11, 1, 1, on_scalar)
-        planes(1, 11, 12, 10)
         release(everything=True)
-        store_scales()
+        turn_y(10, 1, 1, on_vector)
+        planes(1, 8, 10)
+        turn_y(11, 1, 1, on_scalar)
+        quantize_y(1, 10, 11)
+        quantize_y(1, 11, 12)
+        store_codes(1, 10, 12)
+        store_scales(1, 0, USER_TILES, [nc.scalar, nc.sync])

@@ -25,8 +25,7 @@ I_PASSES = I // 512
 ITEM_TILES = I // P
 USER_TILES = B // P
 BANKS = 8
-WARM_N = 256
-WARM_PASSES = 7
+WARM_PASSES = 5
 
 ROUND_LAG = 3
 PREFS_LAG = 3
@@ -77,9 +76,6 @@ def tile_rp3beta_item_scores_k5_kernel(
         y_codes = [kept("y_codes%d" % h, [P, B], U32) for h in range(2)]
         y_scales = kept("y_scales", [P, 2, B], U8)
         gain_rows = kept("gain_rows", [P, P], BF16)
-        warm_bf = kept("warm_bf", [P, 4 * WARM_N], BF16)
-        warm_codes = kept("warm_codes", [P, WARM_N], U32)
-        warm_scales = kept("warm_scales", [P, WARM_N], U8)
         gain_rows_f32 = kept("gain_rows_f32", [P, P], F32)
         gain_cols = kept("gain_cols", [P, 16], F32)
         pop_rows = kept("pop_rows", [P, QUAD], BF16)
@@ -120,14 +116,12 @@ def tile_rp3beta_item_scores_k5_kernel(
 
         ctx.enter_context(tc.manual_schedule())
 
-        nc.gpsimd.memset(warm_bf[:].bitcast(I32), 0)
+        nc.gpsimd.memset(r_scales[1][:].rearrange("p g n -> p (g n)").bitcast(I32), 0)
         clear(l_scales[0][:].rearrange("p g n -> p (g n)"))
         clear(r_scales[0][:].rearrange("p g n -> p (g n)"))
-        nc.vector.quantize_mx(out=warm_codes[:].bitcast(FP8X4), scales=warm_scales[:], in_=warm_bf[:])
         clear(l_scales[1][:].rearrange("p g n -> p (g n)"))
         clear(identity[:])
         make_identity(nc, identity[:], nomemset=True)
-        clear(r_scales[1][:].rearrange("p g n -> p (g n)"))
         clear(gain_rows[:])
         nc.vector.memset(exponent[:], 1.0)
         nc.gpsimd.tensor_scalar(
@@ -135,6 +129,15 @@ def tile_rp3beta_item_scores_k5_kernel(
         )
         load_words(nc.scalar, l_words, item_user_words, 0, 0, 1)
         load_words(nc.scalar, r_words, user_item_words, 0, 0, 1)
+        blank = r_scales[1][:].rearrange("p g n -> p (g n)")
+        warm_bank = next_bank()
+        for w in range(WARM_PASSES):
+            nc.tensor.matmul_mx(
+                out=warm_bank[:],
+                lhsT=blank[:, 0 : 2 * P].bitcast(FP4X4), lhsT_scale=blank[:, 2 * HALF : 2 * HALF + P],
+                rhs=blank[:, 0 : 2 * HALF].bitcast(FP4X4), rhs_scale=blank[:, 2 * HALF : 3 * HALF],
+                start=True, stop=True,
+            )
         load_scales(l_scales, item_user_scales, 0)
         load_scales(r_scales, user_item_scales, 0)
         nc.sync.dma_start(out=pop_rows[:], in_=rows_in_every_quadrant(popularity))
@@ -357,11 +360,12 @@ def tile_rp3beta_item_scores_k5_kernel(
                 in_=y_codes[jh][:, users].bitcast(I32),
             )
 
-        def store_scales(jh, bt0, bt1, queues):
-            users = slice(P * bt0, P * bt1)
+        def store_scales():
             for r in range(4):
-                queues[r % len(queues)].dma_start(
-                    out=out_2[jh, r:16:4, users].bitcast(I32), in_=y_scales[r:P:QUAD, jh, users].bitcast(I32)
+                queue = nc.scalar if r % 2 == 0 else nc.sync
+                queue.dma_start(
+                    out=out_2[:, r:16:4, :].rearrange("g q m -> q g m").bitcast(I32),
+                    in_=y_scales[r:P:QUAD, :, :].bitcast(I32),
                 )
 
         def planes(jh, bt0, bt1):
@@ -384,13 +388,6 @@ def tile_rp3beta_item_scores_k5_kernel(
         def y_steps(tiles, jh):
             return [lambda copy, bt=bt: turn_y(bt, 2, jh, copy) for bt in tiles]
 
-
-        warm_bank = next_bank()
-        for w in range(WARM_PASSES):
-            nc.tensor.matmul_mx(
-                out=warm_bank[:, 0:WARM_N], lhsT=warm_codes[:, 0:P].bitcast(FP8X4), lhsT_scale=warm_scales[:, 0:P],
-                rhs=warm_codes[:].bitcast(FP8X4), rhs_scale=warm_scales[:], start=True, stop=True,
-            )
 
         first_banks = [next_bank() for jt in range(4)]
         for g in range(U_PASSES):
@@ -451,7 +448,6 @@ def tile_rp3beta_item_scores_k5_kernel(
             score(bt, 1)
         in_turn(y_steps((8, 10), 0), on_scalar, on_scalar)
         planes_later(0, 8, 12)
-        later(PLANES_LAG, ("scales", 0), lambda: store_scales(0, 0, USER_TILES, [nc.sync]))
         for bt in range(4, 8):
             score(bt, 1)
         in_turn(y_steps((0, 2), 1), on_scalar, on_scalar)
@@ -469,4 +465,4 @@ def tile_rp3beta_item_scores_k5_kernel(
         quantize_y(1, 10, 11)
         quantize_y(1, 11, 12)
         store_codes(1, 10, 12)
-        store_scales(1, 0, USER_TILES, [nc.scalar, nc.sync])
+        store_scales()

@@ -25,9 +25,9 @@ I_PASSES = I // 512
 ITEM_TILES = I // P
 USER_TILES = B // P
 BANKS = 8
-WARM_PASSES = 5
+WARM_PASSES = 6
 
-ROUND_LAG = 3
+ROUND_LAG = 2
 PREFS_LAG = 3
 SIM_LAG = 3
 PLANES_LAG = 4
@@ -422,23 +422,22 @@ def tile_rp3beta_item_scores_k5_kernel(
         walk(5, 0)
         score(2, 0)
         score(3, 0)
-        in_turn(prefs_steps(range(6, USER_TILES)), on_scalar, on_vector)
         walk(5, 1)
         score(4, 0)
         score(5, 0)
+        in_turn(prefs_steps(range(6, USER_TILES)) + sim_steps((4, 5)), on_scalar, on_vector)
         walk(6, 0)
+        walk(6, 1)
         score(6, 0)
         score(7, 0)
-        in_turn(y_steps((0, 2), 0), on_scalar, on_vector)
-        planes_later(0, 0, 4)
-        in_turn(sim_steps((4, 5)), on_scalar, on_vector)
 
-        walk(6, 1)
         walk(7, 0)
         walk(7, 1)
         score(8, 0)
         score(9, 0)
         in_turn(sim_steps((6, 7)), on_scalar, on_vector)
+        in_turn(y_steps((0, 2), 0), on_scalar, on_scalar)
+        planes_later(0, 0, 4)
         in_turn(y_steps((4, 6), 0), on_scalar, on_scalar)
         planes_later(0, 4, 8)
         score(10, 0)

@@ -68,8 +68,7 @@ def tile_rp3beta_item_scores_k5_kernel(
         prefs_grouped = {}
         prefs_codes = [kept("prefs_codes%d" % k, [P, 2, I_PASSES, P], U32) for k in range(USER_TILES // 2)]
         prefs_scales = [kept("prefs_scales%d" % k, [P, 2, I_PASSES, P], U8) for k in range(USER_TILES // 2)]
-        sim_t = [kept("sim_t%d" % jt, [P, I], BF16) for jt in range(ITEM_TILES)]
-        sim_grouped = [kept("sim_grouped%d" % jt, [P, I_PASSES, P, 4], BF16) for jt in range(ITEM_TILES)]
+        sim_t = {}
         sim_codes = [kept("sim_codes%d" % h, [P, I_PASSES, HALF], U32) for h in range(2)]
         sim_scales = [kept("sim_scales%d" % h, [P, I_PASSES, HALF], U8) for h in range(2)]
         y_grouped = [kept("y_grouped%d" % h, [P, B, 4], BF16) for h in range(2)]
@@ -96,8 +95,8 @@ def tile_rp3beta_item_scores_k5_kernel(
                 in_=src[g0:g1, :, 2 * HALF * h : 2 * HALF * (h + 1)].rearrange("g p n -> p g n").bitcast(I32),
             )
 
-        def load_scales(dst, src, h):
-            for r in range(4):
+        def load_scales(dst, src, h, rows=range(4)):
+            for r in rows:
                 nc.sync.dma_start(
                     out=dst[h][r:P:QUAD, :, :].bitcast(I32),
                     in_=src[:, r:16:4, HALF * h : HALF * (h + 1)].rearrange("g q n -> q g n").bitcast(I32),
@@ -205,8 +204,9 @@ def tile_rp3beta_item_scores_k5_kernel(
             )
 
         def walk_out(bank, jt, ih):
-            target = sim_t[jt][:].rearrange("q (s n z) -> q s n z", s=4, z=16)[:, :, 8 * ih : 8 * (ih + 1), :]
-            source = bank[:].rearrange("q (n s z) -> q s n z", s=4, z=16)
+            sim_t[(jt, ih)] = work.tile([P, HALF], BF16, name="sim_t", tag="sim_t", bufs=8, align_bytes=64)
+            target = sim_t[(jt, ih)][:].rearrange("q (u n z) -> q u n z", u=2, z=16)
+            source = bank[:].rearrange("q (n u z) -> q u n z", u=2, z=16)
             nc.scalar.activation(out=target, in_=source, func=ACT.Copy, scale=damping[:, jt : jt + 1])
 
         def walk(jt, ih):
@@ -216,37 +216,37 @@ def tile_rp3beta_item_scores_k5_kernel(
 
             tensor_step((), passes, lambda bank: walk_out(bank, jt, ih))
 
-        def turn_sim(jt, copy):
-            pairs = sim_t[jt][:].bitcast(F32)
+        def turn_sim(jt, count, g, copy, lag):
+            pairs = [sim_t[(jt + c, g)][:].bitcast(F32) for c in range(count)]
+            grouped = work.tile([P, count * P * 4], BF16, name="sim_grouped", tag="sim_grouped", bufs=4, align_bytes=64)
 
             def group(bank):
-                target = sim_grouped[jt][:].rearrange("q g j t -> q (g j t)").bitcast(F32)
                 copy(
-                    out=target.rearrange("q (g j u) -> q g j u", g=I_PASSES, u=2),
-                    in_=bank[:].rearrange("q (g u j) -> q g j u", g=I_PASSES, u=2),
+                    out=grouped[:].bitcast(F32).rearrange("q (c j u) -> q c j u", c=count, u=2),
+                    in_=bank[:, 0 : 2 * P * count].rearrange("q (c u j) -> q c j u", c=count, u=2),
                 )
 
-            tensor_step((), lambda bank: transposes(bank, [pairs[:, P * s : P * (s + 1)] for s in range(4)]), group)
-            later(SIM_LAG, ("sim", jt // 4), lambda: quantize_sim(jt))
+            sources = [tile_pairs[:, P * u : P * (u + 1)] for tile_pairs in pairs for u in range(2)]
+            tensor_step((), lambda bank: transposes(bank, sources), group)
+            later(lag, ("sim", jt // 2, g), lambda: quantize_sim(jt, count, g, grouped))
 
-        def quantize_sim(jt):
+        def quantize_sim(jt, count, g, grouped):
             jh, c = divmod(jt, 4)
-            columns = slice(P * c, P * (c + 1))
-            for g in range(I_PASSES):
-                nc.vector.quantize_mx(
-                    out=sim_codes[jh][:, g, columns].bitcast(FP8X4),
-                    scales=sim_scales[jh][:, g, columns],
-                    in_=sim_grouped[jt][:, g, :, :].rearrange("q j t -> q (j t)"),
-                )
+            columns = slice(P * c, P * (c + count))
+            nc.vector.quantize_mx(
+                out=sim_codes[jh][:, g, columns].bitcast(FP8X4),
+                scales=sim_scales[jh][:, g, columns],
+                in_=grouped[:],
+            )
 
 
         def split_prefs(k):
-            prefs_split[k] = work.tile([P, 2, I], BF16, name="prefs_split", tag="prefs_split", bufs=6, align_bytes=64)
+            prefs_split[k] = work.tile([P, 2, I], BF16, name="prefs_split", tag="prefs_split", bufs=4, align_bytes=64)
             target = prefs_split[k][:].rearrange("q c i -> q (c i)").bitcast(F32)
             source = prefs_raw[k][:].rearrange("q c i -> q (c i)").bitcast(F32)
             nc.vector.tensor_copy(
-                out=target.rearrange("q (s n r) -> q s n r", s=4, r=8),
-                in_=source.rearrange("q (n s r) -> q s n r", s=4, r=8),
+                out=target.rearrange("q (s u n r) -> q s u n r", s=4, u=2, r=8),
+                in_=source.rearrange("q (s n u r) -> q s u n r", s=4, u=2, r=8),
             )
 
         def group_prefs(bt, copy, source):
@@ -270,25 +270,28 @@ def tile_rp3beta_item_scores_k5_kernel(
             pairs = prefs_split[k][:].rearrange("q c i -> q (c i)").bitcast(F32)
             tensor_step(
                 (),
-                lambda bank: transposes(bank, [pairs[:, P * (2 * s + c) : P * (2 * s + c + 1)] for s in range(4)]),
+                lambda bank: transposes(bank, [pairs[:, P * (4 * c + s) : P * (4 * c + s + 1)] for s in range(4)]),
                 lambda bank: group_prefs(bt, copy, bank[:].rearrange("q (g u b) -> q g b u", g=I_PASSES, u=2)),
             )
             if c == 1:
                 later(PREFS_LAG, ("prefs", k), lambda: quantize_prefs(k))
 
 
-        y_f32 = {}
-        y_split = {}
+        y_pairs = [kept("y%d" % k, [P, 2, I], F32) for k in range(USER_TILES // 2)]
+        y_f32 = [y_pairs[bt // 2][:, bt % 2, :] for bt in range(USER_TILES)]
+        y_split = {(bt, jh): kept("y_bf%d_%d" % (bt, jh), [P, HALF], BF16) for bt in range(USER_TILES) for jh in range(2)}
 
-        def score_passes(bank, bt, jh):
+        def score_passes(out, bt, j0, j1, passes=range(I_PASSES)):
             k, c = divmod(bt, 2)
-            for g in range(I_PASSES):
+            jh, lo = divmod(j0, HALF)
+            columns = slice(lo, lo + j1 - j0)
+            for g in passes:
                 nc.tensor.matmul_mx(
-                    out=bank[:],
+                    out=out,
                     lhsT=prefs_codes[k][:, c, g, :].bitcast(FP8X4),
                     lhsT_scale=prefs_scales[k][:, c, g, :],
-                    rhs=sim_codes[jh][:, g, :].bitcast(FP8X4),
-                    rhs_scale=sim_scales[jh][:, g, :],
+                    rhs=sim_codes[jh][:, g, columns].bitcast(FP8X4),
+                    rhs_scale=sim_scales[jh][:, g, columns],
                     start=(g == 0),
                     stop=(g == I_PASSES - 1),
                 )
@@ -298,37 +301,59 @@ def tile_rp3beta_item_scores_k5_kernel(
                 out=out, in0=scores, scalar=gain_cols[:, bt : bt + 1], in1=bias, op0=ALU.mult, op1=ALU.add
             )
 
-        def finish_y(bank, bt, jh):
-            columns = slice(HALF * jh, HALF * (jh + 1))
-            y_f32[(bt, jh)] = work.tile([P, HALF], F32, name="y", tag="y", bufs=12)
-            gain_and_bias(y_f32[(bt, jh)][:], bank[:], bias_all[:, columns], bt)
-            nc.sync.dma_start(out=out_0[P * bt : P * (bt + 1), columns], in_=y_f32[(bt, jh)][:])
+        def store_y(bt, j0, j1):
+            nc.sync.dma_start(out=out_0[P * bt : P * (bt + 1), j0:j1], in_=y_f32[bt][:, j0:j1])
+
+        def store_y_pair(k, j0, j1):
+            rows = out_0[2 * P * k : 2 * P * (k + 1), j0:j1].rearrange("(c p) j -> p c j", p=P)
+            nc.sync.dma_start(out=rows, in_=y_pairs[k][:, :, j0:j1])
 
         def by_pairs(columns):
             return columns.rearrange("q (m u e) -> q u m e", u=2, e=2)
 
-        def new_y_split(bt, jh):
-            y_split[(bt, jh)] = work.tile([P, HALF], BF16, name="y_bf", tag="y_bf", bufs=16)
-            return y_split[(bt, jh)][:].rearrange("q (u m e) -> q u m e", u=2, e=2)
+        def split_view(bt, j0, j1):
+            jh, lo = divmod(j0, HALF)
+            whole = y_split[(bt, jh)][:].rearrange("q (u m e) -> q u m e", u=2, e=2)
+            return whole[:, :, lo // 4 : (lo + j1 - j0) // 4, :]
 
-        def score(bt, jh):
-            copy = on_scalar if bt % 2 else on_gpsimd
-            tensor_step(
-                (("prefs", bt // 2), ("sim", jh)),
-                lambda bank: score_passes(bank, bt, jh),
-                lambda bank: finish_y(bank, bt, jh),
-            )
-            later(ROUND_LAG, ("y", bt, jh), lambda: copy(out=new_y_split(bt, jh), in_=by_pairs(y_f32[(bt, jh)][:])))
+        def round_y(bt, j0, j1, copy):
+            copy(out=split_view(bt, j0, j1), in_=by_pairs(y_f32[bt][:, j0:j1]))
 
-        def last_score(bt, jh):
+        def score(tiles, j0, j1, stored_from, copies, lag=ROUND_LAG):
+            width = j1 - j0
+
+            def passes(bank):
+                for n, bt in enumerate(tiles):
+                    score_passes(bank[:, width * n : width * (n + 1)], bt, j0, j1)
+
+            def finish(bank):
+                for n, bt in enumerate(tiles):
+                    gain_and_bias(y_f32[bt][:, j0:j1], bank[:, width * n : width * (n + 1)], bias_all[:, j0:j1], bt)
+                if len(tiles) == 2:
+                    store_y_pair(tiles[0] // 2, stored_from, j1)
+                elif stored_from is not None:
+                    store_y(tiles[0], stored_from, j1)
+
+            needed = [("prefs", bt // 2) for bt in tiles]
+            needed.extend(("sim", n, g) for n in range(j0 // (2 * P), j1 // (2 * P)) for g in range(I_PASSES))
+            tensor_step(needed, passes, finish)
+            for bt, copy in zip(tiles, copies):
+                later(lag, ("y", bt, j0 // HALF), lambda bt=bt, copy=copy: round_y(bt, j0, j1, copy))
+
+        def last_score(bt, j0, j1):
+            width = j1 - j0
+
+            def finish(bank):
+                gain_and_bias(y_f32[bt][:, j0:j1], bank[:, 0:width], bias_all[:, j0:j1], bt)
+                store_y(bt, j0, j1)
+
             def rounded(bank):
-                target = new_y_split(bt, jh)
+                target = split_view(bt, j0, j1)
                 for u in range(2):
-                    bias = by_pairs(bias_all[:, HALF * jh : HALF * (jh + 1)])
-                    gain_and_bias(target[:, u], by_pairs(bank[:])[:, u], bias[:, u], bt)
-                later(LAST_LAG, ("y32", bt, jh), lambda: finish_y(bank, bt, jh))
+                    gain_and_bias(target[:, u], by_pairs(bank[:, 0:width])[:, u], by_pairs(bias_all[:, j0:j1])[:, u], bt)
+                later(LAST_LAG, ("y32", bt), lambda: finish(bank))
 
-            tensor_step((), lambda bank: score_passes(bank, bt, jh), rounded)
+            tensor_step((), lambda bank: score_passes(bank[:, 0:width], bt, j0, j1), rounded)
 
 
         def turn_y(bt, count, jh, copy):
@@ -360,33 +385,20 @@ def tile_rp3beta_item_scores_k5_kernel(
                 in_=y_codes[jh][:, users].bitcast(I32),
             )
 
-        def store_scales():
+        def store_scales(halves, bt0, bt1, queues):
+            users = slice(P * bt0, P * bt1)
             for r in range(4):
-                queue = nc.scalar if r % 2 == 0 else nc.sync
-                queue.dma_start(
-                    out=out_2[:, r:16:4, :].rearrange("g q m -> q g m").bitcast(I32),
-                    in_=y_scales[r:P:QUAD, :, :].bitcast(I32),
+                queues[r % len(queues)].dma_start(
+                    out=out_2[halves, r:16:4, users].rearrange("g q m -> q g m").bitcast(I32),
+                    in_=y_scales[r:P:QUAD, halves, users].bitcast(I32),
                 )
 
         def planes(jh, bt0, bt1):
             quantize_y(jh, bt0, bt1)
             store_codes(jh, bt0, bt1)
 
-        def planes_later(jh, bt0, bt1):
-            later(PLANES_LAG, ("planes", jh, bt0), lambda: planes(jh, bt0, bt1))
-
-        def in_turn(steps, first, second):
-            for n, step in enumerate(steps):
-                step(second if n % 2 else first)
-
-        def prefs_steps(tiles):
-            return [lambda copy, bt=bt: turn_prefs(bt, copy) for bt in tiles]
-
-        def sim_steps(tiles):
-            return [lambda copy, jt=jt: turn_sim(jt, copy) for jt in tiles]
-
-        def y_steps(tiles, jh):
-            return [lambda copy, bt=bt: turn_y(bt, 2, jh, copy) for bt in tiles]
+        def planes_later(jh, bt0, bt1, lag=PLANES_LAG):
+            later(lag, ("planes", jh, bt0), lambda: planes(jh, bt0, bt1))
 
 
         first_banks = [next_bank() for jt in range(4)]
@@ -396,72 +408,99 @@ def tile_rp3beta_item_scores_k5_kernel(
         for jt in range(4):
             walk_out(first_banks[jt], jt, 0)
 
+        def first_half(bt, stored):
+            score((bt,), 0, HALF, 0 if stored else None, (on_scalar if bt % 2 else on_gpsimd,))
+
         split_prefs(0)
         walk(0, 1)
-        split_prefs(1)
         walk(1, 1)
+        split_prefs(1)
         walk(2, 1)
+        walk(3, 1)
         nc.vector.tensor_copy(out=gain_rows_f32[:], in_=gain_rows[:])
         tensor_step(
             (),
             lambda bank: transposes(bank, [gain_rows_f32[:]]),
             lambda bank: nc.vector.tensor_copy(out=gain_cols[:], in_=bank[:, 0:16]),
         )
-        in_turn(prefs_steps((0, 1)) + sim_steps((0, 1)), on_vector, on_scalar)
-        split_prefs(2)
-        walk(3, 1)
+        turn_sim(0, 2, 0, on_vector, SIM_LAG)
+        turn_sim(2, 2, 0, on_scalar, SIM_LAG)
+        turn_prefs(0, on_vector)
+        turn_prefs(1, on_scalar)
+        turn_sim(0, 2, 1, on_scalar, SIM_LAG)
+        turn_sim(2, 2, 1, on_scalar, SIM_LAG)
+        turn_prefs(2, on_scalar)
+        turn_prefs(3, on_scalar)
         walk(4, 0)
-        in_turn(sim_steps((2, 3)) + prefs_steps(range(2, 6)), on_vector, on_scalar)
-
+        split_prefs(2)
+        walk(5, 0)
         split_prefs(3)
+        first_half(0, True)
+        first_half(1, True)
         walk(4, 1)
         split_prefs(4)
-        score(0, 0)
-        score(1, 0)
-        split_prefs(5)
-        walk(5, 0)
-        score(2, 0)
-        score(3, 0)
+        first_half(2, True)
+        first_half(3, True)
         walk(5, 1)
-        score(4, 0)
-        score(5, 0)
-        in_turn(prefs_steps(range(6, USER_TILES)) + sim_steps((4, 5)), on_scalar, on_vector)
+        split_prefs(5)
+        turn_prefs(4, on_scalar)
+        turn_prefs(5, on_vector)
+        turn_prefs(6, on_scalar)
+        turn_prefs(7, on_scalar)
+        turn_sim(4, 2, 0, on_vector, SIM_LAG)
+        turn_sim(4, 2, 1, on_scalar, SIM_LAG)
+        turn_prefs(8, on_scalar)
+        turn_prefs(9, on_vector)
+        turn_prefs(10, on_scalar)
+        turn_prefs(11, on_scalar)
+        turn_y(0, 2, 0, on_scalar)
         walk(6, 0)
-        walk(6, 1)
-        score(6, 0)
-        score(7, 0)
-
+        first_half(4, True)
+        first_half(5, True)
+        first_half(6, True)
+        first_half(7, True)
         walk(7, 0)
+        score((8,), 0, HALF, None, (on_gpsimd,))
+        score((9,), 0, HALF, None, (on_scalar,))
+        score((8, 9), HALF, 768, 0, (on_gpsimd, on_scalar))
+        score((10,), 0, HALF, None, (on_gpsimd,))
+        score((11,), 0, HALF, None, (on_scalar,))
+        score((10, 11), HALF, 768, 0, (on_scalar, on_scalar))
+        turn_y(2, 2, 0, on_scalar)
+        turn_y(4, 2, 0, on_vector)
+        planes_later(0, 0, 4, 1)
+        turn_y(6, 2, 0, on_scalar)
+        turn_sim(6, 2, 0, on_vector, 3)
+        planes_later(0, 4, 8, 1)
+        turn_y(8, 2, 0, on_scalar)
+        turn_y(10, 2, 0, on_scalar)
+        planes_later(0, 8, 12, 2)
+        walk(6, 1)
         walk(7, 1)
-        score(8, 0)
-        score(9, 0)
-        in_turn(sim_steps((6, 7)), on_scalar, on_vector)
-        in_turn(y_steps((0, 2), 0), on_scalar, on_scalar)
-        planes_later(0, 0, 4)
-        in_turn(y_steps((4, 6), 0), on_scalar, on_scalar)
-        planes_later(0, 4, 8)
-        score(10, 0)
-        score(11, 0)
-
-        for bt in range(0, 4):
-            score(bt, 1)
-        in_turn(y_steps((8, 10), 0), on_scalar, on_scalar)
-        planes_later(0, 8, 12)
-        for bt in range(4, 8):
-            score(bt, 1)
-        in_turn(y_steps((0, 2), 1), on_scalar, on_scalar)
-        planes_later(1, 0, 4)
-        for bt in range(8, 11):
-            score(bt, 1)
-        last_score(11, 1)
-        in_turn(y_steps((4, 6), 1), on_scalar, on_scalar)
-        planes_later(1, 4, 8)
+        score((0, 1), HALF, 768, HALF, (on_scalar, on_scalar), 4)
+        score((2, 3), HALF, 768, HALF, (on_scalar, on_scalar), 4)
+        store_scales(slice(0, 1), 0, 12, (nc.sync,))
+        turn_sim(6, 1, 1, on_scalar, 2)
+        turn_sim(7, 1, 1, on_scalar, 1)
+        score((4, 5), HALF, 768, HALF, (on_gpsimd, on_scalar))
+        score((6, 7), HALF, 768, HALF, (on_gpsimd, on_scalar))
+        score((0, 1), 768, I, 768, (on_gpsimd, on_scalar))
+        score((2, 3), 768, I, 768, (on_gpsimd, on_scalar))
+        score((4, 5), 768, I, 768, (on_gpsimd, on_scalar))
+        score((6, 7), 768, I, 768, (on_gpsimd, on_scalar))
+        score((8, 9), 768, I, 768, (on_gpsimd, on_scalar))
+        turn_y(0, 2, 1, on_scalar)
+        turn_y(2, 2, 1, on_vector)
+        turn_y(4, 2, 1, on_scalar)
+        last_score(10, 768, I)
+        last_score(11, 768, I)
+        turn_y(6, 2, 1, on_scalar)
+        planes(1, 0, 4)
         turn_y(8, 2, 1, on_scalar)
         release(everything=True)
-        turn_y(10, 1, 1, on_vector)
-        planes(1, 8, 10)
-        turn_y(11, 1, 1, on_scalar)
-        quantize_y(1, 10, 11)
-        quantize_y(1, 11, 12)
-        store_codes(1, 10, 12)
-        store_scales()
+        turn_y(10, 2, 1, on_scalar)
+        planes(1, 4, 8)
+        quantize_y(1, 8, 10)
+        quantize_y(1, 10, 12)
+        store_codes(1, 8, 12)
+        store_scales(slice(1, 2), 0, 12, (nc.scalar, nc.sync))

@@ -71,12 +71,10 @@ def tile_rp3beta_item_scores_k5_kernel(
         sim_t = {}
         sim_codes = [kept("sim_codes%d" % h, [P, I_PASSES, HALF], U32) for h in range(2)]
         sim_scales = [kept("sim_scales%d" % h, [P, I_PASSES, HALF], U8) for h in range(2)]
-        y_grouped = [kept("y_grouped%d" % h, [P, B, 4], BF16) for h in range(2)]
+        y_grouped = {}
         y_codes = [kept("y_codes%d" % h, [P, B], U32) for h in range(2)]
         y_scales = kept("y_scales", [P, 2, B], U8)
-        gain_rows = kept("gain_rows", [P, P], BF16)
-        gain_rows_f32 = kept("gain_rows_f32", [P, P], F32)
-        gain_cols = kept("gain_cols", [P, 16], F32)
+        gain_cols = kept("gain_cols", [P, USER_TILES], BF16)
         pop_rows = kept("pop_rows", [P, QUAD], BF16)
         pop_cols = kept("pop_cols", [P, QUAD], BF16)
         pop_own = kept("pop_own", [P, ITEM_TILES], F32)
@@ -102,10 +100,12 @@ def tile_rp3beta_item_scores_k5_kernel(
                     in_=src[:, r:16:4, HALF * h : HALF * (h + 1)].rearrange("g q n -> q g n").bitcast(I32),
                 )
 
+        def by_tiles(rows):
+            return rows.rearrange("(n p c) x -> n p c x", p=P, c=4)
+
         def load_prefs(k):
-            nc.sync.dma_start(
-                out=prefs_raw[k][:], in_=prefs[2 * P * k : 2 * P * (k + 1), :].rearrange("(c p) i -> p c i", p=P)
-            )
+            n, c = divmod(2 * k, 4)
+            nc.sync.dma_start(out=prefs_raw[k][:], in_=by_tiles(prefs)[n][:, c : c + 2, :])
 
         def clear(tile_ap):
             nc.vector.memset(tile_ap.bitcast(I32), 0)
@@ -121,7 +121,6 @@ def tile_rp3beta_item_scores_k5_kernel(
         clear(l_scales[1][:].rearrange("p g n -> p (g n)"))
         clear(identity[:])
         make_identity(nc, identity[:], nomemset=True)
-        clear(gain_rows[:])
         nc.vector.memset(exponent[:], 1.0)
         nc.gpsimd.tensor_scalar(
             out=exponent[:], in0=exponent[:], scalar1=-BETA, scalar2=0.0, op0=ALU.mult, op1=ALU.add
@@ -147,7 +146,9 @@ def tile_rp3beta_item_scores_k5_kernel(
         load_scales(l_scales, item_user_scales, 1)
         load_words(nc.sync, l_words, item_user_words, 1, 0, U_PASSES)
         load_prefs(0)
-        nc.sync.dma_start(out=gain_rows[0:USER_TILES, :], in_=user_gain.rearrange("(c n) -> c n", n=P))
+        nc.sync.dma_start(
+            out=gain_cols[:].rearrange("p (n c) -> p n c", c=4), in_=user_gain.rearrange("(n p c) -> p n c", p=P, c=4)
+        )
         load_prefs(1)
         load_scales(r_scales, user_item_scales, 1)
         load_words(nc.sync, r_words, user_item_words, 1, 0, U_PASSES)
@@ -216,8 +217,9 @@ def tile_rp3beta_item_scores_k5_kernel(
 
             tensor_step((), passes, lambda bank: walk_out(bank, jt, ih))
 
-        def turn_sim(jt, count, g, copy, lag):
-            pairs = [sim_t[(jt + c, g)][:].bitcast(F32) for c in range(count)]
+        def turn_sim(units, copy, lag):
+            count = len(units)
+            pairs = [sim_t[unit][:].bitcast(F32) for unit in units]
             grouped = work.tile([P, count * P * 4], BF16, name="sim_grouped", tag="sim_grouped", bufs=4, align_bytes=64)
 
             def group(bank):
@@ -228,15 +230,19 @@ def tile_rp3beta_item_scores_k5_kernel(
 
             sources = [tile_pairs[:, P * u : P * (u + 1)] for tile_pairs in pairs for u in range(2)]
             tensor_step((), lambda bank: transposes(bank, sources), group)
-            later(lag, ("sim", jt // 2, g), lambda: quantize_sim(jt, count, g, grouped))
+            if units[0][1] == units[-1][1]:
+                later(lag, ("sim",) + units[0], lambda: quantize_sim(units[0], count, grouped[:]))
+            else:
+                for n, unit in enumerate(units):
+                    part = grouped[:, 4 * P * n : 4 * P * (n + 1)]
+                    later(lag, ("sim",) + unit, lambda unit=unit, part=part: quantize_sim(unit, 1, part))
 
-        def quantize_sim(jt, count, g, grouped):
+        def quantize_sim(unit, count, values):
+            jt, g = unit
             jh, c = divmod(jt, 4)
             columns = slice(P * c, P * (c + count))
             nc.vector.quantize_mx(
-                out=sim_codes[jh][:, g, columns].bitcast(FP8X4),
-                scales=sim_scales[jh][:, g, columns],
-                in_=grouped[:],
+                out=sim_codes[jh][:, g, columns].bitcast(FP8X4), scales=sim_scales[jh][:, g, columns], in_=values
             )
 
 
@@ -277,9 +283,14 @@ def tile_rp3beta_item_scores_k5_kernel(
                 later(PREFS_LAG, ("prefs", k), lambda: quantize_prefs(k))
 
 
-        y_pairs = [kept("y%d" % k, [P, 2, I], F32) for k in range(USER_TILES // 2)]
-        y_f32 = [y_pairs[bt // 2][:, bt % 2, :] for bt in range(USER_TILES)]
-        y_split = {(bt, jh): kept("y_bf%d_%d" % (bt, jh), [P, HALF], BF16) for bt in range(USER_TILES) for jh in range(2)}
+        y_quads = [kept("y%d" % n, [P, 4, I], F32) for n in range(USER_TILES // 4)]
+        y_f32 = [y_quads[bt // 4][:, bt % 4, :] for bt in range(USER_TILES)]
+        first_split = [kept("first_split%d" % h, [P, 2 * HALF], BF16) for h in range(2)]
+        y_split = {(bt, 0): first_split[bt // 2][:, HALF * (bt % 2) : HALF * (bt % 2 + 1)] for bt in range(4)}
+        for bt in range(USER_TILES):
+            for jh in range(2):
+                if (bt, jh) not in y_split:
+                    y_split[(bt, jh)] = kept("y_bf%d_%d" % (bt, jh), [P, HALF], BF16)
 
         def score_passes(out, bt, j0, j1, passes=range(I_PASSES)):
             k, c = divmod(bt, 2)
@@ -301,12 +312,10 @@ def tile_rp3beta_item_scores_k5_kernel(
                 out=out, in0=scores, scalar=gain_cols[:, bt : bt + 1], in1=bias, op0=ALU.mult, op1=ALU.add
             )
 
-        def store_y(bt, j0, j1):
-            nc.sync.dma_start(out=out_0[P * bt : P * (bt + 1), j0:j1], in_=y_f32[bt][:, j0:j1])
-
-        def store_y_pair(k, j0, j1):
-            rows = out_0[2 * P * k : 2 * P * (k + 1), j0:j1].rearrange("(c p) j -> p c j", p=P)
-            nc.sync.dma_start(out=rows, in_=y_pairs[k][:, :, j0:j1])
+        def store_y(bt, count, j0, j1):
+            n, c = divmod(bt, 4)
+            rows = by_tiles(out_0)[n][:, c : c + count, j0:j1]
+            nc.sync.dma_start(out=rows, in_=y_quads[n][:, c : c + count, j0:j1])
 
         def by_pairs(columns):
             return columns.rearrange("q (m u e) -> q u m e", u=2, e=2)
@@ -319,7 +328,7 @@ def tile_rp3beta_item_scores_k5_kernel(
         def round_y(bt, j0, j1, copy):
             copy(out=split_view(bt, j0, j1), in_=by_pairs(y_f32[bt][:, j0:j1]))
 
-        def score(tiles, j0, j1, stored_from, copies, lag=ROUND_LAG):
+        def score(tiles, j0, j1, stored_from, copies, lag=ROUND_LAG, rounded_from=None):
             width = j1 - j0
 
             def passes(bank):
@@ -329,23 +338,22 @@ def tile_rp3beta_item_scores_k5_kernel(
             def finish(bank):
                 for n, bt in enumerate(tiles):
                     gain_and_bias(y_f32[bt][:, j0:j1], bank[:, width * n : width * (n + 1)], bias_all[:, j0:j1], bt)
-                if len(tiles) == 2:
-                    store_y_pair(tiles[0] // 2, stored_from, j1)
-                elif stored_from is not None:
-                    store_y(tiles[0], stored_from, j1)
+                if stored_from is not None:
+                    store_y(tiles[0], len(tiles), stored_from, j1)
 
             needed = [("prefs", bt // 2) for bt in tiles]
-            needed.extend(("sim", n, g) for n in range(j0 // (2 * P), j1 // (2 * P)) for g in range(I_PASSES))
+            needed.extend(("sim", jt, g) for jt in range(j0 // P, j1 // P) for g in range(I_PASSES))
             tensor_step(needed, passes, finish)
+            start = j0 if rounded_from is None else rounded_from
             for bt, copy in zip(tiles, copies):
-                later(lag, ("y", bt, j0 // HALF), lambda bt=bt, copy=copy: round_y(bt, j0, j1, copy))
+                later(lag, ("y", bt, j0 // HALF), lambda bt=bt, copy=copy: round_y(bt, start, j1, copy))
 
         def last_score(bt, j0, j1):
             width = j1 - j0
 
             def finish(bank):
                 gain_and_bias(y_f32[bt][:, j0:j1], bank[:, 0:width], bias_all[:, j0:j1], bt)
-                store_y(bt, j0, j1)
+                store_y(bt, 1, j0, j1)
 
             def rounded(bank):
                 target = split_view(bt, j0, j1)
@@ -356,27 +364,65 @@ def tile_rp3beta_item_scores_k5_kernel(
             tensor_step((), lambda bank: score_passes(bank[:, 0:width], bt, j0, j1), rounded)
 
 
-        def turn_y(bt, count, jh, copy):
+        def turn_y(bt, jh, copy):
+            n, first = divmod(bt, 4)
+            if first == 0:
+                y_grouped[(jh, n)] = work.tile(
+                    [P, 4 * P * 4], BF16, name="y_grouped", tag="y_grouped", bufs=4, align_bytes=64
+                )
+
             def turn(bank):
-                pairs = [y_split[(bt + c, jh)][:].bitcast(F32) for c in range(count)]
+                pairs = [y_split[(bt + c, jh)][:].bitcast(F32) for c in range(2)]
                 transposes(bank, [tile_pairs[:, P * u : P * (u + 1)] for tile_pairs in pairs for u in range(2)])
 
             def group(bank):
-                target = y_grouped[jh][:, P * bt : P * (bt + count), :].rearrange("q b t -> q (b t)").bitcast(F32)
-                copy(
-                    out=target.rearrange("q (c b u) -> q c b u", c=count, u=2),
-                    in_=bank[:, 0 : 2 * P * count].rearrange("q (c u b) -> q c b u", c=count, u=2),
-                )
+                target = y_grouped[(jh, n)][:].bitcast(F32).rearrange("q (b c u) -> q b c u", c=4, u=2)
+                copy(out=target[:, :, first : first + 2, :], in_=bank[:].rearrange("q (c u b) -> q b c u", c=2, u=2))
 
-            tensor_step([("y", bt + c, jh) for c in range(count)], turn, group)
+            tensor_step([("y", bt + c, jh) for c in range(2)], turn, group)
 
-        def quantize_y(jh, bt0, bt1):
-            users = slice(P * bt0, P * bt1)
+        def quantize_y(jh, u0, u1):
+            users = slice(P * u0, P * u1)
             nc.vector.quantize_mx(
                 out=y_codes[jh][:, users].bitcast(FP8X4),
                 scales=y_scales[:, jh, users],
-                in_=y_grouped[jh][:, users, :].rearrange("q b t -> q (b t)"),
+                in_=y_grouped[(jh, u0 // 4)][:, 4 * P * (u0 % 4) : 4 * P * (u0 % 4 + u1 - u0)],
             )
+
+        block_turned = {}
+        block_grouped = {}
+
+        def turn_blocks(h):
+            release([("y", 2 * h + c, 0) for c in range(2)])
+            block_turned[h] = work.tile([P, HALF], F32, name="block_turned", tag="block_turned", bufs=2, align_bytes=64)
+            nc.vector.transpose(out=block_turned[h][:], in_=first_split[h][:].bitcast(F32))
+
+        def group_blocks(h, copy):
+            n, c = divmod(2 * h, 4)
+            if c == 0:
+                block_grouped[n] = work.tile([P, 4 * P * 4], BF16, name="y_grouped", tag="y_grouped", bufs=4, align_bytes=64)
+            target = block_grouped[n][:].bitcast(F32).rearrange("q (b x c u) -> q b x c u", b=4, c=4, u=2)
+            copy(
+                out=target[:, :, :, c : c + 2, :].rearrange("q b x c u -> q b x (c u)"),
+                in_=block_turned[h][:].rearrange("q (s b x) -> q b x s", s=4, b=4),
+            )
+
+        def block_planes(n):
+            users = slice(HALF * n, HALF * (n + 1))
+            nc.vector.quantize_mx(
+                out=y_codes[0][:, users].bitcast(FP8X4), scales=y_scales[:, 0, users], in_=block_grouped[n][:]
+            )
+            rows = out_1[0].rearrange("p m t -> p (m t)").bitcast(I32)[:, users].rearrange("(b c) m -> c b m", c=QUAD)
+            for a in range(4):
+                nc.sync.dma_start(
+                    out=rows[:, :, P * a : P * (a + 1)],
+                    in_=y_codes[0][QUAD * a : QUAD * (a + 1), users].bitcast(I32).rearrange("c (b m) -> c b m", b=4),
+                )
+            for r in range(4):
+                nc.sync.dma_start(
+                    out=out_2[0, r:16:4, users].bitcast(I32).rearrange("b (a m) -> a b m", a=4),
+                    in_=y_scales[r:P:QUAD, 0, users].bitcast(I32).rearrange("a (b m) -> a b m", b=4),
+                )
 
         def store_codes(jh, bt0, bt1):
             users = slice(P * bt0, P * bt1)
@@ -417,20 +463,14 @@ def tile_rp3beta_item_scores_k5_kernel(
         split_prefs(1)
         walk(2, 1)
         walk(3, 1)
-        nc.vector.tensor_copy(out=gain_rows_f32[:], in_=gain_rows[:])
-        tensor_step(
-            (),
-            lambda bank: transposes(bank, [gain_rows_f32[:]]),
-            lambda bank: nc.vector.tensor_copy(out=gain_cols[:], in_=bank[:, 0:16]),
-        )
-        turn_sim(0, 2, 0, on_vector, SIM_LAG)
-        turn_sim(2, 2, 0, on_scalar, SIM_LAG)
-        turn_prefs(0, on_vector)
+        turn_sim([(0, 0), (1, 0)], on_scalar, SIM_LAG)
+        turn_sim([(2, 0), (3, 0)], on_vector, SIM_LAG)
+        turn_prefs(0, on_scalar)
         turn_prefs(1, on_scalar)
-        turn_sim(0, 2, 1, on_scalar, SIM_LAG)
-        turn_sim(2, 2, 1, on_scalar, SIM_LAG)
+        turn_sim([(0, 1), (1, 1)], on_vector, SIM_LAG)
+        turn_sim([(2, 1), (3, 1)], on_scalar, SIM_LAG)
         turn_prefs(2, on_scalar)
-        turn_prefs(3, on_scalar)
+        turn_prefs(3, on_vector)
         walk(4, 0)
         split_prefs(2)
         walk(5, 0)
@@ -441,19 +481,23 @@ def tile_rp3beta_item_scores_k5_kernel(
         split_prefs(4)
         first_half(2, True)
         first_half(3, True)
+        turn_blocks(0)
         walk(5, 1)
         split_prefs(5)
+        turn_blocks(1)
         turn_prefs(4, on_scalar)
-        turn_prefs(5, on_vector)
+        turn_prefs(5, on_scalar)
+        group_blocks(0, on_vector)
+        group_blocks(1, on_vector)
         turn_prefs(6, on_scalar)
         turn_prefs(7, on_scalar)
-        turn_sim(4, 2, 0, on_vector, SIM_LAG)
-        turn_sim(4, 2, 1, on_scalar, SIM_LAG)
+        turn_sim([(4, 0), (5, 0)], on_scalar, SIM_LAG)
+        block_planes(0)
+        turn_sim([(4, 1), (5, 1)], on_scalar, SIM_LAG)
         turn_prefs(8, on_scalar)
-        turn_prefs(9, on_vector)
+        turn_prefs(9, on_scalar)
         turn_prefs(10, on_scalar)
         turn_prefs(11, on_scalar)
-        turn_y(0, 2, 0, on_scalar)
         walk(6, 0)
         first_half(4, True)
         first_half(5, True)
@@ -465,23 +509,21 @@ def tile_rp3beta_item_scores_k5_kernel(
         score((8, 9), HALF, 768, 0, (on_gpsimd, on_scalar))
         score((10,), 0, HALF, None, (on_gpsimd,))
         score((11,), 0, HALF, None, (on_scalar,))
-        score((10, 11), HALF, 768, 0, (on_scalar, on_scalar))
-        turn_y(2, 2, 0, on_scalar)
-        turn_y(4, 2, 0, on_vector)
-        planes_later(0, 0, 4, 1)
-        turn_y(6, 2, 0, on_scalar)
-        turn_sim(6, 2, 0, on_vector, 3)
-        planes_later(0, 4, 8, 1)
-        turn_y(8, 2, 0, on_scalar)
-        turn_y(10, 2, 0, on_scalar)
-        planes_later(0, 8, 12, 2)
+        score((10, 11), HALF, 768, 0, (on_gpsimd, on_scalar))
         walk(6, 1)
+        turn_y(4, 0, on_vector)
+        turn_y(6, 0, on_scalar)
+        planes_later(0, 4, 8, 2)
+        turn_sim([(6, 0), (7, 0)], on_vector, 3)
+        turn_y(8, 0, on_scalar)
+        turn_sim([(6, 1)], on_scalar, 3)
+        turn_y(10, 0, on_scalar)
+        planes_later(0, 8, 12, 2)
         walk(7, 1)
         score((0, 1), HALF, 768, HALF, (on_scalar, on_scalar), 4)
         score((2, 3), HALF, 768, HALF, (on_scalar, on_scalar), 4)
-        store_scales(slice(0, 1), 0, 12, (nc.sync,))
-        turn_sim(6, 1, 1, on_scalar, 2)
-        turn_sim(7, 1, 1, on_scalar, 1)
+        store_scales(slice(0, 1), 4, 12, (nc.sync,))
+        turn_sim([(7, 1)], on_scalar, 1)
         score((4, 5), HALF, 768, HALF, (on_gpsimd, on_scalar))
         score((6, 7), HALF, 768, HALF, (on_gpsimd, on_scalar))
         score((0, 1), 768, I, 768, (on_gpsimd, on_scalar))
@@ -489,18 +531,17 @@ def tile_rp3beta_item_scores_k5_kernel(
         score((4, 5), 768, I, 768, (on_gpsimd, on_scalar))
         score((6, 7), 768, I, 768, (on_gpsimd, on_scalar))
         score((8, 9), 768, I, 768, (on_gpsimd, on_scalar))
-        turn_y(0, 2, 1, on_scalar)
-        turn_y(2, 2, 1, on_vector)
-        turn_y(4, 2, 1, on_scalar)
+        turn_y(0, 1, on_scalar)
+        turn_y(2, 1, on_vector)
+        turn_y(4, 1, on_scalar)
         last_score(10, 768, I)
         last_score(11, 768, I)
-        turn_y(6, 2, 1, on_scalar)
-        planes(1, 0, 4)
-        turn_y(8, 2, 1, on_scalar)
+        turn_y(6, 1, on_scalar)
         release(everything=True)
-        turn_y(10, 2, 1, on_scalar)
+        planes(1, 0, 4)
+        turn_y(8, 1, on_scalar)
+        turn_y(10, 1, on_scalar)
         planes(1, 4, 8)
-        quantize_y(1, 8, 10)
-        quantize_y(1, 10, 12)
-        store_codes(1, 8, 12)
+        planes(1, 8, 10)
+        planes(1, 10, 12)
         store_scales(slice(1, 2), 0, 12, (nc.scalar, nc.sync))

@@ -20,18 +20,19 @@ ACT = mybir.ActivationFunctionType
 P = 128
 QUAD = 32
 HALF = 512
+LAST = 768
 U_PASSES = U // 512
 I_PASSES = I // 512
 ITEM_TILES = I // P
 USER_TILES = B // P
+GROUP = 4
 BANKS = 8
 WARM_PASSES = 6
+VECTOR_TURN = 3
 
 ROUND_LAG = 2
-PREFS_LAG = 3
-SIM_LAG = 3
-PLANES_LAG = 4
-LAST_LAG = 4
+OPERAND_LAG = 3
+PLANES_LAG = 2
 
 
 def tile_rp3beta_item_scores_k5_kernel(
@@ -71,6 +72,8 @@ def tile_rp3beta_item_scores_k5_kernel(
         sim_t = {}
         sim_codes = [kept("sim_codes%d" % h, [P, I_PASSES, HALF], U32) for h in range(2)]
         sim_scales = [kept("sim_scales%d" % h, [P, I_PASSES, HALF], U8) for h in range(2)]
+        y_f32 = [kept("y%d" % n, [P, GROUP, I], F32) for n in range(USER_TILES // GROUP)]
+        y_split = {(bt, jh): kept("y_split%d_%d" % (bt, jh), [P, HALF], BF16) for jh in (0, 1) for bt in range(USER_TILES)}
         y_grouped = {}
         y_codes = [kept("y_codes%d" % h, [P, B], U32) for h in range(2)]
         y_scales = kept("y_scales", [P, 2, B], U8)
@@ -93,18 +96,18 @@ def tile_rp3beta_item_scores_k5_kernel(
                 in_=src[g0:g1, :, 2 * HALF * h : 2 * HALF * (h + 1)].rearrange("g p n -> p g n").bitcast(I32),
             )
 
-        def load_scales(dst, src, h, rows=range(4)):
-            for r in rows:
+        def load_scales(dst, src, h):
+            for r in range(4):
                 nc.sync.dma_start(
                     out=dst[h][r:P:QUAD, :, :].bitcast(I32),
                     in_=src[:, r:16:4, HALF * h : HALF * (h + 1)].rearrange("g q n -> q g n").bitcast(I32),
                 )
 
         def by_tiles(rows):
-            return rows.rearrange("(n p c) x -> n p c x", p=P, c=4)
+            return rows.rearrange("(n p c) x -> n p c x", p=P, c=GROUP)
 
         def load_prefs(k):
-            n, c = divmod(2 * k, 4)
+            n, c = divmod(2 * k, GROUP)
             nc.sync.dma_start(out=prefs_raw[k][:], in_=by_tiles(prefs)[n][:, c : c + 2, :])
 
         def clear(tile_ap):
@@ -147,7 +150,8 @@ def tile_rp3beta_item_scores_k5_kernel(
         load_words(nc.sync, l_words, item_user_words, 1, 0, U_PASSES)
         load_prefs(0)
         nc.sync.dma_start(
-            out=gain_cols[:].rearrange("p (n c) -> p n c", c=4), in_=user_gain.rearrange("(n p c) -> p n c", p=P, c=4)
+            out=gain_cols[:].rearrange("p (n c) -> p n c", c=GROUP),
+            in_=user_gain.rearrange("(n p c) -> p n c", p=P, c=GROUP),
         )
         load_prefs(1)
         load_scales(r_scales, user_item_scales, 1)
@@ -171,10 +175,10 @@ def tile_rp3beta_item_scores_k5_kernel(
         def later(lag, product, call):
             waiting.append((steps_done[0] + lag, product, call))
 
-        def release(needed=(), everything=False):
+        def release(needed=()):
             for entry in list(waiting):
                 due, product, call = entry
-                if everything or (product in needed if needed else due <= steps_done[0]):
+                if product in needed if needed else due <= steps_done[0]:
                     waiting.remove(entry)
                     call()
 
@@ -217,9 +221,8 @@ def tile_rp3beta_item_scores_k5_kernel(
 
             tensor_step((), passes, lambda bank: walk_out(bank, jt, ih))
 
-        def turn_sim(units, copy, lag):
-            count = len(units)
-            pairs = [sim_t[unit][:].bitcast(F32) for unit in units]
+        def turn_sim(jt, count, g, copy):
+            pairs = [sim_t[(jt + c, g)][:].bitcast(F32) for c in range(count)]
             grouped = work.tile([P, count * P * 4], BF16, name="sim_grouped", tag="sim_grouped", bufs=4, align_bytes=64)
 
             def group(bank):
@@ -228,22 +231,16 @@ def tile_rp3beta_item_scores_k5_kernel(
                     in_=bank[:, 0 : 2 * P * count].rearrange("q (c u j) -> q c j u", c=count, u=2),
                 )
 
+            def quantize():
+                jh, c = divmod(jt, 4)
+                columns = slice(P * c, P * (c + count))
+                nc.vector.quantize_mx(
+                    out=sim_codes[jh][:, g, columns].bitcast(FP8X4), scales=sim_scales[jh][:, g, columns], in_=grouped[:]
+                )
+
             sources = [tile_pairs[:, P * u : P * (u + 1)] for tile_pairs in pairs for u in range(2)]
             tensor_step((), lambda bank: transposes(bank, sources), group)
-            if units[0][1] == units[-1][1]:
-                later(lag, ("sim",) + units[0], lambda: quantize_sim(units[0], count, grouped[:]))
-            else:
-                for n, unit in enumerate(units):
-                    part = grouped[:, 4 * P * n : 4 * P * (n + 1)]
-                    later(lag, ("sim",) + unit, lambda unit=unit, part=part: quantize_sim(unit, 1, part))
-
-        def quantize_sim(unit, count, values):
-            jt, g = unit
-            jh, c = divmod(jt, 4)
-            columns = slice(P * c, P * (c + count))
-            nc.vector.quantize_mx(
-                out=sim_codes[jh][:, g, columns].bitcast(FP8X4), scales=sim_scales[jh][:, g, columns], in_=values
-            )
+            return quantize
 
 
         def split_prefs(k):
@@ -255,15 +252,6 @@ def tile_rp3beta_item_scores_k5_kernel(
                 in_=source.rearrange("q (s n u r) -> q s u n r", s=4, u=2, r=8),
             )
 
-        def group_prefs(bt, copy, source):
-            k, c = divmod(bt, 2)
-            if c == 0:
-                prefs_grouped[k] = work.tile(
-                    [P, 2 * I_PASSES * P * 4], BF16, name="prefs_grouped", tag="prefs_grouped", bufs=3, align_bytes=64
-                )
-            target = prefs_grouped[k][:, I * c : I * (c + 1)].bitcast(F32)
-            copy(out=target.rearrange("q (g b u) -> q g b u", g=I_PASSES, u=2), in_=source)
-
         def quantize_prefs(k):
             nc.vector.quantize_mx(
                 out=prefs_codes[k][:].rearrange("q c g b -> q (c g b)").bitcast(FP8X4),
@@ -274,29 +262,29 @@ def tile_rp3beta_item_scores_k5_kernel(
         def turn_prefs(bt, copy):
             k, c = divmod(bt, 2)
             pairs = prefs_split[k][:].rearrange("q c i -> q (c i)").bitcast(F32)
-            tensor_step(
-                (),
-                lambda bank: transposes(bank, [pairs[:, P * (4 * c + s) : P * (4 * c + s + 1)] for s in range(4)]),
-                lambda bank: group_prefs(bt, copy, bank[:].rearrange("q (g u b) -> q g b u", g=I_PASSES, u=2)),
-            )
+            if c == 0:
+                prefs_grouped[k] = work.tile(
+                    [P, 2 * I], BF16, name="prefs_grouped", tag="prefs_grouped", bufs=3, align_bytes=64
+                )
+
+            def group(bank):
+                target = prefs_grouped[k][:, I * c : I * (c + 1)].bitcast(F32)
+                copy(
+                    out=target.rearrange("q (g b u) -> q g b u", g=I_PASSES, u=2),
+                    in_=bank[:].rearrange("q (g u b) -> q g b u", g=I_PASSES, u=2),
+                )
+
+            sources = [pairs[:, P * (4 * c + s) : P * (4 * c + s + 1)] for s in range(4)]
+            tensor_step((), lambda bank: transposes(bank, sources), group)
             if c == 1:
-                later(PREFS_LAG, ("prefs", k), lambda: quantize_prefs(k))
+                later(OPERAND_LAG, ("prefs", k), lambda: quantize_prefs(k))
 
 
-        y_quads = [kept("y%d" % n, [P, 4, I], F32) for n in range(USER_TILES // 4)]
-        y_f32 = [y_quads[bt // 4][:, bt % 4, :] for bt in range(USER_TILES)]
-        first_split = [kept("first_split%d" % h, [P, 2 * HALF], BF16) for h in range(2)]
-        y_split = {(bt, 0): first_split[bt // 2][:, HALF * (bt % 2) : HALF * (bt % 2 + 1)] for bt in range(4)}
-        for bt in range(USER_TILES):
-            for jh in range(2):
-                if (bt, jh) not in y_split:
-                    y_split[(bt, jh)] = kept("y_bf%d_%d" % (bt, jh), [P, HALF], BF16)
-
-        def score_passes(out, bt, j0, j1, passes=range(I_PASSES)):
+        def score_passes(out, bt, j0, j1):
             k, c = divmod(bt, 2)
             jh, lo = divmod(j0, HALF)
             columns = slice(lo, lo + j1 - j0)
-            for g in passes:
+            for g in range(I_PASSES):
                 nc.tensor.matmul_mx(
                     out=out,
                     lhsT=prefs_codes[k][:, c, g, :].bitcast(FP8X4),
@@ -307,15 +295,18 @@ def tile_rp3beta_item_scores_k5_kernel(
                     stop=(g == I_PASSES - 1),
                 )
 
+        def y_tile(bt, j0, j1):
+            n, c = divmod(bt, GROUP)
+            return y_f32[n][:, c, j0:j1]
+
         def gain_and_bias(out, scores, bias, bt):
             nc.vector.scalar_tensor_tensor(
                 out=out, in0=scores, scalar=gain_cols[:, bt : bt + 1], in1=bias, op0=ALU.mult, op1=ALU.add
             )
 
         def store_y(bt, count, j0, j1):
-            n, c = divmod(bt, 4)
-            rows = by_tiles(out_0)[n][:, c : c + count, j0:j1]
-            nc.sync.dma_start(out=rows, in_=y_quads[n][:, c : c + count, j0:j1])
+            n, c = divmod(bt, GROUP)
+            nc.sync.dma_start(out=by_tiles(out_0)[n][:, c : c + count, j0:j1], in_=y_f32[n][:, c : c + count, j0:j1])
 
         def by_pairs(columns):
             return columns.rearrange("q (m u e) -> q u m e", u=2, e=2)
@@ -326,49 +317,59 @@ def tile_rp3beta_item_scores_k5_kernel(
             return whole[:, :, lo // 4 : (lo + j1 - j0) // 4, :]
 
         def round_y(bt, j0, j1, copy):
-            copy(out=split_view(bt, j0, j1), in_=by_pairs(y_f32[bt][:, j0:j1]))
+            copy(out=split_view(bt, j0, j1), in_=by_pairs(y_tile(bt, j0, j1)))
 
-        def score(tiles, j0, j1, stored_from, copies, lag=ROUND_LAG, rounded_from=None):
+        def score(bt, count, j0, j1):
             width = j1 - j0
 
             def passes(bank):
-                for n, bt in enumerate(tiles):
-                    score_passes(bank[:, width * n : width * (n + 1)], bt, j0, j1)
+                for n in range(count):
+                    score_passes(bank[:, width * n : width * (n + 1)], bt + n, j0, j1)
 
             def finish(bank):
-                for n, bt in enumerate(tiles):
-                    gain_and_bias(y_f32[bt][:, j0:j1], bank[:, width * n : width * (n + 1)], bias_all[:, j0:j1], bt)
-                if stored_from is not None:
-                    store_y(tiles[0], len(tiles), stored_from, j1)
+                for n in range(count):
+                    scores = bank[:, width * n : width * (n + 1)]
+                    gain_and_bias(y_tile(bt + n, j0, j1), scores, bias_all[:, j0:j1], bt + n)
 
-            needed = [("prefs", bt // 2) for bt in tiles]
-            needed.extend(("sim", jt, g) for jt in range(j0 // P, j1 // P) for g in range(I_PASSES))
-            tensor_step(needed, passes, finish)
-            start = j0 if rounded_from is None else rounded_from
-            for bt, copy in zip(tiles, copies):
-                later(lag, ("y", bt, j0 // HALF), lambda bt=bt, copy=copy: round_y(bt, start, j1, copy))
+            tensor_step([("prefs", bt // 2)], passes, finish)
 
-        def last_score(bt, j0, j1):
-            width = j1 - j0
+        def score_and_round(bt, count, j0, j1):
+            score(bt, count, j0, j1)
+            for tile in range(bt, bt + count):
+                copy = on_scalar if tile % 2 else on_gpsimd
+                later(ROUND_LAG, ("y", tile, j0 // HALF), lambda tile=tile, copy=copy: round_y(tile, j0, j1, copy))
 
-            def finish(bank):
-                gain_and_bias(y_f32[bt][:, j0:j1], bank[:, 0:width], bias_all[:, j0:j1], bt)
-                store_y(bt, 1, j0, j1)
+        def first_half(tiles):
+            for bt in tiles:
+                score_and_round(bt, 1, 0, HALF)
+                store_y(bt, 1, 0, HALF)
+
+        def quarter(bt, j0, j1):
+            score_and_round(bt, 2, j0, j1)
+            store_y(bt, 2, j0, j1)
+
+        def rounded_score(bt):
+            banks = []
 
             def rounded(bank):
-                target = split_view(bt, j0, j1)
+                scores, bias = by_pairs(bank[:, 0 : I - LAST]), by_pairs(bias_all[:, LAST:I])
                 for u in range(2):
-                    gain_and_bias(target[:, u], by_pairs(bank[:, 0:width])[:, u], by_pairs(bias_all[:, j0:j1])[:, u], bt)
-                later(LAST_LAG, ("y32", bt), lambda: finish(bank))
+                    gain_and_bias(split_view(bt, LAST, I)[:, u], scores[:, u], bias[:, u], bt)
+                banks.append(bank)
 
-            tensor_step((), lambda bank: score_passes(bank[:, 0:width], bt, j0, j1), rounded)
+            def finish():
+                gain_and_bias(y_tile(bt, LAST, I), banks[0][:, 0 : I - LAST], bias_all[:, LAST:I], bt)
+                store_y(bt, 1, LAST, I)
+
+            tensor_step((), lambda bank: score_passes(bank[:, 0 : I - LAST], bt, LAST, I), rounded)
+            return finish
 
 
         def turn_y(bt, jh, copy):
-            n, first = divmod(bt, 4)
+            n, first = divmod(bt, GROUP)
             if first == 0:
                 y_grouped[(jh, n)] = work.tile(
-                    [P, 4 * P * 4], BF16, name="y_grouped", tag="y_grouped", bufs=4, align_bytes=64
+                    [P, GROUP * P * 4], BF16, name="y_grouped", tag="y_grouped", bufs=4, align_bytes=64
                 )
 
             def turn(bank):
@@ -376,75 +377,52 @@ def tile_rp3beta_item_scores_k5_kernel(
                 transposes(bank, [tile_pairs[:, P * u : P * (u + 1)] for tile_pairs in pairs for u in range(2)])
 
             def group(bank):
-                target = y_grouped[(jh, n)][:].bitcast(F32).rearrange("q (b c u) -> q b c u", c=4, u=2)
+                target = y_grouped[(jh, n)][:].bitcast(F32).rearrange("q (b c u) -> q b c u", c=GROUP, u=2)
                 copy(out=target[:, :, first : first + 2, :], in_=bank[:].rearrange("q (c u b) -> q b c u", c=2, u=2))
 
             tensor_step([("y", bt + c, jh) for c in range(2)], turn, group)
 
-        def quantize_y(jh, u0, u1):
-            users = slice(P * u0, P * u1)
+        def planes(jh, n, b0=0, b1=GROUP * P):
+            users = slice(GROUP * P * n + b0, GROUP * P * n + b1)
             nc.vector.quantize_mx(
                 out=y_codes[jh][:, users].bitcast(FP8X4),
                 scales=y_scales[:, jh, users],
-                in_=y_grouped[(jh, u0 // 4)][:, 4 * P * (u0 % 4) : 4 * P * (u0 % 4 + u1 - u0)],
+                in_=y_grouped[(jh, n)][:, 4 * b0 : 4 * b1],
             )
-
-        block_turned = {}
-        block_grouped = {}
-
-        def turn_blocks(h):
-            release([("y", 2 * h + c, 0) for c in range(2)])
-            block_turned[h] = work.tile([P, HALF], F32, name="block_turned", tag="block_turned", bufs=2, align_bytes=64)
-            nc.vector.transpose(out=block_turned[h][:], in_=first_split[h][:].bitcast(F32))
-
-        def group_blocks(h, copy):
-            n, c = divmod(2 * h, 4)
-            if c == 0:
-                block_grouped[n] = work.tile([P, 4 * P * 4], BF16, name="y_grouped", tag="y_grouped", bufs=4, align_bytes=64)
-            target = block_grouped[n][:].bitcast(F32).rearrange("q (b x c u) -> q b x c u", b=4, c=4, u=2)
-            copy(
-                out=target[:, :, :, c : c + 2, :].rearrange("q b x c u -> q b x (c u)"),
-                in_=block_turned[h][:].rearrange("q (s b x) -> q b x s", s=4, b=4),
-            )
-
-        def block_planes(n):
-            users = slice(HALF * n, HALF * (n + 1))
-            nc.vector.quantize_mx(
-                out=y_codes[0][:, users].bitcast(FP8X4), scales=y_scales[:, 0, users], in_=block_grouped[n][:]
-            )
-            rows = out_1[0].rearrange("p m t -> p (m t)").bitcast(I32)[:, users].rearrange("(b c) m -> c b m", c=QUAD)
-            for a in range(4):
-                nc.sync.dma_start(
-                    out=rows[:, :, P * a : P * (a + 1)],
-                    in_=y_codes[0][QUAD * a : QUAD * (a + 1), users].bitcast(I32).rearrange("c (b m) -> c b m", b=4),
-                )
-            for r in range(4):
-                nc.sync.dma_start(
-                    out=out_2[0, r:16:4, users].bitcast(I32).rearrange("b (a m) -> a b m", a=4),
-                    in_=y_scales[r:P:QUAD, 0, users].bitcast(I32).rearrange("a (b m) -> a b m", b=4),
-                )
-
-        def store_codes(jh, bt0, bt1):
-            users = slice(P * bt0, P * bt1)
             nc.sync.dma_start(
                 out=out_1[jh].rearrange("p m t -> p (m t)").bitcast(I32)[:, users],
                 in_=y_codes[jh][:, users].bitcast(I32),
             )
 
-        def store_scales(halves, bt0, bt1, queues):
-            users = slice(P * bt0, P * bt1)
+        def store_scales(jh, queues):
             for r in range(4):
                 queues[r % len(queues)].dma_start(
-                    out=out_2[halves, r:16:4, users].rearrange("g q m -> q g m").bitcast(I32),
-                    in_=y_scales[r:P:QUAD, halves, users].bitcast(I32),
+                    out=out_2[jh, r:16:4, :].bitcast(I32), in_=y_scales[r:P:QUAD, jh, :].bitcast(I32)
                 )
 
-        def planes(jh, bt0, bt1):
-            quantize_y(jh, bt0, bt1)
-            store_codes(jh, bt0, bt1)
 
-        def planes_later(jh, bt0, bt1, lag=PLANES_LAG):
-            later(lag, ("planes", jh, bt0), lambda: planes(jh, bt0, bt1))
+        def run(steps):
+            for n, step in enumerate(steps):
+                step(on_vector if n % VECTOR_TURN == 1 and n < len(steps) - 1 else on_scalar)
+
+        def prefs_steps(tiles):
+            return [lambda copy, bt=bt: turn_prefs(bt, copy) for bt in tiles]
+
+        def sim_steps(tiles, g):
+            return [
+                lambda copy, jt=jt: later(OPERAND_LAG, ("sim", jt, g), turn_sim(jt, 2, g, copy)) for jt in tiles[::2]
+            ]
+
+        def y_steps(tiles, jh):
+            return [lambda copy, bt=bt: turn_y(bt, jh, copy) for bt in tiles[::2]]
+
+        def first_half_y_steps(tiles):
+            def step(copy, bt):
+                turn_y(bt, 0, copy)
+                if bt % GROUP == GROUP - 2:
+                    later(PLANES_LAG, ("planes", bt), lambda: planes(0, bt // GROUP))
+
+            return [lambda copy, bt=bt: step(copy, bt) for bt in tiles[::2]]
 
 
         first_banks = [next_bank() for jt in range(4)]
@@ -454,94 +432,59 @@ def tile_rp3beta_item_scores_k5_kernel(
         for jt in range(4):
             walk_out(first_banks[jt], jt, 0)
 
-        def first_half(bt, stored):
-            score((bt,), 0, HALF, 0 if stored else None, (on_scalar if bt % 2 else on_gpsimd,))
+        for jt in range(4):
+            if jt % 2 == 0:
+                split_prefs(jt // 2)
+            walk(jt, 1)
+        run(sim_steps(range(4), 0) + prefs_steps(range(0, 2)) + sim_steps(range(4), 1) + prefs_steps(range(2, 4)))
 
-        split_prefs(0)
-        walk(0, 1)
-        walk(1, 1)
-        split_prefs(1)
-        walk(2, 1)
-        walk(3, 1)
-        turn_sim([(0, 0), (1, 0)], on_scalar, SIM_LAG)
-        turn_sim([(2, 0), (3, 0)], on_vector, SIM_LAG)
-        turn_prefs(0, on_scalar)
-        turn_prefs(1, on_scalar)
-        turn_sim([(0, 1), (1, 1)], on_vector, SIM_LAG)
-        turn_sim([(2, 1), (3, 1)], on_scalar, SIM_LAG)
-        turn_prefs(2, on_scalar)
-        turn_prefs(3, on_vector)
-        walk(4, 0)
-        split_prefs(2)
-        walk(5, 0)
-        split_prefs(3)
-        first_half(0, True)
-        first_half(1, True)
-        walk(4, 1)
-        split_prefs(4)
-        first_half(2, True)
-        first_half(3, True)
-        turn_blocks(0)
-        walk(5, 1)
-        split_prefs(5)
-        turn_blocks(1)
-        turn_prefs(4, on_scalar)
-        turn_prefs(5, on_scalar)
-        group_blocks(0, on_vector)
-        group_blocks(1, on_vector)
-        turn_prefs(6, on_scalar)
-        turn_prefs(7, on_scalar)
-        turn_sim([(4, 0), (5, 0)], on_scalar, SIM_LAG)
-        block_planes(0)
-        turn_sim([(4, 1), (5, 1)], on_scalar, SIM_LAG)
-        turn_prefs(8, on_scalar)
-        turn_prefs(9, on_scalar)
-        turn_prefs(10, on_scalar)
-        turn_prefs(11, on_scalar)
+        for jt in (4, 5):
+            walk(jt, 0)
+            split_prefs(jt - 2)
+        for jt in (4, 5):
+            first_half(range(2 * jt - 8, 2 * jt - 6))
+            walk(jt, 1)
+            split_prefs(jt)
+        run(
+            prefs_steps(range(4, 8)) + sim_steps(range(4, 6), 0) + sim_steps(range(4, 6), 1)
+            + prefs_steps(range(8, USER_TILES)) + first_half_y_steps(range(0, 2))
+        )
+
         walk(6, 0)
-        first_half(4, True)
-        first_half(5, True)
-        first_half(6, True)
-        first_half(7, True)
+        first_half(range(4, 8))
         walk(7, 0)
-        score((8,), 0, HALF, None, (on_gpsimd,))
-        score((9,), 0, HALF, None, (on_scalar,))
-        score((8, 9), HALF, 768, 0, (on_gpsimd, on_scalar))
-        score((10,), 0, HALF, None, (on_gpsimd,))
-        score((11,), 0, HALF, None, (on_scalar,))
-        score((10, 11), HALF, 768, 0, (on_gpsimd, on_scalar))
-        walk(6, 1)
-        turn_y(4, 0, on_vector)
-        turn_y(6, 0, on_scalar)
-        planes_later(0, 4, 8, 2)
-        turn_sim([(6, 0), (7, 0)], on_vector, 3)
-        turn_y(8, 0, on_scalar)
-        turn_sim([(6, 1)], on_scalar, 3)
-        turn_y(10, 0, on_scalar)
-        planes_later(0, 8, 12, 2)
-        walk(7, 1)
-        score((0, 1), HALF, 768, HALF, (on_scalar, on_scalar), 4)
-        score((2, 3), HALF, 768, HALF, (on_scalar, on_scalar), 4)
-        store_scales(slice(0, 1), 4, 12, (nc.sync,))
-        turn_sim([(7, 1)], on_scalar, 1)
-        score((4, 5), HALF, 768, HALF, (on_gpsimd, on_scalar))
-        score((6, 7), HALF, 768, HALF, (on_gpsimd, on_scalar))
-        score((0, 1), 768, I, 768, (on_gpsimd, on_scalar))
-        score((2, 3), 768, I, 768, (on_gpsimd, on_scalar))
-        score((4, 5), 768, I, 768, (on_gpsimd, on_scalar))
-        score((6, 7), 768, I, 768, (on_gpsimd, on_scalar))
-        score((8, 9), 768, I, 768, (on_gpsimd, on_scalar))
-        turn_y(0, 1, on_scalar)
-        turn_y(2, 1, on_vector)
-        turn_y(4, 1, on_scalar)
-        last_score(10, 768, I)
-        last_score(11, 768, I)
+        for bt in (8, 10):
+            for tile in (bt, bt + 1):
+                score_and_round(tile, 1, 0, HALF)
+            score_and_round(bt, 2, HALF, LAST)
+            store_y(bt, 2, 0, LAST)
+        run(first_half_y_steps(range(2, 4)) + sim_steps(range(6, 8), 0) + first_half_y_steps(range(4, USER_TILES)))
+
+        for jt in (6, 7):
+            walk(jt, 1)
+        for bt in (0, 2):
+            score(bt, 2, HALF, LAST)
+            store_y(bt, 2, HALF, LAST)
+        store_scales(0, (nc.sync,))
+        last_sim = [turn_sim(jt, 1, 1, on_scalar) for jt in (6, 7)]
+        for quantize in last_sim:
+            quantize()
+        for bt in range(4):
+            round_y(bt, HALF, LAST, on_scalar)
+        for bt in (4, 6):
+            quarter(bt, HALF, LAST)
+
+        for bt in range(0, USER_TILES - 2, 2):
+            quarter(bt, LAST, I)
+        run(y_steps(range(0, 6), 1))
+        last_f32 = [rounded_score(bt) for bt in (USER_TILES - 2, USER_TILES - 1)]
         turn_y(6, 1, on_scalar)
-        release(everything=True)
-        planes(1, 0, 4)
-        turn_y(8, 1, on_scalar)
-        turn_y(10, 1, on_scalar)
-        planes(1, 4, 8)
-        planes(1, 8, 10)
-        planes(1, 10, 12)
-        store_scales(slice(1, 2), 0, 12, (nc.scalar, nc.sync))
+        for finish in last_f32:
+            finish()
+        planes(1, 0)
+        for bt in (8, 10):
+            turn_y(bt, 1, on_scalar)
+        planes(1, 1)
+        planes(1, 2, 0, 2 * P)
+        planes(1, 2, 2 * P, GROUP * P)
+        store_scales(1, (nc.scalar, nc.sync))

@@ -25,7 +25,8 @@ U_PASSES = U // 512
 I_PASSES = I // 512
 ITEM_TILES = I // P
 USER_TILES = B // P
-GROUP = 4
+COUPLES = USER_TILES // 2
+GAIN_PAD = 16
 BANKS = 8
 WARM_PASSES = 6
 VECTOR_TURN = 3
@@ -72,12 +73,12 @@ def tile_rp3beta_item_scores_k5_kernel(
         sim_t = {}
         sim_codes = [kept("sim_codes%d" % h, [P, I_PASSES, HALF], U32) for h in range(2)]
         sim_scales = [kept("sim_scales%d" % h, [P, I_PASSES, HALF], U8) for h in range(2)]
-        y_f32 = [kept("y%d" % n, [P, GROUP, I], F32) for n in range(USER_TILES // GROUP)]
+        y_f32 = [kept("y%d" % k, [P, 2, I], F32) for k in range(COUPLES)]
         y_split = {(bt, jh): kept("y_split%d_%d" % (bt, jh), [P, HALF], BF16) for jh in (0, 1) for bt in range(USER_TILES)}
         y_grouped = {}
         y_codes = [kept("y_codes%d" % h, [P, B], U32) for h in range(2)]
         y_scales = kept("y_scales", [P, 2, B], U8)
-        gain_cols = kept("gain_cols", [P, USER_TILES], BF16)
+        gain_cols = kept("gain_cols", [P, COUPLES, GAIN_PAD], BF16)
         pop_rows = kept("pop_rows", [P, QUAD], BF16)
         pop_cols = kept("pop_cols", [P, QUAD], BF16)
         pop_own = kept("pop_own", [P, ITEM_TILES], F32)
@@ -104,11 +105,10 @@ def tile_rp3beta_item_scores_k5_kernel(
                 )
 
         def by_tiles(rows):
-            return rows.rearrange("(n p c) x -> n p c x", p=P, c=GROUP)
+            return rows.rearrange("(k p c) x -> k p c x", p=P, c=2)
 
         def load_prefs(k):
-            n, c = divmod(2 * k, GROUP)
-            nc.sync.dma_start(out=prefs_raw[k][:], in_=by_tiles(prefs)[n][:, c : c + 2, :])
+            nc.sync.dma_start(out=prefs_raw[k][:], in_=by_tiles(prefs)[k])
 
         def clear(tile_ap):
             nc.vector.memset(tile_ap.bitcast(I32), 0)
@@ -141,32 +141,36 @@ def tile_rp3beta_item_scores_k5_kernel(
             )
         load_scales(l_scales, item_user_scales, 0)
         load_scales(r_scales, user_item_scales, 0)
+        load_words(nc.sync, l_words, item_user_words, 0, 1, 2)
+        load_words(nc.sync, r_words, user_item_words, 0, 1, 2)
         nc.sync.dma_start(out=pop_rows[:], in_=rows_in_every_quadrant(popularity))
-        for g0, g1 in ((1, 2), (2, U_PASSES)):
-            load_words(nc.sync, l_words, item_user_words, 0, g0, g1)
-            load_words(nc.sync, r_words, user_item_words, 0, g0, g1)
-        nc.sync.dma_start(out=bias_rows[:], in_=rows_in_every_quadrant(item_bias))
+        load_words(nc.sync, l_words, item_user_words, 0, 2, 3)
+        load_words(nc.sync, r_words, user_item_words, 0, 2, 3)
+        load_words(nc.sync, l_words, item_user_words, 0, 3, 4)
+        load_words(nc.sync, r_words, user_item_words, 0, 3, 4)
         load_scales(l_scales, item_user_scales, 1)
         load_words(nc.sync, l_words, item_user_words, 1, 0, U_PASSES)
         load_prefs(0)
-        nc.sync.dma_start(
-            out=gain_cols[:].rearrange("p (n c) -> p n c", c=GROUP),
-            in_=user_gain.rearrange("(n p c) -> p n c", p=P, c=GROUP),
-        )
         load_prefs(1)
+        nc.sync.dma_start(out=bias_rows[:], in_=rows_in_every_quadrant(item_bias))
         load_scales(r_scales, user_item_scales, 1)
         load_words(nc.sync, r_words, user_item_words, 1, 0, U_PASSES)
-        for k in range(2, USER_TILES // 2):
-            load_prefs(k)
+        nc.sync.dma_start(out=gain_cols[:, :, 0:2], in_=user_gain.rearrange("(k p c) -> p k c", p=P, c=2))
+        load_prefs(2)
+        load_prefs(3)
+        load_prefs(4)
+        load_prefs(5)
 
         nc.vector.transpose(out=pop_cols[:], in_=pop_rows[:])
         for a in range(4):
             quadrant = slice(QUAD * a, QUAD * (a + 1))
             nc.scalar.activation(out=pop_own[quadrant, :], in_=pop_cols[quadrant, a:QUAD:4], func=ACT.Copy)
         nc.gpsimd.tensor_tensor(out=damping[:], in0=pop_own[:], in1=exponent[:], op=ALU.pow)
-        nc.vector.transpose(out=bias_cols[:], in_=bias_rows[:])
-        nc.vector.tensor_copy(out=bias_spread[:], in_=bias_cols[:].unsqueeze(2).to_broadcast([P, QUAD, QUAD]))
-        nc.vector.transpose(out=bias_all[:], in_=bias_spread[:].rearrange("p c y -> p (c y)"))
+
+        def spread_bias():
+            nc.vector.transpose(out=bias_cols[:], in_=bias_rows[:])
+            nc.vector.tensor_copy(out=bias_spread[:], in_=bias_cols[:].unsqueeze(2).to_broadcast([P, QUAD, QUAD]))
+            nc.vector.transpose(out=bias_all[:], in_=bias_spread[:].rearrange("p c y -> p (c y)"))
 
 
         steps_done = [0]
@@ -280,11 +284,11 @@ def tile_rp3beta_item_scores_k5_kernel(
                 later(OPERAND_LAG, ("prefs", k), lambda: quantize_prefs(k))
 
 
-        def score_passes(out, bt, j0, j1):
+        def score_passes(out, bt, j0, j1, passes=range(I_PASSES)):
             k, c = divmod(bt, 2)
             jh, lo = divmod(j0, HALF)
             columns = slice(lo, lo + j1 - j0)
-            for g in range(I_PASSES):
+            for g in passes:
                 nc.tensor.matmul_mx(
                     out=out,
                     lhsT=prefs_codes[k][:, c, g, :].bitcast(FP8X4),
@@ -296,17 +300,18 @@ def tile_rp3beta_item_scores_k5_kernel(
                 )
 
         def y_tile(bt, j0, j1):
-            n, c = divmod(bt, GROUP)
-            return y_f32[n][:, c, j0:j1]
+            k, c = divmod(bt, 2)
+            return y_f32[k][:, c, j0:j1]
 
         def gain_and_bias(out, scores, bias, bt):
             nc.vector.scalar_tensor_tensor(
-                out=out, in0=scores, scalar=gain_cols[:, bt : bt + 1], in1=bias, op0=ALU.mult, op1=ALU.add
+                out=out, in0=scores, scalar=gain_cols[:, bt // 2, bt % 2 : bt % 2 + 1], in1=bias,
+                op0=ALU.mult, op1=ALU.add,
             )
 
         def store_y(bt, count, j0, j1):
-            n, c = divmod(bt, GROUP)
-            nc.sync.dma_start(out=by_tiles(out_0)[n][:, c : c + count, j0:j1], in_=y_f32[n][:, c : c + count, j0:j1])
+            k, c = divmod(bt, 2)
+            nc.sync.dma_start(out=by_tiles(out_0)[k][:, c : c + count, j0:j1], in_=y_f32[k][:, c : c + count, j0:j1])
 
         def by_pairs(columns):
             return columns.rearrange("q (m u e) -> q u m e", u=2, e=2)
@@ -366,10 +371,10 @@ def tile_rp3beta_item_scores_k5_kernel(
 
 
         def turn_y(bt, jh, copy):
-            n, first = divmod(bt, GROUP)
-            if first == 0:
+            n, second = divmod(bt // 2, 2)
+            if second == 0:
                 y_grouped[(jh, n)] = work.tile(
-                    [P, GROUP * P * 4], BF16, name="y_grouped", tag="y_grouped", bufs=4, align_bytes=64
+                    [P, 2, 2 * P * 4], BF16, name="y_grouped", tag="y_grouped", bufs=4, align_bytes=64
                 )
 
             def turn(bank):
@@ -377,33 +382,34 @@ def tile_rp3beta_item_scores_k5_kernel(
                 transposes(bank, [tile_pairs[:, P * u : P * (u + 1)] for tile_pairs in pairs for u in range(2)])
 
             def group(bank):
-                target = y_grouped[(jh, n)][:].bitcast(F32).rearrange("q (b c u) -> q b c u", c=GROUP, u=2)
-                copy(out=target[:, :, first : first + 2, :], in_=bank[:].rearrange("q (c u b) -> q b c u", c=2, u=2))
+                target = y_grouped[(jh, n)][:, second, :].bitcast(F32).rearrange("q (b c u) -> q b c u", c=2, u=2)
+                copy(out=target, in_=bank[:].rearrange("q (c u b) -> q b c u", c=2, u=2))
 
             tensor_step([("y", bt + c, jh) for c in range(2)], turn, group)
 
-        def planes(jh, n, b0=0, b1=GROUP * P):
-            users = slice(GROUP * P * n + b0, GROUP * P * n + b1)
+        def planes(jh, k, count):
+            n, first = divmod(k, 2)
+            users = slice(2 * P * k, 2 * P * (k + count))
             nc.vector.quantize_mx(
                 out=y_codes[jh][:, users].bitcast(FP8X4),
                 scales=y_scales[:, jh, users],
-                in_=y_grouped[(jh, n)][:, 4 * b0 : 4 * b1],
+                in_=y_grouped[(jh, n)][:, first : first + count, :].rearrange("q k x -> q (k x)"),
             )
             nc.sync.dma_start(
                 out=out_1[jh].rearrange("p m t -> p (m t)").bitcast(I32)[:, users],
                 in_=y_codes[jh][:, users].bitcast(I32),
             )
 
-        def store_scales(jh, queues):
+        def store_scales(jh, queues, b0=0, b1=B):
             for r in range(4):
                 queues[r % len(queues)].dma_start(
-                    out=out_2[jh, r:16:4, :].bitcast(I32), in_=y_scales[r:P:QUAD, jh, :].bitcast(I32)
+                    out=out_2[jh, r:16:4, b0:b1].bitcast(I32), in_=y_scales[r:P:QUAD, jh, b0:b1].bitcast(I32)
                 )
 
 
-        def run(steps):
+        def run(steps, turn=VECTOR_TURN):
             for n, step in enumerate(steps):
-                step(on_vector if n % VECTOR_TURN == 1 and n < len(steps) - 1 else on_scalar)
+                step(on_vector if n % turn == 1 and n < len(steps) - 1 else on_scalar)
 
         def prefs_steps(tiles):
             return [lambda copy, bt=bt: turn_prefs(bt, copy) for bt in tiles]
@@ -419,11 +425,17 @@ def tile_rp3beta_item_scores_k5_kernel(
         def first_half_y_steps(tiles):
             def step(copy, bt):
                 turn_y(bt, 0, copy)
-                if bt % GROUP == GROUP - 2:
-                    later(PLANES_LAG, ("planes", bt), lambda: planes(0, bt // GROUP))
+                if bt % 4 == 2:
+                    later(PLANES_LAG, ("planes", bt), lambda: planes(0, bt // 2 - 1, 2))
 
             return [lambda copy, bt=bt: step(copy, bt) for bt in tiles[::2]]
 
+
+        def three_quarters(bt):
+            for tile in (bt, bt + 1):
+                score_and_round(tile, 1, 0, HALF)
+            score_and_round(bt, 2, HALF, LAST)
+            store_y(bt, 2, 0, LAST)
 
         first_banks = [next_bank() for jt in range(4)]
         for g in range(U_PASSES):
@@ -436,8 +448,8 @@ def tile_rp3beta_item_scores_k5_kernel(
             if jt % 2 == 0:
                 split_prefs(jt // 2)
             walk(jt, 1)
+        spread_bias()
         run(sim_steps(range(4), 0) + prefs_steps(range(0, 2)) + sim_steps(range(4), 1) + prefs_steps(range(2, 4)))
-
         for jt in (4, 5):
             walk(jt, 0)
             split_prefs(jt - 2)
@@ -454,18 +466,15 @@ def tile_rp3beta_item_scores_k5_kernel(
         first_half(range(4, 8))
         walk(7, 0)
         for bt in (8, 10):
-            for tile in (bt, bt + 1):
-                score_and_round(tile, 1, 0, HALF)
-            score_and_round(bt, 2, HALF, LAST)
-            store_y(bt, 2, 0, LAST)
+            three_quarters(bt)
         run(first_half_y_steps(range(2, 4)) + sim_steps(range(6, 8), 0) + first_half_y_steps(range(4, USER_TILES)))
-
         for jt in (6, 7):
             walk(jt, 1)
+        release([("planes", bt) for bt in range(USER_TILES)])
+        store_scales(0, (nc.sync,))
         for bt in (0, 2):
             score(bt, 2, HALF, LAST)
             store_y(bt, 2, HALF, LAST)
-        store_scales(0, (nc.sync,))
         last_sim = [turn_sim(jt, 1, 1, on_scalar) for jt in (6, 7)]
         for quantize in last_sim:
             quantize()
@@ -474,17 +483,18 @@ def tile_rp3beta_item_scores_k5_kernel(
         for bt in (4, 6):
             quarter(bt, HALF, LAST)
 
-        for bt in range(0, USER_TILES - 2, 2):
+        for bt in range(0, USER_TILES, 2):
             quarter(bt, LAST, I)
-        run(y_steps(range(0, 6), 1))
-        last_f32 = [rounded_score(bt) for bt in (USER_TILES - 2, USER_TILES - 1)]
+        turn_y(0, 1, on_scalar)
+        turn_y(2, 1, on_vector)
+        turn_y(4, 1, on_scalar)
+        planes(1, 0, 1)
         turn_y(6, 1, on_scalar)
-        for finish in last_f32:
-            finish()
-        planes(1, 0)
-        for bt in (8, 10):
-            turn_y(bt, 1, on_scalar)
-        planes(1, 1)
-        planes(1, 2, 0, 2 * P)
-        planes(1, 2, 2 * P, GROUP * P)
-        store_scales(1, (nc.scalar, nc.sync))
+        planes(1, 1, 1)
+        turn_y(8, 1, on_vector)
+        planes(1, 2, 1)
+        turn_y(10, 1, on_scalar)
+        planes(1, 3, 1)
+        planes(1, 4, 1)
+        planes(1, 5, 1)
+        store_scales(1, (nc.scalar, nc.sync), 0, B)

@@ -118,10 +118,12 @@ def tile_rp3beta_item_scores_k5_kernel(
 
         ctx.enter_context(tc.manual_schedule())
 
-        nc.gpsimd.memset(r_scales[1][:].rearrange("p g n -> p (g n)").bitcast(I32), 0)
+        blank = r_scales[1][:, 0:2, :].rearrange("p g n -> p (g n)")
+        clear(blank)
         clear(l_scales[0][:].rearrange("p g n -> p (g n)"))
         clear(r_scales[0][:].rearrange("p g n -> p (g n)"))
         clear(l_scales[1][:].rearrange("p g n -> p (g n)"))
+        clear(r_scales[1][:, 2:U_PASSES, :].rearrange("p g n -> p (g n)"))
         clear(identity[:])
         make_identity(nc, identity[:], nomemset=True)
         nc.vector.memset(exponent[:], 1.0)
@@ -130,13 +132,12 @@ def tile_rp3beta_item_scores_k5_kernel(
         )
         load_words(nc.scalar, l_words, item_user_words, 0, 0, 1)
         load_words(nc.scalar, r_words, user_item_words, 0, 0, 1)
-        blank = r_scales[1][:].rearrange("p g n -> p (g n)")
         warm_bank = next_bank()
         for w in range(WARM_PASSES):
             nc.tensor.matmul_mx(
                 out=warm_bank[:],
-                lhsT=blank[:, 0 : 2 * P].bitcast(FP4X4), lhsT_scale=blank[:, 2 * HALF : 2 * HALF + P],
-                rhs=blank[:, 0 : 2 * HALF].bitcast(FP4X4), rhs_scale=blank[:, 2 * HALF : 3 * HALF],
+                lhsT=blank[:, 0 : 2 * P].bitcast(FP4X4), lhsT_scale=blank[:, 0:P],
+                rhs=blank[:, 0 : 2 * HALF].bitcast(FP4X4), rhs_scale=blank[:, 0:HALF],
                 start=True, stop=True,
             )
         load_scales(l_scales, item_user_scales, 0)

@@ -150,12 +150,16 @@ def tile_rp3beta_item_scores_k5_kernel(
         load_words(nc.sync, l_words, item_user_words, 0, 3, 4)
         load_words(nc.sync, r_words, user_item_words, 0, 3, 4)
         load_scales(l_scales, item_user_scales, 1)
-        load_words(nc.sync, l_words, item_user_words, 1, 0, U_PASSES)
+        load_words(nc.sync, l_words, item_user_words, 1, 0, 1)
+        load_words(nc.sync, l_words, item_user_words, 1, 1, 2)
+        load_words(nc.sync, l_words, item_user_words, 1, 2, 3)
+        load_words(nc.sync, l_words, item_user_words, 1, 3, 4)
         load_prefs(0)
         load_prefs(1)
         nc.sync.dma_start(out=bias_rows[:], in_=rows_in_every_quadrant(item_bias))
         load_scales(r_scales, user_item_scales, 1)
-        load_words(nc.sync, r_words, user_item_words, 1, 0, U_PASSES)
+        load_words(nc.sync, r_words, user_item_words, 1, 0, 2)
+        load_words(nc.sync, r_words, user_item_words, 1, 2, U_PASSES)
         nc.sync.dma_start(out=gain_cols[:, :, 0:2], in_=user_gain.rearrange("(k p c) -> p k c", p=P, c=2))
         load_prefs(2)
         load_prefs(3)
@@ -348,7 +352,8 @@ def tile_rp3beta_item_scores_k5_kernel(
         def first_half(tiles):
             for bt in tiles:
                 score_and_round(bt, 1, 0, HALF)
-                store_y(bt, 1, 0, HALF)
+                if bt % 2:
+                    store_y(bt - 1, 2, 0, HALF)
 
         def quarter(bt, j0, j1):
             score_and_round(bt, 2, j0, j1)
@@ -445,9 +450,14 @@ def tile_rp3beta_item_scores_k5_kernel(
         for jt in range(4):
             walk_out(first_banks[jt], jt, 0)
 
-        for jt in range(4):
-            if jt % 2 == 0:
-                split_prefs(jt // 2)
+        pair_banks = [next_bank() for jt in range(2)]
+        for g in range(U_PASSES):
+            for jt in range(2):
+                walk_pass(pair_banks[jt], jt, 1, g)
+        for jt in range(2):
+            walk_out(pair_banks[jt], jt, 1)
+        for jt in (2, 3):
+            split_prefs(jt - 2)
             walk(jt, 1)
         spread_bias()
         run(sim_steps(range(4), 0) + prefs_steps(range(0, 2)) + sim_steps(range(4), 1) + prefs_steps(range(2, 4)))

@@ -35,6 +35,11 @@ ROUND_LAG = 2
 OPERAND_LAG = 3
 PLANES_LAG = 2
 
+SIM_T_BUFS = 8
+SPLIT_BUFS = 4
+GROUPED_BUFS = 4
+PREFS_GROUPED_BUFS = 3
+
 
 def tile_rp3beta_item_scores_k5_kernel(
     tc, item_user_words, item_user_scales, user_item_words, user_item_scales,
@@ -65,11 +70,11 @@ def tile_rp3beta_item_scores_k5_kernel(
         r_words = [kept("r_words%d" % h, [P, U_PASSES, 2 * HALF], U8) for h in range(2)]
         l_scales = [kept("l_scales%d" % h, [P, U_PASSES, HALF], U8) for h in range(2)]
         r_scales = [kept("r_scales%d" % h, [P, U_PASSES, HALF], U8) for h in range(2)]
-        prefs_raw = [kept("prefs_raw%d" % k, [P, 2, I], BF16) for k in range(USER_TILES // 2)]
+        prefs_raw = [kept("prefs_raw%d" % k, [P, 2, I], BF16) for k in range(COUPLES)]
         prefs_split = {}
         prefs_grouped = {}
-        prefs_codes = [kept("prefs_codes%d" % k, [P, 2, I_PASSES, P], U32) for k in range(USER_TILES // 2)]
-        prefs_scales = [kept("prefs_scales%d" % k, [P, 2, I_PASSES, P], U8) for k in range(USER_TILES // 2)]
+        prefs_codes = [kept("prefs_codes%d" % k, [P, 2, I_PASSES, P], U32) for k in range(COUPLES)]
+        prefs_scales = [kept("prefs_scales%d" % k, [P, 2, I_PASSES, P], U8) for k in range(COUPLES)]
         sim_t = {}
         sim_codes = [kept("sim_codes%d" % h, [P, I_PASSES, HALF], U32) for h in range(2)]
         sim_scales = [kept("sim_scales%d" % h, [P, I_PASSES, HALF], U8) for h in range(2)]
@@ -91,10 +96,10 @@ def tile_rp3beta_item_scores_k5_kernel(
         bias_all = kept("bias_all", [P, I], BF16)
 
 
-        def load_words(queue, dst, src, h, g0, g1):
+        def load_words(queue, dst, src, h, g0, g1, c0=0, c1=HALF):
             queue.dma_start(
-                out=dst[h][:, g0:g1, :].bitcast(I32),
-                in_=src[g0:g1, :, 2 * HALF * h : 2 * HALF * (h + 1)].rearrange("g p n -> p g n").bitcast(I32),
+                out=dst[h][:, g0:g1, 2 * c0 : 2 * c1].bitcast(I32),
+                in_=src[g0:g1, :, 2 * (HALF * h + c0) : 2 * (HALF * h + c1)].rearrange("g p n -> p g n").bitcast(I32),
             )
 
         def load_scales(dst, src, h):
@@ -130,8 +135,8 @@ def tile_rp3beta_item_scores_k5_kernel(
         nc.gpsimd.tensor_scalar(
             out=exponent[:], in0=exponent[:], scalar1=-BETA, scalar2=0.0, op0=ALU.mult, op1=ALU.add
         )
+        load_words(nc.scalar, r_words, user_item_words, 0, 0, 1, 0, 2 * P)
         load_words(nc.scalar, l_words, item_user_words, 0, 0, 1)
-        load_words(nc.scalar, r_words, user_item_words, 0, 0, 1)
         warm_bank = next_bank()
         for w in range(WARM_PASSES):
             nc.tensor.matmul_mx(
@@ -142,29 +147,23 @@ def tile_rp3beta_item_scores_k5_kernel(
             )
         load_scales(l_scales, item_user_scales, 0)
         load_scales(r_scales, user_item_scales, 0)
-        load_words(nc.sync, l_words, item_user_words, 0, 1, 2)
-        load_words(nc.sync, r_words, user_item_words, 0, 1, 2)
-        nc.sync.dma_start(out=pop_rows[:], in_=rows_in_every_quadrant(popularity))
-        load_words(nc.sync, l_words, item_user_words, 0, 2, 3)
-        load_words(nc.sync, r_words, user_item_words, 0, 2, 3)
-        load_words(nc.sync, l_words, item_user_words, 0, 3, 4)
-        load_words(nc.sync, r_words, user_item_words, 0, 3, 4)
+        load_words(nc.sync, r_words, user_item_words, 0, 0, 1, 2 * P, HALF)
+        for g in range(1, U_PASSES):
+            load_words(nc.sync, l_words, item_user_words, 0, g, g + 1)
+            load_words(nc.sync, r_words, user_item_words, 0, g, g + 1)
+            if g == 1:
+                nc.sync.dma_start(out=pop_rows[:], in_=rows_in_every_quadrant(popularity))
         load_scales(l_scales, item_user_scales, 1)
-        load_words(nc.sync, l_words, item_user_words, 1, 0, 1)
-        load_words(nc.sync, l_words, item_user_words, 1, 1, 2)
-        load_words(nc.sync, l_words, item_user_words, 1, 2, 3)
-        load_words(nc.sync, l_words, item_user_words, 1, 3, 4)
-        load_prefs(0)
-        load_prefs(1)
+        for g in range(U_PASSES):
+            load_words(nc.sync, l_words, item_user_words, 1, g, g + 1)
+        for k in range(2):
+            load_prefs(k)
         nc.sync.dma_start(out=bias_rows[:], in_=rows_in_every_quadrant(item_bias))
         load_scales(r_scales, user_item_scales, 1)
-        load_words(nc.sync, r_words, user_item_words, 1, 0, 2)
-        load_words(nc.sync, r_words, user_item_words, 1, 2, U_PASSES)
+        load_words(nc.sync, r_words, user_item_words, 1, 0, U_PASSES)
         nc.sync.dma_start(out=gain_cols[:, :, 0:2], in_=user_gain.rearrange("(k p c) -> p k c", p=P, c=2))
-        load_prefs(2)
-        load_prefs(3)
-        load_prefs(4)
-        load_prefs(5)
+        for k in range(2, COUPLES):
+            load_prefs(k)
 
         nc.vector.transpose(out=pop_cols[:], in_=pop_rows[:])
         for a in range(4):
@@ -218,7 +217,7 @@ def tile_rp3beta_item_scores_k5_kernel(
             )
 
         def walk_out(bank, jt, ih):
-            sim_t[(jt, ih)] = work.tile([P, HALF], BF16, name="sim_t", tag="sim_t", bufs=8, align_bytes=64)
+            sim_t[(jt, ih)] = work.tile([P, HALF], BF16, name="sim_t", tag="sim_t", bufs=SIM_T_BUFS, align_bytes=64)
             target = sim_t[(jt, ih)][:].rearrange("q (u n z) -> q u n z", u=2, z=16)
             source = bank[:].rearrange("q (n u z) -> q u n z", u=2, z=16)
             nc.scalar.activation(out=target, in_=source, func=ACT.Copy, scale=damping[:, jt : jt + 1])
@@ -230,9 +229,19 @@ def tile_rp3beta_item_scores_k5_kernel(
 
             tensor_step((), passes, lambda bank: walk_out(bank, jt, ih))
 
+        def walks_pass_by_pass(tiles, ih):
+            banks = [next_bank() for jt in tiles]
+            for g in range(U_PASSES):
+                for bank, jt in zip(banks, tiles):
+                    walk_pass(bank, jt, ih, g)
+            for bank, jt in zip(banks, tiles):
+                walk_out(bank, jt, ih)
+
         def turn_sim(jt, count, g, copy):
             pairs = [sim_t[(jt + c, g)][:].bitcast(F32) for c in range(count)]
-            grouped = work.tile([P, count * P * 4], BF16, name="sim_grouped", tag="sim_grouped", bufs=4, align_bytes=64)
+            grouped = work.tile(
+                [P, count * P * 4], BF16, name="sim_grouped", tag="sim_grouped", bufs=GROUPED_BUFS, align_bytes=64
+            )
 
             def group(bank):
                 copy(
@@ -253,7 +262,9 @@ def tile_rp3beta_item_scores_k5_kernel(
 
 
         def split_prefs(k):
-            prefs_split[k] = work.tile([P, 2, I], BF16, name="prefs_split", tag="prefs_split", bufs=4, align_bytes=64)
+            prefs_split[k] = work.tile(
+                [P, 2, I], BF16, name="prefs_split", tag="prefs_split", bufs=SPLIT_BUFS, align_bytes=64
+            )
             target = prefs_split[k][:].rearrange("q c i -> q (c i)").bitcast(F32)
             source = prefs_raw[k][:].rearrange("q c i -> q (c i)").bitcast(F32)
             nc.vector.tensor_copy(
@@ -273,7 +284,7 @@ def tile_rp3beta_item_scores_k5_kernel(
             pairs = prefs_split[k][:].rearrange("q c i -> q (c i)").bitcast(F32)
             if c == 0:
                 prefs_grouped[k] = work.tile(
-                    [P, 2 * I], BF16, name="prefs_grouped", tag="prefs_grouped", bufs=3, align_bytes=64
+                    [P, 2 * I], BF16, name="prefs_grouped", tag="prefs_grouped", bufs=PREFS_GROUPED_BUFS, align_bytes=64
                 )
 
             def group(bank):
@@ -289,11 +300,11 @@ def tile_rp3beta_item_scores_k5_kernel(
                 later(OPERAND_LAG, ("prefs", k), lambda: quantize_prefs(k))
 
 
-        def score_passes(out, bt, j0, j1, passes=range(I_PASSES)):
+        def score_passes(out, bt, j0, j1):
             k, c = divmod(bt, 2)
             jh, lo = divmod(j0, HALF)
             columns = slice(lo, lo + j1 - j0)
-            for g in passes:
+            for g in range(I_PASSES):
                 nc.tensor.matmul_mx(
                     out=out,
                     lhsT=prefs_codes[k][:, c, g, :].bitcast(FP8X4),
@@ -314,9 +325,8 @@ def tile_rp3beta_item_scores_k5_kernel(
                 op0=ALU.mult, op1=ALU.add,
             )
 
-        def store_y(bt, count, j0, j1):
-            k, c = divmod(bt, 2)
-            nc.sync.dma_start(out=by_tiles(out_0)[k][:, c : c + count, j0:j1], in_=y_f32[k][:, c : c + count, j0:j1])
+        def store_y(bt, j0, j1):
+            nc.sync.dma_start(out=by_tiles(out_0)[bt // 2][:, :, j0:j1], in_=y_f32[bt // 2][:, :, j0:j1])
 
         def by_pairs(columns):
             return columns.rearrange("q (m u e) -> q u m e", u=2, e=2)
@@ -353,34 +363,24 @@ def tile_rp3beta_item_scores_k5_kernel(
             for bt in tiles:
                 score_and_round(bt, 1, 0, HALF)
                 if bt % 2:
-                    store_y(bt - 1, 2, 0, HALF)
+                    store_y(bt - 1, 0, HALF)
 
         def quarter(bt, j0, j1):
             score_and_round(bt, 2, j0, j1)
-            store_y(bt, 2, j0, j1)
+            store_y(bt, j0, j1)
 
-        def rounded_score(bt):
-            banks = []
-
-            def rounded(bank):
-                scores, bias = by_pairs(bank[:, 0 : I - LAST]), by_pairs(bias_all[:, LAST:I])
-                for u in range(2):
-                    gain_and_bias(split_view(bt, LAST, I)[:, u], scores[:, u], bias[:, u], bt)
-                banks.append(bank)
-
-            def finish():
-                gain_and_bias(y_tile(bt, LAST, I), banks[0][:, 0 : I - LAST], bias_all[:, LAST:I], bt)
-                store_y(bt, 1, LAST, I)
-
-            tensor_step((), lambda bank: score_passes(bank[:, 0 : I - LAST], bt, LAST, I), rounded)
-            return finish
+        def three_quarters(bt):
+            for tile in (bt, bt + 1):
+                score_and_round(tile, 1, 0, HALF)
+            score_and_round(bt, 2, HALF, LAST)
+            store_y(bt, 0, LAST)
 
 
         def turn_y(bt, jh, copy):
             n, second = divmod(bt // 2, 2)
             if second == 0:
                 y_grouped[(jh, n)] = work.tile(
-                    [P, 2, 2 * P * 4], BF16, name="y_grouped", tag="y_grouped", bufs=4, align_bytes=64
+                    [P, 2, 2 * P * 4], BF16, name="y_grouped", tag="y_grouped", bufs=GROUPED_BUFS, align_bytes=64
                 )
 
             def turn(bank):
@@ -406,16 +406,16 @@ def tile_rp3beta_item_scores_k5_kernel(
                 in_=y_codes[jh][:, users].bitcast(I32),
             )
 
-        def store_scales(jh, queues, b0=0, b1=B):
+        def store_scales(jh, queues):
             for r in range(4):
                 queues[r % len(queues)].dma_start(
-                    out=out_2[jh, r:16:4, b0:b1].bitcast(I32), in_=y_scales[r:P:QUAD, jh, b0:b1].bitcast(I32)
+                    out=out_2[jh, r:16:4, :].bitcast(I32), in_=y_scales[r:P:QUAD, jh, :].bitcast(I32)
                 )
 
 
-        def run(steps, turn=VECTOR_TURN):
+        def run(steps):
             for n, step in enumerate(steps):
-                step(on_vector if n % turn == 1 and n < len(steps) - 1 else on_scalar)
+                step(on_vector if n % VECTOR_TURN == 1 and n < len(steps) - 1 else on_scalar)
 
         def prefs_steps(tiles):
             return [lambda copy, bt=bt: turn_prefs(bt, copy) for bt in tiles]
@@ -425,9 +425,6 @@ def tile_rp3beta_item_scores_k5_kernel(
                 lambda copy, jt=jt: later(OPERAND_LAG, ("sim", jt, g), turn_sim(jt, 2, g, copy)) for jt in tiles[::2]
             ]
 
-        def y_steps(tiles, jh):
-            return [lambda copy, bt=bt: turn_y(bt, jh, copy) for bt in tiles[::2]]
-
         def first_half_y_steps(tiles):
             def step(copy, bt):
                 turn_y(bt, 0, copy)
@@ -436,31 +433,23 @@ def tile_rp3beta_item_scores_k5_kernel(
 
             return [lambda copy, bt=bt: step(copy, bt) for bt in tiles[::2]]
 
+        def second_half_y_steps():
+            def step(copy, k):
+                turn_y(2 * k, 1, copy)
+                if k >= PLANES_LAG:
+                    planes(1, k - PLANES_LAG, 1)
 
-        def three_quarters(bt):
-            for tile in (bt, bt + 1):
-                score_and_round(tile, 1, 0, HALF)
-            score_and_round(bt, 2, HALF, LAST)
-            store_y(bt, 2, 0, LAST)
+            return [lambda copy, k=k: step(copy, k) for k in range(COUPLES)]
 
-        first_banks = [next_bank() for jt in range(4)]
-        for g in range(U_PASSES):
-            for jt in range(4):
-                walk_pass(first_banks[jt], jt, 0, g)
-        for jt in range(4):
-            walk_out(first_banks[jt], jt, 0)
 
-        pair_banks = [next_bank() for jt in range(2)]
-        for g in range(U_PASSES):
-            for jt in range(2):
-                walk_pass(pair_banks[jt], jt, 1, g)
-        for jt in range(2):
-            walk_out(pair_banks[jt], jt, 1)
+        walks_pass_by_pass(range(4), 0)
+        walks_pass_by_pass(range(2), 1)
         for jt in (2, 3):
             split_prefs(jt - 2)
             walk(jt, 1)
         spread_bias()
         run(sim_steps(range(4), 0) + prefs_steps(range(0, 2)) + sim_steps(range(4), 1) + prefs_steps(range(2, 4)))
+
         for jt in (4, 5):
             walk(jt, 0)
             split_prefs(jt - 2)
@@ -479,13 +468,13 @@ def tile_rp3beta_item_scores_k5_kernel(
         for bt in (8, 10):
             three_quarters(bt)
         run(first_half_y_steps(range(2, 4)) + sim_steps(range(6, 8), 0) + first_half_y_steps(range(4, USER_TILES)))
+
         for jt in (6, 7):
             walk(jt, 1)
-        release([("planes", bt) for bt in range(USER_TILES)])
         store_scales(0, (nc.sync,))
         for bt in (0, 2):
             score(bt, 2, HALF, LAST)
-            store_y(bt, 2, HALF, LAST)
+            store_y(bt, HALF, LAST)
         last_sim = [turn_sim(jt, 1, 1, on_scalar) for jt in (6, 7)]
         for quantize in last_sim:
             quantize()
@@ -496,16 +485,7 @@ def tile_rp3beta_item_scores_k5_kernel(
 
         for bt in range(0, USER_TILES, 2):
             quarter(bt, LAST, I)
-        turn_y(0, 1, on_scalar)
-        turn_y(2, 1, on_vector)
-        turn_y(4, 1, on_scalar)
-        planes(1, 0, 1)
-        turn_y(6, 1, on_scalar)
-        planes(1, 1, 1)
-        turn_y(8, 1, on_vector)
-        planes(1, 2, 1)
-        turn_y(10, 1, on_scalar)
-        planes(1, 3, 1)
-        planes(1, 4, 1)
-        planes(1, 5, 1)
-        store_scales(1, (nc.scalar, nc.sync), 0, B)
+        run(second_half_y_steps())
+        for k in range(COUPLES - PLANES_LAG, COUPLES):
+            planes(1, k, 1)
+        store_scales(1, (nc.scalar, nc.sync))

from contextlib import ExitStack

import concourse.mybir as mybir
from concourse.masks import make_identity

U, I, B = 2048, 1024, 1536
BETA = 0.4
FLOPS = 2 * U * I * I + 2 * B * I * I

F32 = mybir.dt.float32
BF16 = mybir.dt.bfloat16
I32 = mybir.dt.int32
U32 = mybir.dt.uint32
U8 = mybir.dt.uint8
FP8X4 = mybir.dt.float8_e4m3fn_x4
FP4X4 = mybir.dt.float4_e2m1fn_x4
ALU = mybir.AluOpType
ACT = mybir.ActivationFunctionType

P = 128
QUAD = 32
HALF = 512
LAST = 768
U_PASSES = U // 512
I_PASSES = I // 512
ITEM_TILES = I // P
USER_TILES = B // P
COUPLES = USER_TILES // 2
GAIN_PAD = 16
BANKS = 8
WARM_PASSES = 6
VECTOR_TURN = 3

ROUND_LAG = 2
OPERAND_LAG = 3
PLANES_LAG = 2

SIM_T_BUFS = 8
SPLIT_BUFS = 4
GROUPED_BUFS = 4
PREFS_GROUPED_BUFS = 3


def tile_rp3beta_item_scores_k5_kernel(
    tc, item_user_words, item_user_scales, user_item_words, user_item_scales,
    popularity, prefs, user_gain, item_bias, out_0, out_1, out_2,
):
    nc = tc.nc
    on_vector, on_scalar = nc.vector.tensor_copy, nc.scalar.copy

    def on_gpsimd(out, in_):
        nc.gpsimd.tensor_scalar(out=out, in0=in_, scalar1=1.0, scalar2=0.0, op0=ALU.mult, op1=ALU.add)

    with ExitStack() as ctx:
        keep = ctx.enter_context(tc.tile_pool(name="keep", bufs=1))
        work = ctx.enter_context(tc.tile_pool(name="work", bufs=3))
        psum = ctx.enter_context(tc.psum_pool(name="psum", bufs=1))

        banks_taken = [0]

        def next_bank():
            k = banks_taken[0] % BANKS
            banks_taken[0] += 1
            return psum.tile([P, HALF], F32, name="bank%d" % k, tag="bank%d" % k)

        def kept(name, shape, dtype):
            return keep.tile(shape, dtype, name=name, tag=name, align_bytes=64)

        l_words = [kept("l_words%d" % h, [P, U_PASSES, 2 * HALF], U8) for h in range(2)]
        r_words = [kept("r_words%d" % h, [P, U_PASSES, 2 * HALF], U8) for h in range(2)]
        l_scales = [kept("l_scales%d" % h, [P, U_PASSES, HALF], U8) for h in range(2)]
        r_scales = [kept("r_scales%d" % h, [P, U_PASSES, HALF], U8) for h in range(2)]
        prefs_raw = [kept("prefs_raw%d" % k, [P, 2, I], BF16) for k in range(COUPLES)]
        prefs_split = {}
        prefs_grouped = {}
        prefs_codes = [kept("prefs_codes%d" % k, [P, 2, I_PASSES, P], U32) for k in range(COUPLES)]
        prefs_scales = [kept("prefs_scales%d" % k, [P, 2, I_PASSES, P], U8) for k in range(COUPLES)]
        sim_t = {}
        sim_codes = [kept("sim_codes%d" % h, [P, I_PASSES, HALF], U32) for h in range(2)]
        sim_scales = [kept("sim_scales%d" % h, [P, I_PASSES, HALF], U8) for h in range(2)]
        y_f32 = [kept("y%d" % k, [P, 2, I], F32) for k in range(COUPLES)]
        y_split = {(bt, jh): kept("y_split%d_%d" % (bt, jh), [P, HALF], BF16) for jh in (0, 1) for bt in range(USER_TILES)}
        y_grouped = {}
        y_codes = [kept("y_codes%d" % h, [P, B], U32) for h in range(2)]
        y_scales = kept("y_scales", [P, 2, B], U8)
        gain_cols = kept("gain_cols", [P, COUPLES, GAIN_PAD], BF16)
        pop_rows = kept("pop_rows", [P, QUAD], BF16)
        pop_cols = kept("pop_cols", [P, QUAD], BF16)
        pop_own = kept("pop_own", [P, ITEM_TILES], F32)
        exponent = kept("exponent", [P, ITEM_TILES], F32)
        damping = kept("damping", [P, ITEM_TILES], F32)
        identity = kept("identity", [P, P], F32)
        bias_rows = kept("bias_rows", [P, QUAD], BF16)
        bias_cols = kept("bias_cols", [P, QUAD], BF16)
        bias_spread = kept("bias_spread", [P, QUAD, QUAD], BF16)
        bias_all = kept("bias_all", [P, I], BF16)


        def load_words(queue, dst, src, h, g0, g1, c0=0, c1=HALF):
            queue.dma_start(
                out=dst[h][:, g0:g1, 2 * c0 : 2 * c1].bitcast(I32),
                in_=src[g0:g1, :, 2 * (HALF * h + c0) : 2 * (HALF * h + c1)].rearrange("g p n -> p g n").bitcast(I32),
            )

        def load_scales(dst, src, h):
            for r in range(4):
                nc.sync.dma_start(
                    out=dst[h][r:P:QUAD, :, :].bitcast(I32),
                    in_=src[:, r:16:4, HALF * h : HALF * (h + 1)].rearrange("g q n -> q g n").bitcast(I32),
                )

        def by_tiles(rows):
            return rows.rearrange("(k p c) x -> k p c x", p=P, c=2)

        def load_prefs(k):
            nc.sync.dma_start(out=prefs_raw[k][:], in_=by_tiles(prefs)[k])

        def clear(tile_ap):
            nc.vector.memset(tile_ap.bitcast(I32), 0)

        def rows_in_every_quadrant(vector):
            return vector.rearrange("(c x) -> c x", x=QUAD).unsqueeze(0).to_broadcast([4, QUAD, QUAD])

        ctx.enter_context(tc.manual_schedule())

        blank = r_scales[1][:, 0:2, :].rearrange("p g n -> p (g n)")
        clear(blank)
        clear(l_scales[0][:].rearrange("p g n -> p (g n)"))
        clear(r_scales[0][:].rearrange("p g n -> p (g n)"))
        clear(l_scales[1][:].rearrange("p g n -> p (g n)"))
        clear(r_scales[1][:, 2:U_PASSES, :].rearrange("p g n -> p (g n)"))
        clear(identity[:])
        make_identity(nc, identity[:], nomemset=True)
        nc.vector.memset(exponent[:], 1.0)
        nc.gpsimd.tensor_scalar(
            out=exponent[:], in0=exponent[:], scalar1=-BETA, scalar2=0.0, op0=ALU.mult, op1=ALU.add
        )
        load_words(nc.scalar, r_words, user_item_words, 0, 0, 1, 0, 2 * P)
        load_words(nc.scalar, l_words, item_user_words, 0, 0, 1)
        warm_bank = next_bank()
        for w in range(WARM_PASSES):
            nc.tensor.matmul_mx(
                out=warm_bank[:],
                lhsT=blank[:, 0 : 2 * P].bitcast(FP4X4), lhsT_scale=blank[:, 0:P],
                rhs=blank[:, 0 : 2 * HALF].bitcast(FP4X4), rhs_scale=blank[:, 0:HALF],
                start=True, stop=True,
            )
        load_scales(l_scales, item_user_scales, 0)
        load_scales(r_scales, user_item_scales, 0)
        load_words(nc.sync, r_words, user_item_words, 0, 0, 1, 2 * P, HALF)
        for g in range(1, U_PASSES):
            load_words(nc.sync, l_words, item_user_words, 0, g, g + 1)
            load_words(nc.sync, r_words, user_item_words, 0, g, g + 1)
            if g == 1:
                nc.sync.dma_start(out=pop_rows[:], in_=rows_in_every_quadrant(popularity))
        load_scales(l_scales, item_user_scales, 1)
        for g in range(U_PASSES):
            load_words(nc.sync, l_words, item_user_words, 1, g, g + 1)
        for k in range(2):
            load_prefs(k)
        nc.sync.dma_start(out=bias_rows[:], in_=rows_in_every_quadrant(item_bias))
        load_scales(r_scales, user_item_scales, 1)
        load_words(nc.sync, r_words, user_item_words, 1, 0, U_PASSES)
        nc.sync.dma_start(out=gain_cols[:, :, 0:2], in_=user_gain.rearrange("(k p c) -> p k c", p=P, c=2))
        for k in range(2, COUPLES):
            load_prefs(k)

        nc.vector.transpose(out=pop_cols[:], in_=pop_rows[:])
        for a in range(4):
            quadrant = slice(QUAD * a, QUAD * (a + 1))
            nc.scalar.activation(out=pop_own[quadrant, :], in_=pop_cols[quadrant, a:QUAD:4], func=ACT.Copy)
        nc.gpsimd.tensor_tensor(out=damping[:], in0=pop_own[:], in1=exponent[:], op=ALU.pow)

        def spread_bias():
            nc.vector.transpose(out=bias_cols[:], in_=bias_rows[:])
            nc.vector.tensor_copy(out=bias_spread[:], in_=bias_cols[:].unsqueeze(2).to_broadcast([P, QUAD, QUAD]))
            nc.vector.transpose(out=bias_all[:], in_=bias_spread[:].rearrange("p c y -> p (c y)"))


        steps_done = [0]
        waiting = []

        def later(lag, product, call):
            waiting.append((steps_done[0] + lag, product, call))

        def release(needed=()):
            for entry in list(waiting):
                due, product, call = entry
                if product in needed if needed else due <= steps_done[0]:
                    waiting.remove(entry)
                    call()

        def tensor_step(needed, tensor_work, empty_bank):
            steps_done[0] += 1
            if needed:
                release(needed)
            bank = next_bank()
            tensor_work(bank)
            release()
            empty_bank(bank)

        def transposes(bank, sources):
            for s, source in enumerate(sources):
                nc.tensor.transpose(bank[:, P * s : P * (s + 1)], source, identity[:])


        def walk_pass(bank, jt, ih, g):
            jh, c = divmod(jt, 4)
            nc.tensor.matmul_mx(
                out=bank[:],
                lhsT=r_words[jh][:, g, 2 * P * c : 2 * P * (c + 1)].bitcast(FP4X4),
                lhsT_scale=r_scales[jh][:, g, P * c : P * (c + 1)],
                rhs=l_words[ih][:, g, :].bitcast(FP4X4),
                rhs_scale=l_scales[ih][:, g, :],
                start=(g == 0),
                stop=(g == U_PASSES - 1),
            )

        def walk_out(bank, jt, ih):
            sim_t[(jt, ih)] = work.tile([P, HALF], BF16, name="sim_t", tag="sim_t", bufs=SIM_T_BUFS, align_bytes=64)
            target = sim_t[(jt, ih)][:].rearrange("q (u n z) -> q u n z", u=2, z=16)
            source = bank[:].rearrange("q (n u z) -> q u n z", u=2, z=16)
            nc.scalar.activation(out=target, in_=source, func=ACT.Copy, scale=damping[:, jt : jt + 1])

        def walk(jt, ih):
            def passes(bank):
                for g in range(U_PASSES):
                    walk_pass(bank, jt, ih, g)

            tensor_step((), passes, lambda bank: walk_out(bank, jt, ih))

        def walks_pass_by_pass(tiles, ih):
            banks = [next_bank() for jt in tiles]
            for g in range(U_PASSES):
                for bank, jt in zip(banks, tiles):
                    walk_pass(bank, jt, ih, g)
            for bank, jt in zip(banks, tiles):
                walk_out(bank, jt, ih)

        def turn_sim(jt, count, g, copy):
            pairs = [sim_t[(jt + c, g)][:].bitcast(F32) for c in range(count)]
            grouped = work.tile(
                [P, count * P * 4], BF16, name="sim_grouped", tag="sim_grouped", bufs=GROUPED_BUFS, align_bytes=64
            )

            def group(bank):
                copy(
                    out=grouped[:].bitcast(F32).rearrange("q (c j u) -> q c j u", c=count, u=2),
                    in_=bank[:, 0 : 2 * P * count].rearrange("q (c u j) -> q c j u", c=count, u=2),
                )

            def quantize():
                jh, c = divmod(jt, 4)
                columns = slice(P * c, P * (c + count))
                nc.vector.quantize_mx(
                    out=sim_codes[jh][:, g, columns].bitcast(FP8X4), scales=sim_scales[jh][:, g, columns], in_=grouped[:]
                )

            sources = [tile_pairs[:, P * u : P * (u + 1)] for tile_pairs in pairs for u in range(2)]
            tensor_step((), lambda bank: transposes(bank, sources), group)
            return quantize


        def split_prefs(k):
            prefs_split[k] = work.tile(
                [P, 2, I], BF16, name="prefs_split", tag="prefs_split", bufs=SPLIT_BUFS, align_bytes=64
            )
            target = prefs_split[k][:].rearrange("q c i -> q (c i)").bitcast(F32)
            source = prefs_raw[k][:].rearrange("q c i -> q (c i)").bitcast(F32)
            nc.vector.tensor_copy(
                out=target.rearrange("q (s u n r) -> q s u n r", s=4, u=2, r=8),
                in_=source.rearrange("q (s n u r) -> q s u n r", s=4, u=2, r=8),
            )

        def quantize_prefs(k):
            nc.vector.quantize_mx(
                out=prefs_codes[k][:].rearrange("q c g b -> q (c g b)").bitcast(FP8X4),
                scales=prefs_scales[k][:].rearrange("q c g b -> q (c g b)"),
                in_=prefs_grouped[k][:],
            )

        def turn_prefs(bt, copy):
            k, c = divmod(bt, 2)
            pairs = prefs_split[k][:].rearrange("q c i -> q (c i)").bitcast(F32)
            if c == 0:
                prefs_grouped[k] = work.tile(
                    [P, 2 * I], BF16, name="prefs_grouped", tag="prefs_grouped", bufs=PREFS_GROUPED_BUFS, align_bytes=64
                )

            def group(bank):
                target = prefs_grouped[k][:, I * c : I * (c + 1)].bitcast(F32)
                copy(
                    out=target.rearrange("q (g b u) -> q g b u", g=I_PASSES, u=2),
                    in_=bank[:].rearrange("q (g u b) -> q g b u", g=I_PASSES, u=2),
                )

            sources = [pairs[:, P * (4 * c + s) : P * (4 * c + s + 1)] for s in range(4)]
            tensor_step((), lambda bank: transposes(bank, sources), group)
            if c == 1:
                later(OPERAND_LAG, ("prefs", k), lambda: quantize_prefs(k))


        def score_passes(out, bt, j0, j1):
            k, c = divmod(bt, 2)
            jh, lo = divmod(j0, HALF)
            columns = slice(lo, lo + j1 - j0)
            for g in range(I_PASSES):
                nc.tensor.matmul_mx(
                    out=out,
                    lhsT=prefs_codes[k][:, c, g, :].bitcast(FP8X4),
                    lhsT_scale=prefs_scales[k][:, c, g, :],
                    rhs=sim_codes[jh][:, g, columns].bitcast(FP8X4),
                    rhs_scale=sim_scales[jh][:, g, columns],
                    start=(g == 0),
                    stop=(g == I_PASSES - 1),
                )

        def y_tile(bt, j0, j1):
            k, c = divmod(bt, 2)
            return y_f32[k][:, c, j0:j1]

        def gain_and_bias(out, scores, bias, bt):
            nc.vector.scalar_tensor_tensor(
                out=out, in0=scores, scalar=gain_cols[:, bt // 2, bt % 2 : bt % 2 + 1], in1=bias,
                op0=ALU.mult, op1=ALU.add,
            )

        def store_y(bt, j0, j1):
            nc.sync.dma_start(out=by_tiles(out_0)[bt // 2][:, :, j0:j1], in_=y_f32[bt // 2][:, :, j0:j1])

        def by_pairs(columns):
            return columns.rearrange("q (m u e) -> q u m e", u=2, e=2)

        def split_view(bt, j0, j1):
            jh, lo = divmod(j0, HALF)
            whole = y_split[(bt, jh)][:].rearrange("q (u m e) -> q u m e", u=2, e=2)
            return whole[:, :, lo // 4 : (lo + j1 - j0) // 4, :]

        def round_y(bt, j0, j1, copy):
            copy(out=split_view(bt, j0, j1), in_=by_pairs(y_tile(bt, j0, j1)))

        def score(bt, count, j0, j1):
            width = j1 - j0

            def passes(bank):
                for n in range(count):
                    score_passes(bank[:, width * n : width * (n + 1)], bt + n, j0, j1)

            def finish(bank):
                for n in range(count):
                    scores = bank[:, width * n : width * (n + 1)]
                    gain_and_bias(y_tile(bt + n, j0, j1), scores, bias_all[:, j0:j1], bt + n)

            tensor_step([("prefs", bt // 2)], passes, finish)

        def score_and_round(bt, count, j0, j1):
            score(bt, count, j0, j1)
            for tile in range(bt, bt + count):
                copy = on_scalar if tile % 2 else on_gpsimd
                later(ROUND_LAG, ("y", tile, j0 // HALF), lambda tile=tile, copy=copy: round_y(tile, j0, j1, copy))

        def first_half(tiles):
            for bt in tiles:
                score_and_round(bt, 1, 0, HALF)
                if bt % 2:
                    store_y(bt - 1, 0, HALF)

        def quarter(bt, j0, j1):
            score_and_round(bt, 2, j0, j1)
            store_y(bt, j0, j1)

        def three_quarters(bt):
            for tile in (bt, bt + 1):
                score_and_round(tile, 1, 0, HALF)
            score_and_round(bt, 2, HALF, LAST)
            store_y(bt, 0, LAST)


        def turn_y(bt, jh, copy):
            n, second = divmod(bt // 2, 2)
            if second == 0:
                y_grouped[(jh, n)] = work.tile(
                    [P, 2, 2 * P * 4], BF16, name="y_grouped", tag="y_grouped", bufs=GROUPED_BUFS, align_bytes=64
                )

            def turn(bank):
                pairs = [y_split[(bt + c, jh)][:].bitcast(F32) for c in range(2)]
                transposes(bank, [tile_pairs[:, P * u : P * (u + 1)] for tile_pairs in pairs for u in range(2)])

            def group(bank):
                target = y_grouped[(jh, n)][:, second, :].bitcast(F32).rearrange("q (b c u) -> q b c u", c=2, u=2)
                copy(out=target, in_=bank[:].rearrange("q (c u b) -> q b c u", c=2, u=2))

            tensor_step([("y", bt + c, jh) for c in range(2)], turn, group)

        def planes(jh, k, count):
            n, first = divmod(k, 2)
            users = slice(2 * P * k, 2 * P * (k + count))
            nc.vector.quantize_mx(
                out=y_codes[jh][:, users].bitcast(FP8X4),
                scales=y_scales[:, jh, users],
                in_=y_grouped[(jh, n)][:, first : first + count, :].rearrange("q k x -> q (k x)"),
            )
            nc.sync.dma_start(
                out=out_1[jh].rearrange("p m t -> p (m t)").bitcast(I32)[:, users],
                in_=y_codes[jh][:, users].bitcast(I32),
            )

        def store_scales(jh, queues):
            for r in range(4):
                queues[r % len(queues)].dma_start(
                    out=out_2[jh, r:16:4, :].bitcast(I32), in_=y_scales[r:P:QUAD, jh, :].bitcast(I32)
                )


        def run(steps):
            for n, step in enumerate(steps):
                step(on_vector if n % VECTOR_TURN == 1 and n < len(steps) - 1 else on_scalar)

        def prefs_steps(tiles):
            return [lambda copy, bt=bt: turn_prefs(bt, copy) for bt in tiles]

        def sim_steps(tiles, g):
            return [
                lambda copy, jt=jt: later(OPERAND_LAG, ("sim", jt, g), turn_sim(jt, 2, g, copy)) for jt in tiles[::2]
            ]

        def first_half_y_steps(tiles):
            def step(copy, bt):
                turn_y(bt, 0, copy)
                if bt % 4 == 2:
                    later(PLANES_LAG, ("planes", bt), lambda: planes(0, bt // 2 - 1, 2))

            return [lambda copy, bt=bt: step(copy, bt) for bt in tiles[::2]]

        def second_half_y_steps():
            def step(copy, k):
                turn_y(2 * k, 1, copy)
                if k >= PLANES_LAG:
                    planes(1, k - PLANES_LAG, 1)

            return [lambda copy, k=k: step(copy, k) for k in range(COUPLES)]


        walks_pass_by_pass(range(4), 0)
        walks_pass_by_pass(range(2), 1)
        for jt in (2, 3):
            split_prefs(jt - 2)
            walk(jt, 1)
        spread_bias()
        run(sim_steps(range(4), 0) + prefs_steps(range(0, 2)) + sim_steps(range(4), 1) + prefs_steps(range(2, 4)))

        for jt in (4, 5):
            walk(jt, 0)
            split_prefs(jt - 2)
        for jt in (4, 5):
            first_half(range(2 * jt - 8, 2 * jt - 6))
            walk(jt, 1)
            split_prefs(jt)
        run(
            prefs_steps(range(4, 8)) + sim_steps(range(4, 6), 0) + sim_steps(range(4, 6), 1)
            + prefs_steps(range(8, USER_TILES)) + first_half_y_steps(range(0, 2))
        )

        walk(6, 0)
        first_half(range(4, 8))
        walk(7, 0)
        for bt in (8, 10):
            three_quarters(bt)
        run(first_half_y_steps(range(2, 4)) + sim_steps(range(6, 8), 0) + first_half_y_steps(range(4, USER_TILES)))

        for jt in (6, 7):
            walk(jt, 1)
        store_scales(0, (nc.sync,))
        for bt in (0, 2):
            score(bt, 2, HALF, LAST)
            store_y(bt, HALF, LAST)
        last_sim = [turn_sim(jt, 1, 1, on_scalar) for jt in (6, 7)]
        for quantize in last_sim:
            quantize()
        for bt in range(4):
            round_y(bt, HALF, LAST, on_scalar)
        for bt in (4, 6):
            quarter(bt, HALF, LAST)

        for bt in range(0, USER_TILES, 2):
            quarter(bt, LAST, I)
        run(second_half_y_steps())
        for k in range(COUPLES - PLANES_LAG, COUPLES):
            planes(1, k, 1)
        store_scales(1, (nc.scalar, nc.sync))
